import numpy as np, ml_dtypes
CORES = [35,38,43,46]
N = 4
BF = ml_dtypes.bfloat16
def gentries(a):
    return np.ascontiguousarray(a.reshape(8, 16, -1).transpose(0, 2, 1)).reshape(8, -1)
def gtable(e):
    e = np.asarray(e); return np.ascontiguousarray(e.reshape(8, -1, 16).transpose(0, 2, 1)).reshape(128, -1).astype(np.int32)
TT, P, R, S, CAP = 1024, 368, 2, 2, 48
def walk(planes, nbr, x, c):
    A = planes.astype(np.int64).reshape(N, 4, 4, TT).transpose(0, 3, 1, 2).reshape(N * TT, 4, 4); B = nbr.astype(np.int64).transpose(0, 2, 1).reshape(N * TT, 4)
    h = np.concatenate([x.astype(np.int64), np.ones((len(x), 1), np.int64)], 1); c = c.astype(np.int64); w = [c]
    for k in range(R):
        q = c // TT
        for s in range(S):
            v = np.einsum("mfc,mc->mf", A[c], h); face = np.argmin(v, 1)
            c = np.where((c // TT == q) & (np.min(v, 1) < 0), B[c, face], c)
        w.append(c)
    return np.stack(w)
def codes(rng, shape, own):
    r = np.arange(N).reshape(N, 1, 1); q = np.where(rng.random(shape) < own, r, (r + rng.integers(1, N, shape)) % N)
    return q * TT + rng.integers(0, TT, shape)
def mesh(rng, big, lo, hi):
    p = rng.integers(-big, big + 1, (N, 4, 4, TT)); p[:, :, 3] = rng.integers(lo, hi + 1, (N, 4, TT)); return p
def roomy(rng, p):
    h = np.stack([1 + rng.permutation(TT - 2)[:TT // 16] for r in range(N)]); k = h.shape[1]
    for r in range(N):
        u = p[r]; u[:, :3, h[r]] = rng.integers(-255, 256, (4, 3, k)); u[:, 3, h[r]] = rng.integers(3 * 255 * 1023, 2 ** 20 + 1, (4, k))
    return h
def choose(rng, p, h, b, x, c):
    big = int(np.abs(x).max()); r = np.arange(N).reshape(N, 1, 1)
    x = np.concatenate([x, rng.integers(-big, big + 1, (N, 8, P, 3))], 2); c = np.concatenate([c, r * TT + h[r, rng.integers(0, h.shape[1], (N, 8, P))]], 2)
    planes = p.reshape(N, 16, TT).astype(np.int32); m = c.shape[2]
    w = walk(planes, b, x.reshape(-1, 3), c.reshape(-1))[:R].reshape(R, N, 8, m) // TT
    cap = np.where(np.eye(N, dtype=bool), P, CAP); cnt = np.zeros((R, N, 8, N), np.int64); n = np.zeros((N, 8), np.int64); keep = np.zeros((N, 8, m), bool)
    k, i, g = np.ogrid[:R, :N, :8]
    for j in range(m):
        q = w[:, :, :, j]; ok = np.all(cnt[k, i, g, q] < cap[i, q], axis=0) & (n < P)
        cnt[k, i, g, q] += ok; n += ok; keep[:, :, j] = ok
    e = rng.permuted(np.nonzero(keep.reshape(N * 8, m))[1].reshape(N, 8, P), axis=2)
    x = np.take_along_axis(x, e[:, :, :, None], 2); c = np.take_along_axis(c, e, 2)
    return {"planes": planes, "nbr": b.astype(np.int32), "pts": np.ascontiguousarray(x.transpose(0, 1, 3, 2)).reshape(N, 24, P).astype(np.int32), "tet0": np.stack([gtable(u) for u in c])}
def setup_inputs(rng):
    p = mesh(rng, 127, -20000, 60000); h = roomy(rng, p)
    return choose(rng, p, h, codes(rng, (N, 4, TT), 0.6), rng.integers(-255, 256, (N, 8, 3 * P, 3)), codes(rng, (N, 8, 3 * P), 0.5))
def setup_inputs_full(rng):
    p = mesh(rng, 127, -20000, 60000); h = roomy(rng, p); r = np.arange(N).reshape(N, 1, 1); m = (N - 1) * CAP
    q = np.broadcast_to((r + 1 + np.arange(m) // CAP) % N, (N, 8, m)); c = q * TT + h[q, rng.integers(0, h.shape[1], (N, 8, m))]
    c = np.where(np.arange(8).reshape(1, 8, 1) % 2 == 0, c, codes(rng, (N, 8, m), 0.0)); c = np.concatenate([c, codes(rng, (N, 8, 2 * P), 0.8)], 2)
    return choose(rng, p, h, codes(rng, (N, 4, TT), 0.6), rng.integers(-255, 256, (N, 8, m + 2 * P, 3)), c)
def setup_inputs_ties(rng):
    p = mesh(rng, 1, -1, 2)
    p[:, 3] = np.where(rng.random((N, 1, TT)) < 0.5, p[:, 1], p[:, 3]); p[:, 2] = np.where(rng.random((N, 1, TT)) < 0.5, p[:, 0], p[:, 2]); h = roomy(rng, p)
    return choose(rng, p, h, codes(rng, (N, 4, TT), 0.6), rng.integers(-2, 3, (N, 8, 3 * P, 3)), codes(rng, (N, 8, 3 * P), 0.5))
def setup_inputs_few(rng):
    p = mesh(rng, 127, -20000, 60000); h = roomy(rng, p); b = codes(rng, (N, 4, TT), 1.0); q = rng.integers(0, N); b[q] = codes(rng, (N, 4, TT), 0.3)[q]
    c = codes(rng, (N, 8, 3 * P), 1.0); out = []
    for v in (b, c):
        u = rng.random(v.shape); out.append(np.where(u < 0.2, v // TT * TT, np.where(u < 0.4, v // TT * TT + TT - 1, v)))
    b, c = out; x = rng.integers(-255, 256, (N, 8, 3 * P, 3)); one = rng.random((N, 8, 3 * P)) < 0.4
    c = np.where(one, c[:, :, :1], c); x = np.where(one[:, :, :, None], x[:, :, :1], x)
    return choose(rng, p, h, b, x, c)
def setup_inputs_spread(rng):
    def some(bits, top, shape, plus):
        v = np.minimum(np.floor(np.exp2(bits * rng.random(shape))).astype(np.int64), top); v = np.where(rng.random(shape) < 0.125, top, v)
        return np.where(rng.random(shape) < plus, v, -v)
    p = some(10, 1023, (N, 4, 4, TT), 0.5); p[:, :, 3] = some(20, 2 ** 20, (N, 4, TT), 0.75); h = roomy(rng, p)
    return choose(rng, p, h, codes(rng, (N, 4, TT), 0.6), some(10, 1023, (N, 8, 3 * P, 3), 0.5), codes(rng, (N, 8, 3 * P), 0.5))
def points(pts, tet0):
    return pts.reshape(N, 8, 3, P).transpose(0, 1, 3, 2).reshape(-1, 3), np.stack([gentries(a) for a in tet0]).reshape(-1)
def check_inputs(d):
    bad = []; p = d["planes"].astype(np.int64).reshape(N, 4, 4, TT)
    if np.abs(p[:, :, :3]).max() > 1023 or np.abs(p[:, :, 3]).max() > 2 ** 20: bad.append("planes out of range")
    if np.abs(d["pts"].astype(np.int64)).max() > 1023: bad.append("pts out of range")
    for a in ("nbr", "tet0"):
        if d[a].min() < 0 or d[a].max() >= N * TT: bad.append(a + " out of range")
    if bad: return bad
    x, c = points(d["pts"], d["tet0"]); w = walk(d["planes"], d["nbr"], x, c)[:R].reshape(R, N, 8, P) // TT
    for q in range(N):
        n = np.count_nonzero(w == q, axis=3); n[:, q] = 0
        if n.max() > CAP: bad.append("more than CAP points of a group on rank " + str(q))
    return bad
def reference(planes, nbr, pts, tet0):
    x, c = points(pts, tet0); e = walk(planes, nbr, x, c)[R].reshape(N, 8, P)
    return {"y": np.stack([gtable(u) for u in e]).astype(np.float32)}

@@ -1,0 +1,351 @@
+from concourse.mybir import AluOpType as ALU, ActivationFunctionType as ACTF
+
+I32, F32, F16, B16, U16 = "int32", "float32", "float16", "bfloat16", "uint16"
+WN = 2050
+FLAG = 8192
+SCRATCH = {}
+for _d, _s, _n in (
+        (I32, [128, 8, 16], "ixp"), (I32, [128, 16, 16], "ixd ixq"), (I32, [128, 4, 32], "ic"), (I32, [128, 32], "i_s i_n"),
+        (I32, [128, 8, 4, 4], "i_e"), (I32, [128, 8], "i_p i_g i_q i_r"), (I32, [128, 16], "i_m"),
+        (I32, [128, 64], "i_t pb32 pbb dn dsh dd2 dhi dlo"), (I32, [128, 128], "pl32 plb"), (I32, [128, 23], "tl32"),
+        (I32, [128, 92], "pf32"), (I32, [128, 368], "pr32"), (B16, [128, 8, 16], "izp"), (B16, [128, 16, 16], "izd izq"),
+        (B16, [128, 8, 8, 16], "yp"), (B16, [128, 16, 8, 16], "yd qq"), (B16, [128, 4, 4, 32], "cc"), (B16, [128, 512], "z0"),
+        (B16, [128, 32], "rn"), (B16, [128, 8, 4, 4], "e24"), (B16, [128, 240], "ee"), (B16, [128, 2064], "w2"),
+        (F32, [128, 2056], "w1"), (F32, [128, 32], "s4 s4a s4b rna rnb"), (F32, [128, 8], "gm xb wb wc"),
+        (F32, [128, 64], "tto ttm dfl ddd"), (F32, [128, 24], "yo"), (F16, [128, 192], "tw tn"), (F16, [128, 92], "lp lpn"),
+        (F16, [128, 24], "llh llf"), (F16, [128, 64], "ex"), (F16, [128, 8, 3], "ina inb inc woh wof weh wef"),
+        (F16, [128, 368], "pth ptf"), (F16, [128, 8, 24], "rmh rmf"), (F16, [128, 2, 8, 32], "tbh tbf"),
+        (F32, [128, 384], "xh xf prh prf"), (B16, [128, 384], "nbh nbf"), (U16, [128, 24], "offh offf"),
+        (F32, [128, 16, 3], "aah aaf m1h m1f sah saf"), (F32, [128, 8, 3], "mmh mmf sbh sbf sth stf vah vaf vbh vbf flh flf dfh dff"),
+        (F32, [128, 32, 3], "eqh eqf pph ppf"), (F32, [128, 4, 32], "trh trf")):
+    for _k in _n.split():
+        SCRATCH[_k] = ("sbuf", _s, _d)
+for _s, _n in (([128, 512], "stg0 stg1"), ([128, 32, 16], "uh uf nh nf"), ([128, 16, 32], "lh lf")):
+    for _k in _n.split():
+        SCRATCH[_k] = ("psum", _s, F32)
+SEMAPHORES = ["sv", "sa", "sp", "sg"] + ["d%d" % k for k in range(10)] + [a + b for a in ("arr", "loc") for b in "TLABC"]
+
+
+def rank_program(g, core, T, topo):
+    rank = T.rank_of(core)
+    if rank is None:
+        return
+    chips = [topo.chip(c) for c in T.cores]
+    mate = [r for r in range(len(chips)) if r != rank and chips[r] == chips[rank]][0]
+    part = [r for r in range(len(chips)) if chips[r] != chips[rank] and topo.die(T.cores[r]) == topo.die(core)][0]
+    low = min(rank, mate)
+    V, S, PE, SY = g.vector, g.scalar, g.tensor, g.sync
+    Q = {"v": V, "a": S, "p": PE, "s": SY, "g": g}
+    CS = {"v": "sv", "a": "sa", "p": "sp", "g": "sg"}
+    cnt, known, snap, Wt, Rd = {}, {q: {} for q in Q}, {}, {}, {}
+
+    def need(q, toks):
+        kn = known[q]
+        for sem, c in sorted(toks, key=lambda t: -t[1]):
+            if kn.get(sem, 0) < c:
+                Q[q].wait_ge(T.sem[sem], c)
+                kn[sem] = c
+                for s2, c2 in snap.get((sem, c), {}).items():
+                    kn[s2] = max(kn.get(s2, 0), c2)
+
+    def emit(q, fn, r=(), w=(), dma=None):
+        own = None if dma else CS[q]
+        t = set()
+        for k in r:
+            t |= set(Wt.get(k, []))
+        for k in w:
+            k0 = k.lstrip("+")
+            t |= set(Rd.get(k0, [])) | {tok for tok in Wt.get(k0, []) if k0 == k or tok[0] != own}
+        need(q, t)
+        sem, inc = (dma, 16) if dma else (own, 1)
+        fn().then_inc(T.sem[sem], inc)
+        cnt[sem] = cnt.get(sem, 0) + inc
+        tok = (sem, cnt[sem])
+        snap[tok] = dict(known[q])
+        for k in r:
+            Rd.setdefault(k, []).append(tok)
+        for k in w:
+            Wt[k.lstrip("+")], Rd[k.lstrip("+")] = [tok], []
+        return tok
+
+    def send(name, dst_rank, out, src, rkey, engines):
+        rid, pid, _ = topo.addr(T.cores[dst_rank])
+        need("g", Wt[rkey])
+        g.remote_dma(out, src, T.sem["arr" + name], T.sem["loc" + name], pid, rid, sum(1 << e for e in engines))
+        tok = ("loc" + name, len(engines))
+        cnt[tok[0]] = tok[1]
+        snap[tok] = dict(known["g"])
+        Rd.setdefault(rkey, []).append(tok)
+
+    def landing(name, key, n):
+        cnt["arr" + name] = n
+        Wt[key] = [("arr" + name, n)]
+
+    def ts(out, i, s1, s2, o0, *o1, r=(), w=()):
+        return emit("v", lambda: V.tensor_scalar(out, i, s1, s2, o0, *o1), r, w)
+
+    def tt(out, a, b, op, r=(), w=()):
+        return emit("v", lambda: V.tensor_tensor(out, a, b, op), r, w)
+
+    def cp(out, i, r=(), w=()):
+        return emit("v", lambda: V.tensor_copy(out, i), r, w)
+
+    def ms(out, c, w=()):
+        return emit("v", lambda: V.memset(out, c), (), w)
+
+    def act(out, i, r=(), w=(), bias=0.0):
+        return emit("a", lambda: S.activation(out, i, ACTF.Identity, bias=bias), r, w)
+
+    def mm(out, l, rhs, a, b, r=(), w=()):
+        return emit("p", lambda: PE.matmul(out, l, rhs, a, b), r, w)
+
+    def ld(q, sem, out, i, r=(), w=()):
+        return emit(q, lambda: Q[q].dma_start(out, i), r, w, dma=sem)
+
+    def io(key, pat, base, cm):
+        emit("g", lambda: g.iota(T[key][:], pat, base, cm), (), [key])
+
+    on = topo.engines(core, T.cores[mate])[::2]
+    off_ = topo.engines(core, T.cores[part])
+    landing("T", "tn", len(on))
+    landing("L", "lpn", len(off_))
+    for nm in "abc":
+        landing(nm.upper(), "in" + nm, len(off_))
+
+    ld("s", "d0", T.pl32[:], T.planes[:, :], w=["pl32"])
+    ld("a", "d1", T.pb32[0:64, :], T.planes[3::4, :], w=["pb32d"])
+    ld("s", "d2", T.pb32[64:128, :], T.nbr[:, :], w=["pb32n"])
+    ld("a", "d3", T.tl32[:], T.tet0[:, :], w=["tl32"])
+    ld("s", "d4", T.pf32[0:96, :], T.pts[:, :], w=["pf32p"])
+    ld("s", "d8", T.pf32[96:128, :], T.tet0[:, :], w=["pf32t"])
+    ld("s", "d5", T.pr32[0:24, :], T.pts[:, :], w=["pr32"])
+    io("ixp", [[1, 8], [8, 16]], 0, -1)
+    io("ixq", [[1, 16], [16, 4], [500, 4]], -1500, -1)
+    io("i_p", [[0, 8]], 0, 1)
+    io("ixd", [[1, 16], [16, 16]], 0, -1)
+    io("i_t", [[1, 64]], 0, 64)
+    ts(T.izp[:], T.ixp[:], 0, None, ALU.is_equal, r=["ixp"], w=["izp"])
+    ts(T.izq[:], T.ixq[:], 0, 2048, ALU.is_equal, ALU.mult, r=["ixq"], w=["izq"])
+    for k in range(8):
+        cp(T.yp[:, :, k, :], T.izp[:], r=["izp"], w=["+yp"])
+        act(T.qq[0:64, :, k, :], T.izq[0:64], r=["izq"], w=["+qq"])
+    ts(T.i_q[:], T.i_p[:], 3, None, ALU.bitwise_and, r=["i_p"], w=["i_q"])
+    ts(T.i_r[:], T.i_p[:], 15, 2, ALU.bitwise_and, ALU.arith_shift_right, r=["i_p"], w=["i_r"])
+    ts(T.xb[:], T.i_q[:], 3, None, ALU.is_equal, r=["i_q"], w=["xb"])
+    ts(T.wc[:], T.i_r[:], 0.25, None, ALU.mult, r=["i_r"], w=["wc"])
+    tt(T.wb[:], T.wc[:], T.xb[:], ALU.mult, r=["wc", "xb"], w=["wb"])
+    ts(T.plb[:], T.pl32[:], 1024, None, ALU.add, r=["pl32"], w=["plb"])
+    ts(T.pbb[0:64, :], T.pb32[0:64, :], 1024, None, ALU.add, r=["pb32d"], w=["pbb"])
+    ts(T.pl32[:], T.plb[:], 2047, None, ALU.bitwise_and, r=["plb"], w=["pl32"])
+    ts(T.pb32[0:64, :], T.pbb[0:64, :], 11, None, ALU.arith_shift_right, r=["pbb"], w=["pb32d"])
+    ts(T.tw[64:128, 128:192], T.pb32[64:128, :], -2047, None, ALU.add, r=["pb32n"], w=["tw2"])
+    ts(T.tw[:, 0:128], T.pl32[:], -1024, None, ALU.add, r=["pl32"], w=["tw0"])
+    Wt["tw"] = [cp(T.tw[0:64, 128:192], T.pb32[0:64, :], r=["pb32d"], w=["tw1"])]
+    send("T", mate, T.tn[:], T.tw[:], "tw", on)
+    cp(T.lp[0:96, :], T.pf32[0:96, :], r=["pf32p"], w=["lp0"])
+    Wt["lp"] = [ts(T.lp[96:128, :], T.pf32[96:128, :], -2047, None, ALU.add, r=["pf32t"], w=["lp1"])]
+    send("L", part, T.lpn[:], T.lp[:], "lp", off_)
+    ts(T.llh[:, 0:23], T.tl32[:], -2047, None, ALU.add, r=["tl32"], w=["llh"])
+    io("i_e", [[3, 8], [0, 4], [1, 4]], 0, -1)
+    io("i_m", [[-1, 16]], 256, 1)
+    io("i_g", [[-16, 2], [-32, 4]], 0, 1)
+    io("i_s", [[-4, 4], [-16, 2], [-32, 4]], 0, 1)
+    io("i_n", [[-1, 4], [-16, 2], [-32, 4]], 0, 1)
+    io("ic", [[32, 4], [1, 32]], 0, -1)
+    ts(T.izd[:], T.ixd[:], 0, None, ALU.is_equal, r=["ixd"], w=["izd"])
+    for k in range(8):
+        cp(T.yd[:, :, k, :], T.izd[:], r=["izd"], w=["+yd"])
+    ts(T.dn[:], T.i_t[:], 1023, None, ALU.bitwise_and, r=["i_t"], w=["dn"])
+    ts(T.tto[64:128, :], T.dn[64:128, :], 1024 * rank - 2047, None, ALU.add, r=["dn"], w=["tto"])
+    ts(T.ttm[64:128, :], T.dn[64:128, :], 1024 * mate - 2047, None, ALU.add, r=["dn"], w=["ttm"])
+
+    def first_list(s):
+        off, v = T["off" + s], T["ll" + s][:, 0:23]
+        ms(off[:, 23:24], 0, w=["+off" + s])
+        if low == 0:
+            ts(off[:, 0:23], v, 1, 2048, ALU.min, ALU.add, r=["ll" + s], w=["+off" + s])
+        else:
+            ts(off[:, 0:23], v, 0, None, ALU.max, r=["ll" + s], w=["+off" + s])
+
+    nb_ = [0, 0]
+
+    def bank():
+        nb_[0] ^= 1
+        return ("stg0", "stg1")[nb_[0]]
+
+    def copy_out(dst, src, bias, r, w):
+        nb_[1] ^= 1
+        if nb_[1]:
+            act(dst, src, r, w, bias=0.0 if bias is None else bias)
+        elif bias is None:
+            cp(dst, src, r, w)
+        else:
+            ts(dst, src, bias, None, ALU.add, r=r, w=w)
+
+    def expand_planes(src, key, z):
+        for h in range(2):
+            b = bank()
+            for tb in range(8 * h, 8 * h + 8):
+                o = T[b][:, 64 * (tb % 8):64 * (tb % 8) + 64]
+                mm(o, T.yp[:, tb // 2], src[:, 64 * (tb % 2):64 * (tb % 2) + 64], True, False, r=["yp", key], w=["+" + b])
+                mm(o, T.qq[0:64, tb], src[0:64, 128:192], False, True, r=["qq", key], w=["+" + b])
+            c0 = 1 + 1024 * z + 512 * h
+            copy_out(T.w1[:, c0:c0 + 512], T[b][:], T.wb[:, 0:1], [b, "wb"], ["w1_%d_%d" % (z, h)])
+
+    def moves(src, key, q, tcol, tkey):
+        n, P = src[64:128, 128:192], slice(64, 128)
+        ts(T.dn[P, :], n, 2047, None, ALU.add, r=[key], w=["dn"])
+        tt(T.ddd[P, :], n, tcol[P, :], ALU.subtract, r=[key, tkey], w=["ddd"])
+        ts(T.dsh[P, :], T.dn[P, :], 10, None, ALU.arith_shift_right, r=["dn"], w=["dsh"])
+        ts(T.dfl[P, :], T.dsh[P, :], q, FLAG, ALU.not_equal, ALU.mult, r=["dsh"], w=["dfl"])
+        tt(T.dd2[P, :], T.ddd[P, :], T.dfl[P, :], ALU.add, r=["ddd", "dfl"], w=["dd2"])
+        ts(T.dhi[P, :], T.dd2[P, :], 6, None, ALU.arith_shift_right, r=["dd2"], w=["dhi"])
+        ts(T.dlo[P, :], T.dd2[P, :], 63, None, ALU.bitwise_and, r=["dd2"], w=["dlo"])
+        cp(T.ex[P, :], T.dhi[P, :], r=["dhi"], w=["+ex"])
+        cp(T.ex[0:64, :], T.dlo[P, :], r=["dlo"], w=["+ex"])
+
+    def expand_moves(z):
+        for h in range(2):
+            b = bank()
+            for tb in range(8 * h, 8 * h + 8):
+                mm(T[b][:, 64 * (tb % 8):64 * (tb % 8) + 64], T.yd[:, tb], T.ex[:], True, True, r=["yd", "ex"], w=["+" + b])
+            c0 = 1 + 1024 * z + 512 * h
+            copy_out(T.w2[:, c0:c0 + 512], T[b][:], None, [b], ["w2_%d_%d" % (z, h)])
+
+    def expand_points(s):
+        b, x = bank(), T["x" + s]
+        mm(T[b][:, 0:368], T.e24[0:24], T["pt" + s][0:24, :], True, True, r=["e24", "pt" + s], w=["+" + b])
+        act(x[:, 0:368], T[b][:, 0:368], [b, "xb"], ["x" + s], bias=T.xb[:, 0:1])
+
+    def to_points(s):
+        rm, l = T["rm" + s], T["l" + s]
+        cp(rm[:, :, 23:24], T.z0[:, 0:8], r=["z0"], w=["+rm" + s])
+        for k in range(8):
+            ts(rm[:, k, 0:23], T["ll" + s][:, 0:23], T.gm[:, k:k + 1], None, ALU.mult, r=["gm", "ll" + s], w=["+rm" + s])
+        for b in range(8):
+            mm(l[:, 0, 0:24], T.ee[:, 112 - 16 * b:240 - 16 * b], rm[:, :, b::8], b == 0, b == 7, r=["ee", "rm" + s], w=["+l" + s])
+        cp(T["st" + s][:], l[:, 0, 0:24], r=["l" + s], w=["st" + s])
+
+    zw, zh = (0, 1) if rank == low else (1, 0)
+    moves(T.tw, "tw", rank, T.tto, "tto")
+    expand_planes(T.tw, "tw", zw)
+    expand_moves(zw)
+    ms(T.z0[:], 0, w=["z0"])
+    ts(T.e24[0:32], T.i_e[0:32], 0, None, ALU.is_equal, r=["i_e"], w=["e24"])
+    ms(T.e24[0:32, :, :, 3], 0, w=["e24"])
+    cp(T.pth[0:24, :], T.pr32[0:24, :], r=["pr32"], w=["pth"])
+    ms(T.xh[:, 368:384], 0, w=["xhp"])
+    ms(T.xf[:, 368:384], 0, w=["xfp"])
+    expand_points("h")
+    first_list("h")
+    ms(T.ee[:], 0, w=["ee"])
+    ms(T.cc[:], 0, w=["cc"])
+    ts(T.i_q[:, 0:8], T.i_g[:], 4, None, ALU.arith_shift_right, r=["i_g"], w=["i_q"])
+    ts(T.pbb[:, 0:16], T.i_m[:], 15, None, ALU.bitwise_and, r=["i_m"], w=["pbb"])
+    ts(T.s4a[:], T.i_s[:], 0, 4, ALU.is_ge, ALU.mult, r=["i_s"], w=["s4a"])
+    ts(T.s4b[:], T.i_s[:], 3, None, ALU.is_le, r=["i_s"], w=["s4b"])
+    ts(T.rna[:], T.i_n[:], 4, 64, ALU.is_equal, ALU.mult, r=["i_n"], w=["rna"])
+    ts(T.rnb[:], T.i_n[:], 0, None, ALU.is_equal, r=["i_n"], w=["rnb"])
+    ts(T.gm[:], T.i_q[:], 0, None, ALU.is_equal, r=["i_q"], w=["gm"])
+    ts(T.ee[:, 112:128], T.pbb[:, 0:16], 0, None, ALU.is_equal, r=["pbb"], w=["ee"])
+    tt(T.s4[:], T.s4a[:], T.s4b[:], ALU.mult, r=["s4a", "s4b"], w=["s4"])
+    tt(T.rn[:], T.rna[:], T.rnb[:], ALU.add, r=["rna", "rnb"], w=["rn"])
+    for k, (c, val) in enumerate(((0, 0), (16, 16), (0, -16), (16, 0))):
+        ts(T.cc[:, k, :, c:c + 16], T.ic[:, :, c:c + 16], val, None, ALU.is_equal, r=["ic"], w=["+cc" if k else "cc"])
+    for s in "hf":
+        for e in range(2):
+            cp(T["tb" + s][:, e], T.z0[:, 0:256], r=["z0"], w=["tb%s%d" % (s, e)])
+    for c in (0, WN - 1):
+        cp(T.w1[:, c:c + 1], T.xb[:, 0:1], r=["xb"], w=["+w1_d"])
+        ms(T.w2[:, c:c + 1], 0, w=["+w2_d"])
+    to_points("h")
+    ld("s", "d9", T.llf[:, 0:23], T.lpn[96:128, :], r=["lpn"], w=["llf"])
+    ld("s", "d6", T.ptf[0:24, :], T.lpn[0:96, :], r=["lpn"], w=["ptf"])
+    moves(T.tn, "tn", mate, T.ttm, "ttm")
+    expand_planes(T.tn, "tn", zh)
+    expand_moves(zh)
+
+    halves = ["_d"] + ["_%d_%d" % (z, h) for z in range(2) for h in range(2)]
+
+    def gather(s):
+        off = T["off" + s][:, 0:24]
+        emit("v", lambda: V.tensor_tensor(T["pr" + s][:], T.w1[:, 0:WN].indirect(off), T["x" + s][:], ALU.mult),
+             ["w1" + k for k in halves] + ["off" + s, "x" + s, "x%sp" % s], ["pr" + s])
+        act(T["nb" + s][:], T.w2[:, 0:WN].indirect(off), ["w2" + k for k in halves] + ["off" + s], ["nb" + s])
+        for d, src, m in (("u", "pr", "s4"), ("n", "nb", "rn")):
+            for r in range(3):
+                mm(T[d + s][:, :, r], T[src + s][:, 128 * r:128 * r + 128], T[m][:], True, True, r=[src + s, m], w=["+" + d + s])
+
+    def choose(s):
+        u, n = T["u" + s], T["n" + s]
+        aa, m1, mn, eq, pp, sa, sb = (T[k + s] for k in ("aa", "m1", "mm", "eq", "pp", "sa", "sb"))
+        ts(aa[:], u[:, 0:16, 0:3], -0.5, None, ALU.min, r=["u" + s], w=["aa" + s])
+        tt(m1[:], aa[:], u[:, 16:32, 0:3], ALU.min, r=["aa" + s, "u" + s], w=["m1" + s])
+        tt(mn[:], m1[:, 0:8, :], m1[:, 8:16, :], ALU.min, r=["m1" + s], w=["mm" + s])
+        for f in range(4):
+            tt(eq[:, 8 * f:8 * f + 8, :], u[:, 8 * f:8 * f + 8, 0:3], mn[:], ALU.is_equal, r=["u" + s, "mm" + s], w=["+eq" + s])
+        tt(pp[:], eq[:], n[:, :, 0:3], ALU.mult, r=["eq" + s, "n" + s], w=["pp" + s])
+        tt(sa[:], pp[:, 0:16, :], pp[:, 16:32, :], ALU.add, r=["pp" + s], w=["sa" + s])
+        tt(sb[:], sa[:, 0:8, :], sa[:, 8:16, :], ALU.add, r=["sa" + s], w=["sb" + s])
+
+    def to_list(s, a, b, keys, last=False):
+        tb, l, tr = T["tb" + s], T["l" + s], T["tr" + s]
+        for e in range(2):
+            k = "tb%s%d" % (s, e)
+            tt(tb[:, e, :, e:e + 5:2], a, b, ALU.add, r=keys, w=[k])
+            for par in range(2):
+                mm(l[:, 0:4, :], tb[:, e, 4 * par:4 * par + 4, :], T.cc[:, 2 * e + par], e + par == 0, e + par == 2, r=[k, "cc"], w=["+l" + s])
+        emit("v", lambda: V.transpose(tr[:], l[:, 0:4, :]), ["l" + s], ["tr" + s])
+        for r in range(3):
+            src, c = tr[:, :, 2 * r:2 * r + 2], slice(8 * r, 8 * r + 8)
+            if last:
+                ts(T.yo[:, c], src, 2047, None, ALU.add, r=["tr" + s], w=["+yo"])
+            elif low == 0:
+                ts(T["off" + s][:, c], src, 1, 2048, ALU.min, ALU.add, r=["tr" + s], w=["+off" + s])
+            else:
+                ts(T["off" + s][:, c], src, 2049, 0, ALU.min, ALU.max, r=["tr" + s], w=["+off" + s])
+
+    def step1_end(s):
+        choose(s)
+        to_list(s, T["sb" + s][:], T["st" + s][:], ["sb" + s, "st" + s])
+        tt(T["va" + s][:], T["sb" + s][:], T["st" + s][:], ALU.add, r=["sb" + s, "st" + s], w=["va" + s])
+
+    def step2_end(s, wo, name):
+        choose(s)
+        vb, fl, w = T["vb" + s], T["fl" + s], T[wo + s]
+        tt(vb[:], T["sb" + s][:], T["va" + s][:], ALU.add, r=["sb" + s, "va" + s], w=["vb" + s])
+        ts(fl[:], vb[:], 3000, -FLAG, ALU.is_ge, ALU.mult, r=["vb" + s], w=["fl" + s])
+        tt(w[:], vb[:], fl[:], ALU.add, r=["vb" + s, "fl" + s], w=[wo + s])
+        if name:
+            send(name, part, T["in" + name.lower()][:], w[:], wo + s, off_)
+        tt(T["df" + s][:], w[:], T["st" + s][:], ALU.subtract, r=[wo + s, "st" + s], w=["df" + s])
+
+    def merge(s, inn, last=False):
+        to_list(s, T["df" + s][:], T[inn][:], ["df" + s, inn], last)
+        if not last:
+            tt(T["st" + s][:], T["df" + s][:], T[inn][:], ALU.add, r=["df" + s, inn], w=["st" + s])
+
+    gather("h")
+    step1_end("h")
+    gather("h")
+    first_list("f")
+    expand_points("f")
+    to_points("f")
+    gather("f")
+    step2_end("h", "wo", "A")
+    step1_end("f")
+    gather("f")
+    step2_end("f", "wo", "B")
+    merge("f", "ina")
+    gather("f")
+    step1_end("f")
+    gather("f")
+    merge("h", "inb")
+    gather("h")
+    step2_end("f", "we", "C")
+    step1_end("h")
+    gather("h")
+    step2_end("h", "we", None)
+    merge("h", "inc", last=True)
+    ld("s", "d7", T.y[:, :], T.yo[:, 0:23], r=["yo"])
+    need("g", [(k, c) for k, c in cnt.items()])

@@ -6,14 +6,14 @@ FLAG = 8192
 SCRATCH = {}
 for _d, _s, _n in (
         (I32, [128, 8, 16], "ixp"), (I32, [128, 16, 16], "ixd ixq"), (I32, [128, 4, 32], "ic"), (I32, [128, 32], "i_s i_n"),
-        (I32, [128, 8, 4, 4], "i_e"), (I32, [128, 8], "i_p i_g i_q i_r"), (I32, [128, 16], "i_m"),
-        (I32, [128, 64], "i_t pb32 pbb dn dsh dd2 dhi dlo"), (I32, [128, 128], "pl32 plb"), (I32, [128, 23], "tl32"),
+        (I32, [128, 8, 4, 4], "i_e"), (I32, [128, 8], "i_p i_g i_q i_r i_h"), (I32, [128, 16], "i_m i_l"),
+        (I32, [128, 64], "i_t pb32 pbb dt dn dsh dd2 dhi dlo dnm dshm dd2m dhim dlom"), (I32, [128, 128], "pl32 plb"), (I32, [128, 23], "tl32"),
         (I32, [128, 92], "pf32"), (I32, [128, 368], "pr32"), (B16, [128, 8, 16], "izp"), (B16, [128, 16, 16], "izd izq"),
         (B16, [128, 8, 8, 16], "yp"), (B16, [128, 16, 8, 16], "yd qq"), (B16, [128, 4, 4, 32], "cc"), (B16, [128, 512], "z0"),
         (B16, [128, 32], "rn"), (B16, [128, 8, 4, 4], "e24"), (B16, [128, 240], "ee"), (B16, [128, 2064], "w2"),
         (F32, [128, 2056], "w1"), (F32, [128, 32], "s4 s4a s4b rna rnb"), (F32, [128, 8], "gm xb wb wc"),
-        (F32, [128, 64], "tto ttm dfl ddd"), (F32, [128, 24], "yo"), (F16, [128, 192], "tw tn"), (F16, [128, 92], "lp lpn"),
-        (F16, [128, 24], "llh llf"), (F16, [128, 64], "ex"), (F16, [128, 8, 3], "ina inb inc woh wof weh wef"),
+        (F32, [128, 64], "tto ttm dfl ddd dflm dddm"), (F32, [128, 24], "yo"), (F16, [128, 192], "tw tn"), (F16, [128, 92], "lp lpn"),
+        (F16, [128, 24], "llh llf"), (F16, [128, 64], "ex exm"), (F16, [128, 8, 3], "ina inb inc woh wof weh wef"),
         (F16, [128, 368], "pth ptf"), (F16, [128, 8, 24], "rmh rmf"), (F16, [128, 2, 8, 32], "tbh tbf"),
         (F32, [128, 384], "xh xf prh prf"), (B16, [128, 384], "nbh nbf"), (U16, [128, 24], "offh offf"),
         (F32, [128, 16, 3], "aah aaf m1h m1f sah saf"), (F32, [128, 8, 3], "mmh mmf sbh sbf sth stf vah vaf vbh vbf flh flf dfh dff"),
@@ -24,6 +24,10 @@ for _s, _n in (([128, 512], "stg0 stg1"), ([128, 32, 16], "uh uf nh nf"), ([128,
     for _k in _n.split():
         SCRATCH[_k] = ("psum", _s, F32)
 SEMAPHORES = ["sv", "sa", "sp", "sg"] + ["d%d" % k for k in range(10)] + [a + b for a in ("arr", "loc") for b in "TLABC"]
+CS = {"v": "sv", "a": "sa", "p": "sp", "g": "sg"}
+WAKE = 0.12
+SHORT = {"v": 0.07, "a": 0.3, "p": 0.065, "g": 0.4, "s": 0.06}
+DMA_T, SEND_T = 2.2, {"T": 6.0, "L": 4.0, "A": 3.0, "B": 3.0, "C": 3.0}
 
 
 def rank_program(g, core, T, topo):
@@ -36,81 +40,64 @@ def rank_program(g, core, T, topo):
     low = min(rank, mate)
     V, S, PE, SY = g.vector, g.scalar, g.tensor, g.sync
     Q = {"v": V, "a": S, "p": PE, "s": SY, "g": g}
-    CS = {"v": "sv", "a": "sa", "p": "sp", "g": "sg"}
-    cnt, known, snap, Wt, Rd = {}, {q: {} for q in Q}, {}, {}, {}
 
-    def need(q, toks):
-        kn = known[q]
-        for sem, c in sorted(toks, key=lambda t: -t[1]):
-            if kn.get(sem, 0) < c:
-                Q[q].wait_ge(T.sem[sem], c)
-                kn[sem] = c
-                for s2, c2 in snap.get((sem, c), {}).items():
-                    kn[s2] = max(kn.get(s2, 0), c2)
+    ops, base, app, rd = [], {}, {}, {}
 
-    def emit(q, fn, r=(), w=(), dma=None):
-        own = None if dma else CS[q]
-        t = set()
+    def add(q, fn, r=(), w=(), cost=None, dma=None, send=None, arr=None):
+        n = len(ops)
+        hard, soft = set(), set()
         for k in r:
-            t |= set(Wt.get(k, []))
+            hard |= set(base.get(k, [])) | set(app.get(k, []))
         for k in w:
             k0 = k.lstrip("+")
-            t |= set(Rd.get(k0, [])) | {tok for tok in Wt.get(k0, []) if k0 == k or tok[0] != own}
-        need(q, t)
-        sem, inc = (dma, 16) if dma else (own, 1)
-        fn().then_inc(T.sem[sem], inc)
-        cnt[sem] = cnt.get(sem, 0) + inc
-        tok = (sem, cnt[sem])
-        snap[tok] = dict(known[q])
+            if k0 != k:
+                if rd.get(k0):
+                    base[k0], app[k0] = list(rd[k0]), []
+                    rd[k0] = []
+                hard |= set(base.get(k0, []))
+                if q == "p":
+                    soft |= set(app.get(k0, [])[-1:])
+                app.setdefault(k0, []).append(n)
+            else:
+                hard |= set(base.get(k0, [])) | set(app.get(k0, [])) | set(rd.get(k0, []))
+                base[k0], app[k0], rd[k0] = [n], [], []
         for k in r:
-            Rd.setdefault(k, []).append(tok)
-        for k in w:
-            Wt[k.lstrip("+")], Rd[k.lstrip("+")] = [tok], []
-        return tok
+            rd.setdefault(k, []).append(n)
+        ops.append(dict(q=q, fn=fn, hard=hard - {n}, soft=soft, cost=SHORT[q] if cost is None else cost, dma=dma, send=send, arr=arr))
 
-    def send(name, dst_rank, out, src, rkey, engines):
-        rid, pid, _ = topo.addr(T.cores[dst_rank])
-        need("g", Wt[rkey])
-        g.remote_dma(out, src, T.sem["arr" + name], T.sem["loc" + name], pid, rid, sum(1 << e for e in engines))
-        tok = ("loc" + name, len(engines))
-        cnt[tok[0]] = tok[1]
-        snap[tok] = dict(known["g"])
-        Rd.setdefault(rkey, []).append(tok)
+    def ts(out, i, s1, s2, o0, *o1, r=(), w=(), cost=None):
+        add("v", lambda: V.tensor_scalar(out, i, s1, s2, o0, *o1), r, w, cost)
 
-    def landing(name, key, n):
-        cnt["arr" + name] = n
-        Wt[key] = [("arr" + name, n)]
+    def tt(out, a, b, op, r=(), w=(), cost=None):
+        add("v", lambda: V.tensor_tensor(out, a, b, op), r, w, cost)
 
-    def ts(out, i, s1, s2, o0, *o1, r=(), w=()):
-        return emit("v", lambda: V.tensor_scalar(out, i, s1, s2, o0, *o1), r, w)
+    def cp(out, i, r=(), w=(), cost=None):
+        add("v", lambda: V.tensor_copy(out, i), r, w, cost)
 
-    def tt(out, a, b, op, r=(), w=()):
-        return emit("v", lambda: V.tensor_tensor(out, a, b, op), r, w)
+    def ms(out, c, w=(), cost=None):
+        add("v", lambda: V.memset(out, c), (), w, cost)
 
-    def cp(out, i, r=(), w=()):
-        return emit("v", lambda: V.tensor_copy(out, i), r, w)
+    def act(out, i, r=(), w=(), bias=0.0, cost=None):
+        add("a", lambda: S.activation(out, i, ACTF.Identity, bias=bias), r, w, cost)
 
-    def ms(out, c, w=()):
-        return emit("v", lambda: V.memset(out, c), (), w)
-
-    def act(out, i, r=(), w=(), bias=0.0):
-        return emit("a", lambda: S.activation(out, i, ACTF.Identity, bias=bias), r, w)
-
-    def mm(out, l, rhs, a, b, r=(), w=()):
-        return emit("p", lambda: PE.matmul(out, l, rhs, a, b), r, w)
+    def mm(out, l, rhs, a, b, r=(), w=(), cost=None):
+        add("p", lambda: PE.matmul(out, l, rhs, a, b), r, w, cost)
 
     def ld(q, sem, out, i, r=(), w=()):
-        return emit(q, lambda: Q[q].dma_start(out, i), r, w, dma=sem)
+        add(q, lambda: Q[q].dma_start(out, i), r, w, dma=sem)
 
-    def io(key, pat, base, cm):
-        emit("g", lambda: g.iota(T[key][:], pat, base, cm), (), [key])
+    def io(key, pat, first, cm):
+        add("g", lambda: g.iota(T[key][:], pat, first, cm), (), [key])
+
+    def send(name, dst_rank, out, src, keys, landing, engines):
+        rid, pid, _ = topo.addr(T.cores[dst_rank])
+        add("g", lambda: g.remote_dma(out, src, T.sem["arr" + name], T.sem["loc" + name], pid, rid, sum(1 << e for e in engines)),
+            keys, cost=0.6, send=(name, len(engines)))
+        ops.append(dict(q=None, fn=None, hard={len(ops) - 1}, soft=set(), cost=0.0, dma=None, send=None, arr=(name, len(engines))))
+        base[landing] = [len(ops) - 1]
 
     on = topo.engines(core, T.cores[mate])[::2]
     off_ = topo.engines(core, T.cores[part])
-    landing("T", "tn", len(on))
-    landing("L", "lpn", len(off_))
-    for nm in "abc":
-        landing(nm.upper(), "in" + nm, len(off_))
 
     ld("s", "d0", T.pl32[:], T.planes[:, :], w=["pl32"])
     ld("a", "d1", T.pb32[0:64, :], T.planes[3::4, :], w=["pb32d"])
@@ -119,45 +106,70 @@ def rank_program(g, core, T, topo):
     ld("s", "d4", T.pf32[0:96, :], T.pts[:, :], w=["pf32p"])
     ld("s", "d8", T.pf32[96:128, :], T.tet0[:, :], w=["pf32t"])
     ld("s", "d5", T.pr32[0:24, :], T.pts[:, :], w=["pr32"])
-    io("ixp", [[1, 8], [8, 16]], 0, -1)
-    io("ixq", [[1, 16], [16, 4], [500, 4]], -1500, -1)
-    io("i_p", [[0, 8]], 0, 1)
-    io("ixd", [[1, 16], [16, 16]], 0, -1)
-    io("i_t", [[1, 64]], 0, 64)
-    ts(T.izp[:], T.ixp[:], 0, None, ALU.is_equal, r=["ixp"], w=["izp"])
-    ts(T.izq[:], T.ixq[:], 0, 2048, ALU.is_equal, ALU.mult, r=["ixq"], w=["izq"])
-    for k in range(8):
-        cp(T.yp[:, :, k, :], T.izp[:], r=["izp"], w=["+yp"])
-        act(T.qq[0:64, :, k, :], T.izq[0:64], r=["izq"], w=["+qq"])
-    ts(T.i_q[:], T.i_p[:], 3, None, ALU.bitwise_and, r=["i_p"], w=["i_q"])
-    ts(T.i_r[:], T.i_p[:], 15, 2, ALU.bitwise_and, ALU.arith_shift_right, r=["i_p"], w=["i_r"])
-    ts(T.xb[:], T.i_q[:], 3, None, ALU.is_equal, r=["i_q"], w=["xb"])
-    ts(T.wc[:], T.i_r[:], 0.25, None, ALU.mult, r=["i_r"], w=["wc"])
-    tt(T.wb[:], T.wc[:], T.xb[:], ALU.mult, r=["wc", "xb"], w=["wb"])
     ts(T.plb[:], T.pl32[:], 1024, None, ALU.add, r=["pl32"], w=["plb"])
     ts(T.pbb[0:64, :], T.pb32[0:64, :], 1024, None, ALU.add, r=["pb32d"], w=["pbb"])
     ts(T.pl32[:], T.plb[:], 2047, None, ALU.bitwise_and, r=["plb"], w=["pl32"])
     ts(T.pb32[0:64, :], T.pbb[0:64, :], 11, None, ALU.arith_shift_right, r=["pbb"], w=["pb32d"])
     ts(T.tw[64:128, 128:192], T.pb32[64:128, :], -2047, None, ALU.add, r=["pb32n"], w=["tw2"])
     ts(T.tw[:, 0:128], T.pl32[:], -1024, None, ALU.add, r=["pl32"], w=["tw0"])
-    Wt["tw"] = [cp(T.tw[0:64, 128:192], T.pb32[0:64, :], r=["pb32d"], w=["tw1"])]
-    send("T", mate, T.tn[:], T.tw[:], "tw", on)
+    cp(T.tw[0:64, 128:192], T.pb32[0:64, :], r=["pb32d"], w=["tw1"])
+    send("T", mate, T.tn[:], T.tw[:], ["tw0", "tw1", "tw2"], "tn", on)
     cp(T.lp[0:96, :], T.pf32[0:96, :], r=["pf32p"], w=["lp0"])
-    Wt["lp"] = [ts(T.lp[96:128, :], T.pf32[96:128, :], -2047, None, ALU.add, r=["pf32t"], w=["lp1"])]
-    send("L", part, T.lpn[:], T.lp[:], "lp", off_)
+    ts(T.lp[96:128, :], T.pf32[96:128, :], -2047, None, ALU.add, r=["pf32t"], w=["lp1"])
+    send("L", part, T.lpn[:], T.lp[:], ["lp0", "lp1"], "lpn", off_)
     ts(T.llh[:, 0:23], T.tl32[:], -2047, None, ALU.add, r=["tl32"], w=["llh"])
+    io("ixp", [[1, 8], [8, 16]], 0, -1)
+    io("ixq", [[1, 16], [16, 4], [500, 4]], -1500, -1)
+    io("i_p", [[0, 8]], 0, 1)
+    io("ixd", [[1, 16], [16, 16]], 0, -1)
+    io("i_t", [[1, 64]], 0, 64)
     io("i_e", [[3, 8], [0, 4], [1, 4]], 0, -1)
     io("i_m", [[-1, 16]], 256, 1)
     io("i_g", [[-16, 2], [-32, 4]], 0, 1)
     io("i_s", [[-4, 4], [-16, 2], [-32, 4]], 0, 1)
     io("i_n", [[-1, 4], [-16, 2], [-32, 4]], 0, 1)
     io("ic", [[32, 4], [1, 32]], 0, -1)
-    ts(T.izd[:], T.ixd[:], 0, None, ALU.is_equal, r=["ixd"], w=["izd"])
+    ts(T.izp[:], T.ixp[:], 0, None, ALU.is_equal, r=["ixp"], w=["izp"], cost=0.13)
+    ts(T.izq[:], T.ixq[:], 0, 2048, ALU.is_equal, ALU.mult, r=["ixq"], w=["izq"], cost=0.26)
+    ts(T.izd[:], T.ixd[:], 0, None, ALU.is_equal, r=["ixd"], w=["izd"], cost=0.26)
     for k in range(8):
-        cp(T.yd[:, :, k, :], T.izd[:], r=["izd"], w=["+yd"])
-    ts(T.dn[:], T.i_t[:], 1023, None, ALU.bitwise_and, r=["i_t"], w=["dn"])
-    ts(T.tto[64:128, :], T.dn[64:128, :], 1024 * rank - 2047, None, ALU.add, r=["dn"], w=["tto"])
-    ts(T.ttm[64:128, :], T.dn[64:128, :], 1024 * mate - 2047, None, ALU.add, r=["dn"], w=["ttm"])
+        cp(T.yp[:, :, k, :], T.izp[:], r=["izp"], w=["+yp"])
+        act(T.qq[0:64, :, k, :], T.izq[0:64], r=["izq"], w=["+qq"], cost=0.45)
+        cp(T.yd[:, :, k, :], T.izd[:], r=["izd"], w=["+yd"], cost=0.13)
+    ts(T.i_q[:], T.i_p[:], 3, None, ALU.bitwise_and, r=["i_p"], w=["i_q"])
+    ts(T.i_r[:], T.i_p[:], 15, 2, ALU.bitwise_and, ALU.arith_shift_right, r=["i_p"], w=["i_r"])
+    ts(T.xb[:], T.i_q[:], 3, None, ALU.is_equal, r=["i_q"], w=["xb"])
+    ts(T.wc[:], T.i_r[:], 0.25, None, ALU.mult, r=["i_r"], w=["wc"])
+    tt(T.wb[:], T.wc[:], T.xb[:], ALU.mult, r=["wc", "xb"], w=["wb"])
+    ts(T.dt[:], T.i_t[:], 1023, None, ALU.bitwise_and, r=["i_t"], w=["dt"])
+    ts(T.tto[64:128, :], T.dt[64:128, :], 1024 * rank - 2047, None, ALU.add, r=["dt"], w=["tto"])
+    ts(T.ttm[64:128, :], T.dt[64:128, :], 1024 * mate - 2047, None, ALU.add, r=["dt"], w=["ttm"])
+    ms(T.z0[:], 0, w=["z0"], cost=0.26)
+    ts(T.e24[0:32], T.i_e[0:32], 0, None, ALU.is_equal, r=["i_e"], w=["e24"], cost=0.13)
+    ms(T.e24[0:32, :, :, 3], 0, w=["e24"])
+    cp(T.pth[0:24, :], T.pr32[0:24, :], r=["pr32"], w=["pth"], cost=0.37)
+    ms(T.xh[:, 368:384], 0, w=["xhp"])
+    ms(T.xf[:, 368:384], 0, w=["xfp"])
+    ms(T.ee[:], 0, w=["ee"], cost=0.12)
+    ms(T.cc[:], 0, w=["cc"], cost=0.26)
+    ts(T.i_h[:], T.i_g[:], 4, None, ALU.arith_shift_right, r=["i_g"], w=["i_h"])
+    ts(T.i_l[:], T.i_m[:], 15, None, ALU.bitwise_and, r=["i_m"], w=["i_l"])
+    ts(T.s4a[:], T.i_s[:], 0, 4, ALU.is_ge, ALU.mult, r=["i_s"], w=["s4a"])
+    ts(T.s4b[:], T.i_s[:], 3, None, ALU.is_le, r=["i_s"], w=["s4b"])
+    ts(T.rna[:], T.i_n[:], 4, 64, ALU.is_equal, ALU.mult, r=["i_n"], w=["rna"])
+    ts(T.rnb[:], T.i_n[:], 0, None, ALU.is_equal, r=["i_n"], w=["rnb"])
+    ts(T.gm[:], T.i_h[:], 0, None, ALU.is_equal, r=["i_h"], w=["gm"])
+    ts(T.ee[:, 112:128], T.i_l[:], 0, None, ALU.is_equal, r=["i_l"], w=["ee"])
+    tt(T.s4[:], T.s4a[:], T.s4b[:], ALU.mult, r=["s4a", "s4b"], w=["s4"])
+    tt(T.rn[:], T.rna[:], T.rnb[:], ALU.add, r=["rna", "rnb"], w=["rn"])
+    for k, (c, val) in enumerate(((0, 0), (16, 16), (0, -16), (16, 0))):
+        ts(T.cc[:, k, :, c:c + 16], T.ic[:, :, c:c + 16], val, None, ALU.is_equal, r=["ic"], w=["+cc"])
+    for s in "hf":
+        for e in range(2):
+            cp(T["tb" + s][:, e], T.z0[:, 0:256], r=["z0"], w=["tb%s%d" % (s, e)], cost=0.13)
+    for c in (0, WN - 1):
+        cp(T.w1[:, c:c + 1], T.xb[:, 0:1], r=["xb"], w=["+w1_d"])
+        ms(T.w2[:, c:c + 1], 0, w=["+w2_d"])
 
     def first_list(s):
         off, v = T["off" + s], T["ll" + s][:, 0:23]
@@ -176,46 +188,47 @@ def rank_program(g, core, T, topo):
     def copy_out(dst, src, bias, r, w):
         nb_[1] ^= 1
         if nb_[1]:
-            act(dst, src, r, w, bias=0.0 if bias is None else bias)
+            act(dst, src, r, w, bias=0.0 if bias is None else bias, cost=0.7)
         elif bias is None:
-            cp(dst, src, r, w)
+            cp(dst, src, r, w, cost=0.5)
         else:
-            ts(dst, src, bias, None, ALU.add, r=r, w=w)
+            ts(dst, src, bias, None, ALU.add, r=r, w=w, cost=0.5)
 
-    def expand_planes(src, key, z):
+    def expand_planes(src, keys, z):
         for h in range(2):
             b = bank()
             for tb in range(8 * h, 8 * h + 8):
-                o = T[b][:, 64 * (tb % 8):64 * (tb % 8) + 64]
-                mm(o, T.yp[:, tb // 2], src[:, 64 * (tb % 2):64 * (tb % 2) + 64], True, False, r=["yp", key], w=["+" + b])
-                mm(o, T.qq[0:64, tb], src[0:64, 128:192], False, True, r=["qq", key], w=["+" + b])
+                o, lh, rh = T[b][:, 64 * (tb % 8):64 * (tb % 8) + 64], T.yp[:, tb // 2], src[:, 64 * (tb % 2):64 * (tb % 2) + 64]
+                mm(o, lh, rh, True, False, r=["yp", keys[0]], w=["+" + b])
+                mm(o, T.qq[0:64, tb], src[0:64, 128:192], False, True, r=["qq", keys[1]], w=["+" + b])
             c0 = 1 + 1024 * z + 512 * h
             copy_out(T.w1[:, c0:c0 + 512], T[b][:], T.wb[:, 0:1], [b, "wb"], ["w1_%d_%d" % (z, h)])
 
-    def moves(src, key, q, tcol, tkey):
+    def moves(src, key, q, tcol, m):
         n, P = src[64:128, 128:192], slice(64, 128)
-        ts(T.dn[P, :], n, 2047, None, ALU.add, r=[key], w=["dn"])
-        tt(T.ddd[P, :], n, tcol[P, :], ALU.subtract, r=[key, tkey], w=["ddd"])
-        ts(T.dsh[P, :], T.dn[P, :], 10, None, ALU.arith_shift_right, r=["dn"], w=["dsh"])
-        ts(T.dfl[P, :], T.dsh[P, :], q, FLAG, ALU.not_equal, ALU.mult, r=["dsh"], w=["dfl"])
-        tt(T.dd2[P, :], T.ddd[P, :], T.dfl[P, :], ALU.add, r=["ddd", "dfl"], w=["dd2"])
-        ts(T.dhi[P, :], T.dd2[P, :], 6, None, ALU.arith_shift_right, r=["dd2"], w=["dhi"])
-        ts(T.dlo[P, :], T.dd2[P, :], 63, None, ALU.bitwise_and, r=["dd2"], w=["dlo"])
-        cp(T.ex[P, :], T.dhi[P, :], r=["dhi"], w=["+ex"])
-        cp(T.ex[0:64, :], T.dlo[P, :], r=["dlo"], w=["+ex"])
+        dn, dd, sh, fl, d2, hi, lo, ex = (T[k + m] for k in ("dn", "ddd", "dsh", "dfl", "dd2", "dhi", "dlo", "ex"))
+        ts(dn[P, :], n, 2047, None, ALU.add, r=[key], w=["dn" + m])
+        tt(dd[P, :], n, T[tcol][P, :], ALU.subtract, r=[key, tcol], w=["dd" + m], cost=0.13)
+        ts(sh[P, :], dn[P, :], 10, None, ALU.arith_shift_right, r=["dn" + m], w=["sh" + m])
+        ts(fl[P, :], sh[P, :], q, FLAG, ALU.not_equal, ALU.mult, r=["sh" + m], w=["fl" + m + "_"])
+        tt(d2[P, :], dd[P, :], fl[P, :], ALU.add, r=["dd" + m, "fl" + m + "_"], w=["d2" + m], cost=0.13)
+        ts(hi[P, :], d2[P, :], 6, None, ALU.arith_shift_right, r=["d2" + m], w=["hi" + m])
+        ts(lo[P, :], d2[P, :], 63, None, ALU.bitwise_and, r=["d2" + m], w=["lo" + m])
+        cp(ex[P, :], hi[P, :], r=["hi" + m], w=["+ex" + m])
+        cp(ex[0:64, :], lo[P, :], r=["lo" + m], w=["+ex" + m])
 
-    def expand_moves(z):
+    def expand_moves(z, m):
         for h in range(2):
             b = bank()
             for tb in range(8 * h, 8 * h + 8):
-                mm(T[b][:, 64 * (tb % 8):64 * (tb % 8) + 64], T.yd[:, tb], T.ex[:], True, True, r=["yd", "ex"], w=["+" + b])
+                mm(T[b][:, 64 * (tb % 8):64 * (tb % 8) + 64], T.yd[:, tb], T["ex" + m][:], True, True, r=["yd", "ex" + m], w=["+" + b])
             c0 = 1 + 1024 * z + 512 * h
             copy_out(T.w2[:, c0:c0 + 512], T[b][:], None, [b], ["w2_%d_%d" % (z, h)])
 
     def expand_points(s):
         b, x = bank(), T["x" + s]
-        mm(T[b][:, 0:368], T.e24[0:24], T["pt" + s][0:24, :], True, True, r=["e24", "pt" + s], w=["+" + b])
-        act(x[:, 0:368], T[b][:, 0:368], [b, "xb"], ["x" + s], bias=T.xb[:, 0:1])
+        mm(T[b][:, 0:368], T.e24[0:24], T["pt" + s][0:24, :], True, True, r=["e24", "pt" + s], w=["+" + b], cost=0.37)
+        act(x[:, 0:368], T[b][:, 0:368], [b, "xb"], ["x" + s], bias=T.xb[:, 0:1], cost=0.57)
 
     def to_points(s):
         rm, l = T["rm" + s], T["l" + s]
@@ -227,54 +240,31 @@ def rank_program(g, core, T, topo):
         cp(T["st" + s][:], l[:, 0, 0:24], r=["l" + s], w=["st" + s])
 
     zw, zh = (0, 1) if rank == low else (1, 0)
-    moves(T.tw, "tw", rank, T.tto, "tto")
-    expand_planes(T.tw, "tw", zw)
-    expand_moves(zw)
-    ms(T.z0[:], 0, w=["z0"])
-    ts(T.e24[0:32], T.i_e[0:32], 0, None, ALU.is_equal, r=["i_e"], w=["e24"])
-    ms(T.e24[0:32, :, :, 3], 0, w=["e24"])
-    cp(T.pth[0:24, :], T.pr32[0:24, :], r=["pr32"], w=["pth"])
-    ms(T.xh[:, 368:384], 0, w=["xhp"])
-    ms(T.xf[:, 368:384], 0, w=["xfp"])
+    moves(T.tw, "tw2", rank, "tto", "")
+    expand_planes(T.tw, ("tw0", "tw1"), zw)
+    expand_moves(zw, "")
     expand_points("h")
     first_list("h")
-    ms(T.ee[:], 0, w=["ee"])
-    ms(T.cc[:], 0, w=["cc"])
-    ts(T.i_q[:, 0:8], T.i_g[:], 4, None, ALU.arith_shift_right, r=["i_g"], w=["i_q"])
-    ts(T.pbb[:, 0:16], T.i_m[:], 15, None, ALU.bitwise_and, r=["i_m"], w=["pbb"])
-    ts(T.s4a[:], T.i_s[:], 0, 4, ALU.is_ge, ALU.mult, r=["i_s"], w=["s4a"])
-    ts(T.s4b[:], T.i_s[:], 3, None, ALU.is_le, r=["i_s"], w=["s4b"])
-    ts(T.rna[:], T.i_n[:], 4, 64, ALU.is_equal, ALU.mult, r=["i_n"], w=["rna"])
-    ts(T.rnb[:], T.i_n[:], 0, None, ALU.is_equal, r=["i_n"], w=["rnb"])
-    ts(T.gm[:], T.i_q[:], 0, None, ALU.is_equal, r=["i_q"], w=["gm"])
-    ts(T.ee[:, 112:128], T.pbb[:, 0:16], 0, None, ALU.is_equal, r=["pbb"], w=["ee"])
-    tt(T.s4[:], T.s4a[:], T.s4b[:], ALU.mult, r=["s4a", "s4b"], w=["s4"])
-    tt(T.rn[:], T.rna[:], T.rnb[:], ALU.add, r=["rna", "rnb"], w=["rn"])
-    for k, (c, val) in enumerate(((0, 0), (16, 16), (0, -16), (16, 0))):
-        ts(T.cc[:, k, :, c:c + 16], T.ic[:, :, c:c + 16], val, None, ALU.is_equal, r=["ic"], w=["+cc" if k else "cc"])
-    for s in "hf":
-        for e in range(2):
-            cp(T["tb" + s][:, e], T.z0[:, 0:256], r=["z0"], w=["tb%s%d" % (s, e)])
-    for c in (0, WN - 1):
-        cp(T.w1[:, c:c + 1], T.xb[:, 0:1], r=["xb"], w=["+w1_d"])
-        ms(T.w2[:, c:c + 1], 0, w=["+w2_d"])
     to_points("h")
+    moves(T.tn, "tn", mate, "ttm", "m")
+    expand_planes(T.tn, ("tn", "tn"), zh)
+    expand_moves(zh, "m")
     ld("s", "d9", T.llf[:, 0:23], T.lpn[96:128, :], r=["lpn"], w=["llf"])
     ld("s", "d6", T.ptf[0:24, :], T.lpn[0:96, :], r=["lpn"], w=["ptf"])
-    moves(T.tn, "tn", mate, T.ttm, "ttm")
-    expand_planes(T.tn, "tn", zh)
-    expand_moves(zh)
+    first_list("f")
+    expand_points("f")
+    to_points("f")
 
     halves = ["_d"] + ["_%d_%d" % (z, h) for z in range(2) for h in range(2)]
 
     def gather(s):
         off = T["off" + s][:, 0:24]
-        emit("v", lambda: V.tensor_tensor(T["pr" + s][:], T.w1[:, 0:WN].indirect(off), T["x" + s][:], ALU.mult),
-             ["w1" + k for k in halves] + ["off" + s, "x" + s, "x%sp" % s], ["pr" + s])
-        act(T["nb" + s][:], T.w2[:, 0:WN].indirect(off), ["w2" + k for k in halves] + ["off" + s], ["nb" + s])
-        for d, src, m in (("u", "pr", "s4"), ("n", "nb", "rn")):
+        add("v", lambda: V.tensor_tensor(T["pr" + s][:], T.w1[:, 0:WN].indirect(off), T["x" + s][:], ALU.mult),
+            ["w1" + k for k in halves] + ["off" + s, "x" + s, "x%sp" % s], ["pr" + s], cost=0.62)
+        act(T["nb" + s][:], T.w2[:, 0:WN].indirect(off), ["w2" + k for k in halves] + ["off" + s], ["nb" + s], cost=0.77)
+        for d, src, m, c in (("u", "pr", "s4", 0.26), ("n", "nb", "rn", None)):
             for r in range(3):
-                mm(T[d + s][:, :, r], T[src + s][:, 128 * r:128 * r + 128], T[m][:], True, True, r=[src + s, m], w=["+" + d + s])
+                mm(T[d + s][:, :, r], T[src + s][:, 128 * r:128 * r + 128], T[m][:], True, True, r=[src + s, m], w=["+" + d + s], cost=c)
 
     def choose(s):
         u, n = T["u" + s], T["n" + s]
@@ -284,8 +274,8 @@ def rank_program(g, core, T, topo):
         tt(mn[:], m1[:, 0:8, :], m1[:, 8:16, :], ALU.min, r=["m1" + s], w=["mm" + s])
         for f in range(4):
             tt(eq[:, 8 * f:8 * f + 8, :], u[:, 8 * f:8 * f + 8, 0:3], mn[:], ALU.is_equal, r=["u" + s, "mm" + s], w=["+eq" + s])
-        tt(pp[:], eq[:], n[:, :, 0:3], ALU.mult, r=["eq" + s, "n" + s], w=["pp" + s])
-        tt(sa[:], pp[:, 0:16, :], pp[:, 16:32, :], ALU.add, r=["pp" + s], w=["sa" + s])
+        tt(pp[:], eq[:], n[:, :, 0:3], ALU.mult, r=["eq" + s, "n" + s], w=["pp" + s], cost=0.1)
+        tt(sa[:], pp[:, 0:16, :], pp[:, 16:32, :], ALU.add, r=["pp" + s], w=["sa" + s], cost=0.1)
         tt(sb[:], sa[:, 0:8, :], sa[:, 8:16, :], ALU.add, r=["sa" + s], w=["sb" + s])
 
     def to_list(s, a, b, keys, last=False):
@@ -294,8 +284,8 @@ def rank_program(g, core, T, topo):
             k = "tb%s%d" % (s, e)
             tt(tb[:, e, :, e:e + 5:2], a, b, ALU.add, r=keys, w=[k])
             for par in range(2):
-                mm(l[:, 0:4, :], tb[:, e, 4 * par:4 * par + 4, :], T.cc[:, 2 * e + par], e + par == 0, e + par == 2, r=[k, "cc"], w=["+l" + s])
-        emit("v", lambda: V.transpose(tr[:], l[:, 0:4, :]), ["l" + s], ["tr" + s])
+                mm(l[:, 0:4, :], tb[:, e, 4 * par:4 * par + 4, :], T.cc[:, 2 * e + par], e + par == 0, e + par == 2, r=[k, "cc"], w=["+l" + s], cost=0.13)
+        add("v", lambda: V.transpose(tr[:], l[:, 0:4, :]), ["l" + s], ["tr" + s], cost=0.13)
         for r in range(3):
             src, c = tr[:, :, 2 * r:2 * r + 2], slice(8 * r, 8 * r + 8)
             if last:
@@ -310,14 +300,14 @@ def rank_program(g, core, T, topo):
         to_list(s, T["sb" + s][:], T["st" + s][:], ["sb" + s, "st" + s])
         tt(T["va" + s][:], T["sb" + s][:], T["st" + s][:], ALU.add, r=["sb" + s, "st" + s], w=["va" + s])
 
-    def step2_end(s, wo, name):
+    def step2_end(s, wo, name, landing):
         choose(s)
         vb, fl, w = T["vb" + s], T["fl" + s], T[wo + s]
         tt(vb[:], T["sb" + s][:], T["va" + s][:], ALU.add, r=["sb" + s, "va" + s], w=["vb" + s])
         ts(fl[:], vb[:], 3000, -FLAG, ALU.is_ge, ALU.mult, r=["vb" + s], w=["fl" + s])
         tt(w[:], vb[:], fl[:], ALU.add, r=["vb" + s, "fl" + s], w=[wo + s])
         if name:
-            send(name, part, T["in" + name.lower()][:], w[:], wo + s, off_)
+            send(name, part, T[landing][:], w[:], [wo + s], landing, off_)
         tt(T["df" + s][:], w[:], T["st" + s][:], ALU.subtract, r=[wo + s, "st" + s], w=["df" + s])
 
     def merge(s, inn, last=False):
@@ -325,27 +315,76 @@ def rank_program(g, core, T, topo):
         if not last:
             tt(T["st" + s][:], T["df" + s][:], T[inn][:], ALU.add, r=["df" + s, inn], w=["st" + s])
 
-    gather("h")
-    step1_end("h")
-    gather("h")
-    first_list("f")
-    expand_points("f")
-    to_points("f")
-    gather("f")
-    step2_end("h", "wo", "A")
-    step1_end("f")
-    gather("f")
-    step2_end("f", "wo", "B")
-    merge("f", "ina")
-    gather("f")
-    step1_end("f")
-    gather("f")
-    merge("h", "inb")
-    gather("h")
-    step2_end("f", "we", "C")
-    step1_end("h")
-    gather("h")
-    step2_end("h", "we", None)
+    for s, name in (("h", "A"), ("f", "B")):
+        gather(s)
+        step1_end(s)
+        gather(s)
+        step2_end(s, "wo", name, "in" + name.lower())
+    for s, name, inn in (("f", "C", "ina"), ("h", None, "inb")):
+        merge(s, inn)
+        gather(s)
+        step1_end(s)
+        gather(s)
+        step2_end(s, "we", name, "inc")
     merge("h", "inc", last=True)
     ld("s", "d7", T.y[:, :], T.yo[:, 0:23], r=["yo"])
-    need("g", [(k, c) for k, c in cnt.items()])
+
+    N = len(ops)
+    succ = [[] for _ in ops]
+    for n, o in enumerate(ops):
+        for d in o["hard"] | o["soft"]:
+            succ[d].append(n)
+
+    def lat(o):
+        return o["cost"] + (DMA_T if o["dma"] else 0.0) + (SEND_T[o["send"][0]] if o["send"] else 0.0)
+
+    tail = [0.0] * N
+    for n in range(N - 1, -1, -1):
+        tail[n] = lat(ops[n]) + max([tail[m] + WAKE for m in succ[n]], default=0.0)
+    left = [len(o["hard"] | o["soft"]) for o in ops]
+    at, free, order = [0.0] * N, {q: 0.0 for q in Q}, []
+    ready = {n for n in range(N) if not left[n]}
+    while ready:
+        start = {n: max(at[n], free.get(ops[n]["q"], 0.0)) for n in ready}
+        t0 = min(start.values())
+        q0 = ops[min((n for n in ready), key=lambda n: (start[n], n))]["q"]
+        n = max((n for n in ready if ops[n]["q"] == q0 and start[n] <= t0 + 0.03), key=lambda n: (tail[n], -n))
+        ready.discard(n)
+        order.append(n)
+        if q0:
+            free[q0] = start[n] + ops[n]["cost"]
+        for m in succ[n]:
+            at[m] = max(at[m], start[n] + (lat(ops[n]) + WAKE if n in ops[m]["hard"] else 0.0))
+            left[m] -= 1
+            if not left[m]:
+                ready.add(m)
+
+    cnt, known, snap, tok = {}, {q: {} for q in Q}, {}, {}
+
+    def need(q, toks):
+        kn = known[q]
+        for sem, c in sorted(toks, key=lambda t: -t[1]):
+            if kn.get(sem, 0) < c:
+                Q[q].wait_ge(T.sem[sem], c)
+                kn[sem] = c
+                for s2, c2 in snap.get((sem, c), {}).items():
+                    kn[s2] = max(kn.get(s2, 0), c2)
+
+    for n in order:
+        o = ops[n]
+        if o["arr"]:
+            tok[n] = ("arr" + o["arr"][0], o["arr"][1])
+            cnt[tok[n][0]] = tok[n][1]
+            continue
+        need(o["q"], {tok[d] for d in o["hard"]})
+        ins = o["fn"]()
+        if o["send"]:
+            tok[n] = ("loc" + o["send"][0], o["send"][1])
+            cnt[tok[n][0]] = tok[n][1]
+        else:
+            sem, inc = (o["dma"], 16) if o["dma"] else (CS[o["q"]], 1)
+            ins.then_inc(T.sem[sem], inc)
+            cnt[sem] = cnt.get(sem, 0) + inc
+            tok[n] = (sem, cnt[sem])
+        snap[tok[n]] = dict(known[o["q"]])
+    need("g", list(cnt.items()))

@@ -5,29 +5,29 @@ WN = 2050
 FLAG = 8192
 SCRATCH = {}
 for _d, _s, _n in (
-        (I32, [128, 8, 16], "ixp"), (I32, [128, 16, 16], "ixd ixq"), (I32, [128, 4, 32], "ic"), (I32, [128, 32], "i_s i_n"),
+        (I32, [128, 8, 16], "ixp"), (I32, [128, 16, 16], "ixd ixq"), (I32, [128, 8, 32], "ic"), (I32, [128, 8, 5], "i_s i_n"),
         (I32, [128, 8, 4, 4], "i_e"), (I32, [128, 8], "i_p i_g i_q i_r i_h"), (I32, [128, 16], "i_m i_l"),
-        (I32, [128, 64], "i_t pb32 pbb dt dn dsh dd2 dhi dlo dnm dshm dd2m dhim dlom"), (I32, [128, 128], "pl32 plb"), (I32, [128, 23], "tl32"),
-        (I32, [128, 92], "pf32"), (I32, [128, 368], "pr32"), (B16, [128, 8, 16], "izp"), (B16, [128, 16, 16], "izd izq"),
-        (B16, [128, 8, 8, 16], "yp"), (B16, [128, 16, 8, 16], "yd qq"), (B16, [128, 4, 4, 32], "cc"), (B16, [128, 512], "z0"),
-        (B16, [128, 32], "rn"), (B16, [128, 8, 4, 4], "e24"), (B16, [128, 240], "ee"), (B16, [128, 2064], "w2"),
-        (F32, [128, 2056], "w1"), (F32, [128, 32], "s4 s4a s4b rna rnb"), (F32, [128, 8], "gm xb wb wc"),
-        (F32, [128, 64], "tto ttm dfl ddd dflm dddm"), (F32, [128, 24], "yo"), (F16, [128, 192], "tw tn"), (F16, [128, 92], "lp lpn"),
-        (F16, [128, 24], "llh llf"), (F16, [128, 64], "ex exm"), (F16, [128, 8, 3], "ina inb inc woh wof weh wef"),
-        (F16, [128, 368], "pth ptf"), (F16, [128, 8, 24], "rmh rmf"), (F16, [128, 2, 8, 32], "tbh tbf"),
+        (I32, [128, 64], "pb32 pbb dn dsh dhi dlo dnm dshm dhim dlom"), (I32, [128, 128], "pl32 plb ixi"), (I32, [128, 23], "tl32"),
+        (I32, [128, 92], "pf32"), (I32, [128, 16, 23], "pr32"), (B16, [128, 8, 16], "izp"), (B16, [128, 16, 16], "izd izq"),
+        (B16, [128, 8, 8, 16], "yp"), (B16, [128, 16, 8, 16], "yd qq"), (B16, [128, 2, 8, 32], "cc"), (B16, [128, 8, 32], "z0"),
+        (B16, [128, 8, 5], "rn"), (B16, [128, 8, 4, 4], "e24"), (B16, [128, 240], "ee"), (B16, [128, 2064], "w2"),
+        (F32, [128, 2056], "w1"), (F32, [128, 8, 5], "s4 s4a s4b rna rnb"), (F32, [128, 8], "gm xb wb wc"), (F32, [128, 128], "id"),
+        (F32, [128, 64], "dfl dflm"), (F32, [128, 24], "yo"), (F16, [128, 192], "tw tn"), (F16, [128, 92], "lp lpn"),
+        (F16, [128, 24], "llh llf ina inb inc woh wof weh wef"), (F16, [128, 64], "ex exm"),
+        (F16, [128, 16, 23], "pth ptf"), (F16, [128, 24, 8], "rmh rmf"), (F16, [128, 8, 32], "tbh tbf"),
         (F32, [128, 384], "xh xf prh prf"), (B16, [128, 384], "nbh nbf"), (U16, [128, 24], "offh offf"),
-        (F32, [128, 16, 3], "aah aaf m1h m1f sah saf"), (F32, [128, 8, 3], "mmh mmf sbh sbf sth stf vah vaf vbh vbf flh flf dfh dff"),
-        (F32, [128, 32, 3], "eqh eqf pph ppf"), (F32, [128, 4, 32], "trh trf")):
+        (F32, [128, 120], "rs zsh zsf mnh mnf eqh eqf neh nef pph ppf soh sof"), (F32, [128, 24], "sth stf flh flf dfh dff"),
+        (F32, [128, 8, 32], "trh trf")):
     for _k in _n.split():
         SCRATCH[_k] = ("sbuf", _s, _d)
-for _s, _n in (([128, 512], "stg0 stg1"), ([128, 32, 16], "uh uf nh nf"), ([128, 16, 32], "lh lf")):
+for _s, _n in (([128, 512], "uh uf nh nf stg0 stg1"), ([128, 16, 32], "lh lf")):
     for _k in _n.split():
         SCRATCH[_k] = ("psum", _s, F32)
 SEMAPHORES = ["sv", "sa", "sp", "sg"] + ["d%d" % k for k in range(10)] + [a + b for a in ("arr", "loc") for b in "TLABC"]
 CS = {"v": "sv", "a": "sa", "p": "sp", "g": "sg"}
 WAKE = 0.12
 SHORT = {"v": 0.07, "a": 0.3, "p": 0.065, "g": 0.4, "s": 0.06}
-DMA_T, SEND_T = 2.2, {"T": 6.0, "L": 4.0, "A": 3.0, "B": 3.0, "C": 3.0}
+DMA_T, SEND_T = 2.2, {"T": 3.5, "L": 5.5, "A": 2.2, "B": 2.2, "C": 2.2}
 
 
 def rank_program(g, core, T, topo):
@@ -55,7 +55,7 @@ def rank_program(g, core, T, topo):
                     base[k0], app[k0] = list(rd[k0]), []
                     rd[k0] = []
                 hard |= set(base.get(k0, []))
-                if q == "p":
+                if q in "pg":
                     soft |= set(app.get(k0, [])[-1:])
                 app.setdefault(k0, []).append(n)
             else:
@@ -70,6 +70,9 @@ def rank_program(g, core, T, topo):
 
     def tt(out, a, b, op, r=(), w=(), cost=None):
         add("v", lambda: V.tensor_tensor(out, a, b, op), r, w, cost)
+
+    def scan(out, a, b, o0, o1, r=(), w=()):
+        add("v", lambda: V.tensor_tensor_scan(out, a, b, 0.0, o0, o1), r, w, 0.12)
 
     def cp(out, i, r=(), w=(), cost=None):
         add("v", lambda: V.tensor_copy(out, i), r, w, cost)
@@ -92,7 +95,7 @@ def rank_program(g, core, T, topo):
     def send(name, dst_rank, out, src, keys, landing, engines):
         rid, pid, _ = topo.addr(T.cores[dst_rank])
         add("g", lambda: g.remote_dma(out, src, T.sem["arr" + name], T.sem["loc" + name], pid, rid, sum(1 << e for e in engines)),
-            keys, cost=0.6, send=(name, len(engines)))
+            keys, w=["+order"] if name in "LT" else (), cost=0.6, send=(name, len(engines)))
         ops.append(dict(q=None, fn=None, hard={len(ops) - 1}, soft=set(), cost=0.0, dma=None, send=None, arr=(name, len(engines))))
         base[landing] = [len(ops) - 1]
 
@@ -101,57 +104,59 @@ def rank_program(g, core, T, topo):
 
     ld("s", "d0", T.pl32[:], T.planes[:, :], w=["pl32"])
     ld("a", "d1", T.pb32[0:64, :], T.planes[3::4, :], w=["pb32d"])
+    ld("s", "d4", T.pf32[0:96, :], T.pts[:, :], w=["pf32p"])
+    ld("a", "d8", T.pf32[96:128, :], T.tet0[:, :], w=["pf32t"])
     ld("s", "d2", T.pb32[64:128, :], T.nbr[:, :], w=["pb32n"])
     ld("a", "d3", T.tl32[:], T.tet0[:, :], w=["tl32"])
-    ld("s", "d4", T.pf32[0:96, :], T.pts[:, :], w=["pf32p"])
-    ld("s", "d8", T.pf32[96:128, :], T.tet0[:, :], w=["pf32t"])
-    ld("s", "d5", T.pr32[0:24, :], T.pts[:, :], w=["pr32"])
-    ts(T.plb[:], T.pl32[:], 1024, None, ALU.add, r=["pl32"], w=["plb"])
+    ld("s", "d5", T.pr32[0:24], T.pts[:, :], w=["pr32"])
+    cp(T.lp[0:96, :], T.pf32[0:96, :], r=["pf32p"], w=["lp0"], cost=0.1)
+    ts(T.lp[96:128, :], T.pf32[96:128, :], -2047, None, ALU.add, r=["pf32t"], w=["lp1"], cost=0.1)
+    send("L", part, T.lpn[:], T.lp[:], ["lp0", "lp1"], "lpn", off_)
+    ts(T.plb[:], T.pl32[:], 1024, None, ALU.add, r=["pl32"], w=["plb"], cost=0.13)
     ts(T.pbb[0:64, :], T.pb32[0:64, :], 1024, None, ALU.add, r=["pb32d"], w=["pbb"])
-    ts(T.pl32[:], T.plb[:], 2047, None, ALU.bitwise_and, r=["plb"], w=["pl32"])
+    ts(T.pl32[:], T.plb[:], 2047, None, ALU.bitwise_and, r=["plb"], w=["pl32"], cost=0.13)
     ts(T.pb32[0:64, :], T.pbb[0:64, :], 11, None, ALU.arith_shift_right, r=["pbb"], w=["pb32d"])
     ts(T.tw[64:128, 128:192], T.pb32[64:128, :], -2047, None, ALU.add, r=["pb32n"], w=["tw2"])
-    ts(T.tw[:, 0:128], T.pl32[:], -1024, None, ALU.add, r=["pl32"], w=["tw0"])
+    ts(T.tw[:, 0:128], T.pl32[:], -1024, None, ALU.add, r=["pl32"], w=["tw0"], cost=0.13)
     cp(T.tw[0:64, 128:192], T.pb32[0:64, :], r=["pb32d"], w=["tw1"])
     send("T", mate, T.tn[:], T.tw[:], ["tw0", "tw1", "tw2"], "tn", on)
-    cp(T.lp[0:96, :], T.pf32[0:96, :], r=["pf32p"], w=["lp0"])
-    ts(T.lp[96:128, :], T.pf32[96:128, :], -2047, None, ALU.add, r=["pf32t"], w=["lp1"])
-    send("L", part, T.lpn[:], T.lp[:], ["lp0", "lp1"], "lpn", off_)
     ts(T.llh[:, 0:23], T.tl32[:], -2047, None, ALU.add, r=["tl32"], w=["llh"])
     io("ixp", [[1, 8], [8, 16]], 0, -1)
     io("ixq", [[1, 16], [16, 4], [500, 4]], -1500, -1)
     io("i_p", [[0, 8]], 0, 1)
     io("ixd", [[1, 16], [16, 16]], 0, -1)
-    io("i_t", [[1, 64]], 0, 64)
     io("i_e", [[3, 8], [0, 4], [1, 4]], 0, -1)
     io("i_m", [[-1, 16]], 256, 1)
     io("i_g", [[-16, 2], [-32, 4]], 0, 1)
-    io("i_s", [[-4, 4], [-16, 2], [-32, 4]], 0, 1)
-    io("i_n", [[-1, 4], [-16, 2], [-32, 4]], 0, 1)
-    io("ic", [[32, 4], [1, 32]], 0, -1)
+    io("i_s", [[-16, 2], [-32, 4], [-4, 5]], 4, 1)
+    io("i_n", [[-16, 2], [-32, 4], [-1, 5]], 1, 1)
+    io("ic", [[16, 8], [1, 32]], 0, -1)
+    io("ixi", [[1, 128]], 0, -1)
     ts(T.izp[:], T.ixp[:], 0, None, ALU.is_equal, r=["ixp"], w=["izp"], cost=0.13)
     ts(T.izq[:], T.ixq[:], 0, 2048, ALU.is_equal, ALU.mult, r=["ixq"], w=["izq"], cost=0.26)
     ts(T.izd[:], T.ixd[:], 0, None, ALU.is_equal, r=["ixd"], w=["izd"], cost=0.26)
     for k in range(8):
         cp(T.yp[:, :, k, :], T.izp[:], r=["izp"], w=["+yp"])
-        act(T.qq[0:64, :, k, :], T.izq[0:64], r=["izq"], w=["+qq"], cost=0.45)
-        cp(T.yd[:, :, k, :], T.izd[:], r=["izd"], w=["+yd"], cost=0.13)
+        for out, i, key, w in ((T.qq[0:64, :, k, :], T.izq[0:64], "izq", "+qq"), (T.yd[:, :, k, :], T.izd[:], "izd", "+yd")):
+            if k % 2:
+                act(out, i, r=[key], w=[w], cost=0.45)
+            else:
+                cp(out, i, r=[key], w=[w], cost=0.13)
     ts(T.i_q[:], T.i_p[:], 3, None, ALU.bitwise_and, r=["i_p"], w=["i_q"])
     ts(T.i_r[:], T.i_p[:], 15, 2, ALU.bitwise_and, ALU.arith_shift_right, r=["i_p"], w=["i_r"])
     ts(T.xb[:], T.i_q[:], 3, None, ALU.is_equal, r=["i_q"], w=["xb"])
-    ts(T.wc[:], T.i_r[:], 0.25, None, ALU.mult, r=["i_r"], w=["wc"])
+    ts(T.wc[:], T.i_r[:], 1, 0.25, ALU.add, ALU.mult, r=["i_r"], w=["wc"])
     tt(T.wb[:], T.wc[:], T.xb[:], ALU.mult, r=["wc", "xb"], w=["wb"])
-    ts(T.dt[:], T.i_t[:], 1023, None, ALU.bitwise_and, r=["i_t"], w=["dt"])
-    ts(T.tto[64:128, :], T.dt[64:128, :], 1024 * rank - 2047, None, ALU.add, r=["dt"], w=["tto"])
-    ts(T.ttm[64:128, :], T.dt[64:128, :], 1024 * mate - 2047, None, ALU.add, r=["dt"], w=["ttm"])
-    ms(T.z0[:], 0, w=["z0"], cost=0.26)
+    ms(T.z0[:], 0, w=["z0"], cost=0.13)
     ts(T.e24[0:32], T.i_e[0:32], 0, None, ALU.is_equal, r=["i_e"], w=["e24"], cost=0.13)
     ms(T.e24[0:32, :, :, 3], 0, w=["e24"])
-    cp(T.pth[0:24, :], T.pr32[0:24, :], r=["pr32"], w=["pth"], cost=0.37)
+    cp(T.pth[0:24], T.pr32[0:24], r=["pr32"], w=["pth"], cost=0.37)
     ms(T.xh[:, 368:384], 0, w=["xhp"])
     ms(T.xf[:, 368:384], 0, w=["xfp"])
     ms(T.ee[:], 0, w=["ee"], cost=0.12)
     ms(T.cc[:], 0, w=["cc"], cost=0.26)
+    ms(T.rs[:], -1e9, w=["rs"], cost=0.12)
+    ms(T.rs[:, 0:120:5], 0, w=["rs"])
     ts(T.i_h[:], T.i_g[:], 4, None, ALU.arith_shift_right, r=["i_g"], w=["i_h"])
     ts(T.i_l[:], T.i_m[:], 15, None, ALU.bitwise_and, r=["i_m"], w=["i_l"])
     ts(T.s4a[:], T.i_s[:], 0, 4, ALU.is_ge, ALU.mult, r=["i_s"], w=["s4a"])
@@ -160,24 +165,27 @@ def rank_program(g, core, T, topo):
     ts(T.rnb[:], T.i_n[:], 0, None, ALU.is_equal, r=["i_n"], w=["rnb"])
     ts(T.gm[:], T.i_h[:], 0, None, ALU.is_equal, r=["i_h"], w=["gm"])
     ts(T.ee[:, 112:128], T.i_l[:], 0, None, ALU.is_equal, r=["i_l"], w=["ee"])
+    ts(T.id[:], T.ixi[:], 0, None, ALU.is_equal, r=["ixi"], w=["id"], cost=0.13)
     tt(T.s4[:], T.s4a[:], T.s4b[:], ALU.mult, r=["s4a", "s4b"], w=["s4"])
+    ms(T.s4[:, :, 0], 0, w=["s4"])
     tt(T.rn[:], T.rna[:], T.rnb[:], ALU.add, r=["rna", "rnb"], w=["rn"])
-    for k, (c, val) in enumerate(((0, 0), (16, 16), (0, -16), (16, 0))):
-        ts(T.cc[:, k, :, c:c + 16], T.ic[:, :, c:c + 16], val, None, ALU.is_equal, r=["ic"], w=["+cc"])
+    ms(T.rn[:, :, 0], 0, w=["rn"])
+    for k in range(2):
+        ts(T.cc[:, k, :, 16 * k:16 * k + 16], T.ic[:, :, 16 * k:16 * k + 16], 16 * k, None, ALU.is_equal, r=["ic"], w=["+cc"], cost=0.13)
     for s in "hf":
-        for e in range(2):
-            cp(T["tb" + s][:, e], T.z0[:, 0:256], r=["z0"], w=["tb%s%d" % (s, e)], cost=0.13)
+        ms(T["zs" + s][:], 0, w=["zs" + s], cost=0.12)
+        cp(T["tb" + s][:], T.z0[:], r=["z0"], w=["tb" + s], cost=0.13)
     for c in (0, WN - 1):
         cp(T.w1[:, c:c + 1], T.xb[:, 0:1], r=["xb"], w=["+w1_d"])
         ms(T.w2[:, c:c + 1], 0, w=["+w2_d"])
 
     def first_list(s):
-        off, v = T["off" + s], T["ll" + s][:, 0:23]
-        ms(off[:, 23:24], 0, w=["+off" + s])
+        off, v, ks = T["off" + s], T["ll" + s][:, 0:23], ["+off%s%d" % (s, r) for r in range(3)]
+        ms(off[:, 23:24], 0, w=ks[2:])
         if low == 0:
-            ts(off[:, 0:23], v, 1, 2048, ALU.min, ALU.add, r=["ll" + s], w=["+off" + s])
+            ts(off[:, 0:23], v, 1, 2048, ALU.min, ALU.add, r=["ll" + s], w=ks)
         else:
-            ts(off[:, 0:23], v, 0, None, ALU.max, r=["ll" + s], w=["+off" + s])
+            ts(off[:, 0:23], v, 0, None, ALU.max, r=["ll" + s], w=ks)
 
     nb_ = [0, 0]
 
@@ -199,23 +207,21 @@ def rank_program(g, core, T, topo):
             b = bank()
             for tb in range(8 * h, 8 * h + 8):
                 o, lh, rh = T[b][:, 64 * (tb % 8):64 * (tb % 8) + 64], T.yp[:, tb // 2], src[:, 64 * (tb % 2):64 * (tb % 2) + 64]
-                mm(o, lh, rh, True, False, r=["yp", keys[0]], w=["+" + b])
-                mm(o, T.qq[0:64, tb], src[0:64, 128:192], False, True, r=["qq", keys[1]], w=["+" + b])
+                mm(o, lh, rh, True, False, r=["yp", keys[0]], w=["+" + b, "+half%d" % z])
+                mm(o, T.qq[0:64, tb], src[0:64, 128:192], False, True, r=["qq", keys[1]], w=["+" + b, "+half%d" % z])
             c0 = 1 + 1024 * z + 512 * h
             copy_out(T.w1[:, c0:c0 + 512], T[b][:], T.wb[:, 0:1], [b, "wb"], ["w1_%d_%d" % (z, h)])
 
-    def moves(src, key, q, tcol, m):
+    def moves(src, key, q, m):
         n, P = src[64:128, 128:192], slice(64, 128)
-        dn, dd, sh, fl, d2, hi, lo, ex = (T[k + m] for k in ("dn", "ddd", "dsh", "dfl", "dd2", "dhi", "dlo", "ex"))
-        ts(dn[P, :], n, 2047, None, ALU.add, r=[key], w=["dn" + m])
-        tt(dd[P, :], n, T[tcol][P, :], ALU.subtract, r=[key, tcol], w=["dd" + m], cost=0.13)
+        dn, sh, fl, hi, lo, ex = (T[k + m] for k in ("dn", "dsh", "dfl", "dhi", "dlo", "ex"))
+        ts(dn[P, :], n, -1, None, ALU.add, r=[key], w=["dn" + m])
         ts(sh[P, :], dn[P, :], 10, None, ALU.arith_shift_right, r=["dn" + m], w=["sh" + m])
-        ts(fl[P, :], sh[P, :], q, FLAG, ALU.not_equal, ALU.mult, r=["sh" + m], w=["fl" + m + "_"])
-        tt(d2[P, :], dd[P, :], fl[P, :], ALU.add, r=["dd" + m, "fl" + m + "_"], w=["d2" + m], cost=0.13)
-        ts(hi[P, :], d2[P, :], 6, None, ALU.arith_shift_right, r=["d2" + m], w=["hi" + m])
-        ts(lo[P, :], d2[P, :], 63, None, ALU.bitwise_and, r=["d2" + m], w=["lo" + m])
-        cp(ex[P, :], hi[P, :], r=["hi" + m], w=["+ex" + m])
-        cp(ex[0:64, :], lo[P, :], r=["lo" + m], w=["+ex" + m])
+        ts(fl[P, :], sh[P, :], q - 2, FLAG // 64, ALU.not_equal, ALU.mult, r=["sh" + m], w=["fl_" + m])
+        ts(hi[P, :], dn[P, :], 6, None, ALU.arith_shift_right, r=["dn" + m], w=["hi" + m])
+        ts(lo[P, :], dn[P, :], 63, None, ALU.bitwise_and, r=["dn" + m], w=["lo" + m])
+        tt(ex[P, :], hi[P, :], fl[P, :], ALU.add, r=["hi" + m, "fl_" + m], w=["+ex" + m], cost=0.13)
+        ts(ex[0:64, :], lo[P, :], 1, None, ALU.add, r=["lo" + m], w=["+ex" + m])
 
     def expand_moves(z, m):
         for h in range(2):
@@ -226,106 +232,105 @@ def rank_program(g, core, T, topo):
             copy_out(T.w2[:, c0:c0 + 512], T[b][:], None, [b], ["w2_%d_%d" % (z, h)])
 
     def expand_points(s):
-        b, x = bank(), T["x" + s]
-        mm(T[b][:, 0:368], T.e24[0:24], T["pt" + s][0:24, :], True, True, r=["e24", "pt" + s], w=["+" + b], cost=0.37)
-        act(x[:, 0:368], T[b][:, 0:368], [b, "xb"], ["x" + s], bias=T.xb[:, 0:1], cost=0.57)
+        b, x = T["l" + s][:, :, 0:23], T["x" + s]
+        mm(b, T.e24[0:24], T["pt" + s][0:24], True, True, r=["e24", "pt" + s], w=["+l" + s], cost=0.37)
+        ts(x[:, 0:368], b, T.xb[:, 0:1], None, ALU.add, r=["l" + s, "xb"], w=["x" + s], cost=0.37)
 
     def to_points(s):
         rm, l = T["rm" + s], T["l" + s]
-        cp(rm[:, :, 23:24], T.z0[:, 0:8], r=["z0"], w=["+rm" + s])
+        cp(rm[:, 23, :], T.z0[:, 0, 0:8], r=["z0"], w=["+rm" + s])
         for k in range(8):
-            ts(rm[:, k, 0:23], T["ll" + s][:, 0:23], T.gm[:, k:k + 1], None, ALU.mult, r=["gm", "ll" + s], w=["+rm" + s])
+            ts(rm[:, 0:23, k], T["ll" + s][:, 0:23], T.gm[:, k:k + 1], None, ALU.mult, r=["gm", "ll" + s], w=["+rm" + s])
         for b in range(8):
-            mm(l[:, 0, 0:24], T.ee[:, 112 - 16 * b:240 - 16 * b], rm[:, :, b::8], b == 0, b == 7, r=["ee", "rm" + s], w=["+l" + s])
-        cp(T["st" + s][:], l[:, 0, 0:24], r=["l" + s], w=["st" + s])
+            mm(l[:, 0:3, 0:8], T.ee[:, 112 - 16 * b:240 - 16 * b], rm[:, b::8, :], b == 0, b == 7, r=["ee", "rm" + s], w=["+l" + s])
+        cp(T["st" + s][:], l[:, 0:3, 0:8], r=["l" + s], w=["st" + s])
 
     zw, zh = (0, 1) if rank == low else (1, 0)
-    moves(T.tw, "tw2", rank, "tto", "")
+    moves(T.tw, "tw2", rank, "")
     expand_planes(T.tw, ("tw0", "tw1"), zw)
     expand_moves(zw, "")
     expand_points("h")
     first_list("h")
     to_points("h")
-    moves(T.tn, "tn", mate, "ttm", "m")
+    moves(T.tn, "tn", mate, "m")
     expand_planes(T.tn, ("tn", "tn"), zh)
     expand_moves(zh, "m")
     ld("s", "d9", T.llf[:, 0:23], T.lpn[96:128, :], r=["lpn"], w=["llf"])
-    ld("s", "d6", T.ptf[0:24, :], T.lpn[0:96, :], r=["lpn"], w=["ptf"])
+    ld("s", "d6", T.ptf[0:24], T.lpn[0:96, :], r=["lpn"], w=["ptf"])
     first_list("f")
     expand_points("f")
     to_points("f")
 
     halves = ["_d"] + ["_%d_%d" % (z, h) for z in range(2) for h in range(2)]
 
-    def gather(s):
-        off = T["off" + s][:, 0:24]
-        add("v", lambda: V.tensor_tensor(T["pr" + s][:], T.w1[:, 0:WN].indirect(off), T["x" + s][:], ALU.mult),
-            ["w1" + k for k in halves] + ["off" + s, "x" + s, "x%sp" % s], ["pr" + s], cost=0.62)
-        act(T["nb" + s][:], T.w2[:, 0:WN].indirect(off), ["w2" + k for k in halves] + ["off" + s], ["nb" + s], cost=0.77)
-        for d, src, m, c in (("u", "pr", "s4", 0.26), ("n", "nb", "rn", None)):
-            for r in range(3):
-                mm(T[d + s][:, :, r], T[src + s][:, 128 * r:128 * r + 128], T[m][:], True, True, r=[src + s, m], w=["+" + d + s], cost=c)
+    def gather(s, state, key):
+        off, ks = T["off" + s], ["off%s%d" % (s, r) for r in range(3)]
+
+        def third(r):
+            c = slice(128 * r, 128 * r + 128)
+            add("v", lambda: V.tensor_tensor(T["pr" + s][:, c], T.w1[:, 0:WN].indirect(off[:, 8 * r:8 * r + 8]), T["x" + s][:, c], ALU.mult),
+                ["w1" + k for k in halves] + [ks[r], "x" + s, "x%sp" % s], ["pr%s%d" % (s, r)], cost=0.25)
+            mm(T["u" + s][:, 40 * r:40 * r + 40], T["pr" + s][:, c], T.s4[:], True, True, r=["pr%s%d" % (s, r), "s4"], w=["+u" + s], cost=0.26)
+
+        cp(T["zs" + s][:, 0:120:5], state, r=[key], w=["zs" + s])
+        mm(T["n" + s][:, 0:120], T.id[:], T["zs" + s][:], True, False, r=["id", "zs" + s], w=["+n" + s], cost=0.48)
+        for r in range(3):
+            third(r)
+        act(T["nb" + s][:], T.w2[:, 0:WN].indirect(off[:, 0:24]), ["w2" + k for k in halves] + ks, ["nb" + s], cost=0.77)
+        for r in range(3):
+            mm(T["n" + s][:, 40 * r:40 * r + 40], T["nb" + s][:, 128 * r:128 * r + 128], T.rn[:], False, r == 2, r=["nb" + s, "rn"], w=["+n" + s])
 
     def choose(s):
-        u, n = T["u" + s], T["n" + s]
-        aa, m1, mn, eq, pp, sa, sb = (T[k + s] for k in ("aa", "m1", "mm", "eq", "pp", "sa", "sb"))
-        ts(aa[:], u[:, 0:16, 0:3], -0.5, None, ALU.min, r=["u" + s], w=["aa" + s])
-        tt(m1[:], aa[:], u[:, 16:32, 0:3], ALU.min, r=["aa" + s, "u" + s], w=["m1" + s])
-        tt(mn[:], m1[:, 0:8, :], m1[:, 8:16, :], ALU.min, r=["m1" + s], w=["mm" + s])
-        for f in range(4):
-            tt(eq[:, 8 * f:8 * f + 8, :], u[:, 8 * f:8 * f + 8, 0:3], mn[:], ALU.is_equal, r=["u" + s, "mm" + s], w=["+eq" + s])
-        tt(pp[:], eq[:], n[:, :, 0:3], ALU.mult, r=["eq" + s, "n" + s], w=["pp" + s], cost=0.1)
-        tt(sa[:], pp[:, 0:16, :], pp[:, 16:32, :], ALU.add, r=["pp" + s], w=["sa" + s], cost=0.1)
-        tt(sb[:], sa[:, 0:8, :], sa[:, 8:16, :], ALU.add, r=["sa" + s], w=["sb" + s])
+        u, n = T["u" + s][:, 0:120], T["n" + s][:, 0:120]
+        mn, eq, ne, pp, so = (T[k + s][:] for k in ("mn", "eq", "ne", "pp", "so"))
+        scan(mn, T.rs[:], u, ALU.max, ALU.min, r=["rs", "u" + s], w=["mn" + s])
+        tt(eq, u, mn, ALU.is_equal, r=["u" + s, "mn" + s], w=["eq" + s], cost=0.12)
+        tt(pp, eq, n, ALU.mult, r=["eq" + s, "n" + s], w=["pp" + s], cost=0.12)
+        tt(ne, u, mn, ALU.not_equal, r=["u" + s, "mn" + s], w=["ne" + s], cost=0.12)
+        scan(so, ne, pp, ALU.mult, ALU.add, r=["ne" + s, "pp" + s], w=["so" + s])
 
-    def to_list(s, a, b, keys, last=False):
+    def to_list(s, put, last=False):
         tb, l, tr = T["tb" + s], T["l" + s], T["tr" + s]
-        for e in range(2):
-            k = "tb%s%d" % (s, e)
-            tt(tb[:, e, :, e:e + 5:2], a, b, ALU.add, r=keys, w=[k])
-            for par in range(2):
-                mm(l[:, 0:4, :], tb[:, e, 4 * par:4 * par + 4, :], T.cc[:, 2 * e + par], e + par == 0, e + par == 2, r=[k, "cc"], w=["+l" + s], cost=0.13)
-        add("v", lambda: V.transpose(tr[:], l[:, 0:4, :]), ["l" + s], ["tr" + s], cost=0.13)
         for r in range(3):
-            src, c = tr[:, :, 2 * r:2 * r + 2], slice(8 * r, 8 * r + 8)
+            put(tb[:, :, r], r, "+tb" + s)
+        for par in range(2):
+            mm(l[:, 0:8, :], tb[:, 4 * par:4 * par + 4, :], T.cc[:, par], par == 0, par == 1, r=["tb" + s, "cc"], w=["+l" + s], cost=0.26)
+        add("v", lambda: V.transpose(tr[:], l[:, 0:8, :]), ["l" + s], ["tr" + s], cost=0.26)
+        for r in range(3):
+            src, c, k = tr[:, :, r], slice(8 * r, 8 * r + 8), ["off%s%d" % (s, r)]
             if last:
                 ts(T.yo[:, c], src, 2047, None, ALU.add, r=["tr" + s], w=["+yo"])
             elif low == 0:
-                ts(T["off" + s][:, c], src, 1, 2048, ALU.min, ALU.add, r=["tr" + s], w=["+off" + s])
+                ts(T["off" + s][:, c], src, 1, 2048, ALU.min, ALU.add, r=["tr" + s], w=k)
             else:
-                ts(T["off" + s][:, c], src, 2049, 0, ALU.min, ALU.max, r=["tr" + s], w=["+off" + s])
+                ts(T["off" + s][:, c], src, 2049, 0, ALU.min, ALU.max, r=["tr" + s], w=k)
 
-    def step1_end(s):
+    def rounds(s, wo, name, landing):
+        so, st, fl, w = T["so" + s], T["st" + s], T["fl" + s], T[wo + s]
+        gather(s, st[:], "st" + s)
         choose(s)
-        to_list(s, T["sb" + s][:], T["st" + s][:], ["sb" + s, "st" + s])
-        tt(T["va" + s][:], T["sb" + s][:], T["st" + s][:], ALU.add, r=["sb" + s, "st" + s], w=["va" + s])
-
-    def step2_end(s, wo, name, landing):
+        to_list(s, lambda out, r, k: cp(out, so[:, 40 * r + 4:40 * r + 40:5], r=["so" + s], w=[k]))
+        gather(s, so[:, 4:120:5], "so" + s)
         choose(s)
-        vb, fl, w = T["vb" + s], T["fl" + s], T[wo + s]
-        tt(vb[:], T["sb" + s][:], T["va" + s][:], ALU.add, r=["sb" + s, "va" + s], w=["vb" + s])
-        ts(fl[:], vb[:], 3000, -FLAG, ALU.is_ge, ALU.mult, r=["vb" + s], w=["fl" + s])
-        tt(w[:], vb[:], fl[:], ALU.add, r=["vb" + s, "fl" + s], w=[wo + s])
+        v = so[:, 4:120:5]
+        ts(fl[:], v, 3000, -FLAG, ALU.is_ge, ALU.mult, r=["so" + s], w=["fl" + s])
+        tt(w[:], v, fl[:], ALU.add, r=["so" + s, "fl" + s], w=[wo + s])
         if name:
             send(name, part, T[landing][:], w[:], [wo + s], landing, off_)
-        tt(T["df" + s][:], w[:], T["st" + s][:], ALU.subtract, r=[wo + s, "st" + s], w=["df" + s])
+        tt(T["df" + s][:], w[:], st[:], ALU.subtract, r=[wo + s, "st" + s], w=["df" + s])
 
     def merge(s, inn, last=False):
-        to_list(s, T["df" + s][:], T[inn][:], ["df" + s, inn], last)
+        df, i, ks = T["df" + s], T[inn], ["df" + s, inn]
+        to_list(s, lambda out, r, k: tt(out, df[:, 8 * r:8 * r + 8], i[:, 8 * r:8 * r + 8], ALU.add, r=ks, w=[k]), last)
         if not last:
-            tt(T["st" + s][:], T["df" + s][:], T[inn][:], ALU.add, r=["df" + s, inn], w=["st" + s])
+            tt(T["st" + s][:], df[:], i[:], ALU.add, r=ks, w=["st" + s])
 
-    for s, name in (("h", "A"), ("f", "B")):
-        gather(s)
-        step1_end(s)
-        gather(s)
-        step2_end(s, "wo", name, "in" + name.lower())
-    for s, name, inn in (("f", "C", "ina"), ("h", None, "inb")):
-        merge(s, inn)
-        gather(s)
-        step1_end(s)
-        gather(s)
-        step2_end(s, "we", name, "inc")
+    rounds("h", "wo", "A", "ina")
+    rounds("f", "wo", "B", "inb")
+    merge("f", "ina")
+    rounds("f", "we", "C", "inc")
+    merge("h", "inb")
+    rounds("h", "we", None, None)
     merge("h", "inc", last=True)
     ld("s", "d7", T.y[:, :], T.yo[:, 0:23], r=["yo"])
 
@@ -348,7 +353,7 @@ def rank_program(g, core, T, topo):
         start = {n: max(at[n], free.get(ops[n]["q"], 0.0)) for n in ready}
         t0 = min(start.values())
         q0 = ops[min((n for n in ready), key=lambda n: (start[n], n))]["q"]
-        n = max((n for n in ready if ops[n]["q"] == q0 and start[n] <= t0 + 0.03), key=lambda n: (tail[n], -n))
+        n = max((n for n in ready if ops[n]["q"] == q0 and start[n] <= t0 + 0.02), key=lambda n: (tail[n], -n))
         ready.discard(n)
         order.append(n)
         if q0:

@@ -1,33 +1,35 @@
-from concourse.mybir import AluOpType as ALU, ActivationFunctionType as ACTF
+from concourse.mybir import AluOpType as ALU, ActivationFunctionType as ACTF, AxisListType as AX
 
 I32, F32, F16, B16, U16 = "int32", "float32", "float16", "bfloat16", "uint16"
 WN = 2050
 FLAG = 8192
 SCRATCH = {}
 for _d, _s, _n in (
-        (I32, [128, 8, 16], "ixp"), (I32, [128, 16, 16], "ixd ixq"), (I32, [128, 8, 32], "ic"), (I32, [128, 8, 5], "i_s i_n"),
-        (I32, [128, 8, 4, 4], "i_e"), (I32, [128, 8], "i_p i_g i_q i_r i_h"), (I32, [128, 16], "i_m i_l"),
-        (I32, [128, 64], "pb32 pbb dn dsh dhi dlo dnm dshm dhim dlom"), (I32, [128, 128], "pl32 plb ixi"), (I32, [128, 23], "tl32"),
-        (I32, [128, 92], "pf32"), (I32, [128, 16, 23], "pr32"), (B16, [128, 8, 16], "izp"), (B16, [128, 16, 16], "izd izq"),
-        (B16, [128, 8, 8, 16], "yp"), (B16, [128, 16, 8, 16], "yd qq"), (B16, [128, 2, 8, 32], "cc"), (B16, [128, 8, 32], "z0"),
-        (B16, [128, 8, 5], "rn"), (B16, [128, 8, 4, 4], "e24"), (B16, [128, 240], "ee"), (B16, [128, 2064], "w2"),
-        (F32, [128, 2056], "w1"), (F32, [128, 8, 5], "s4 s4a s4b rna rnb"), (F32, [128, 8], "gm xb wb wc"), (F32, [128, 128], "id"),
-        (F32, [128, 64], "dfl dflm"), (F32, [128, 24], "yo"), (F16, [128, 192], "tw tn"), (F16, [128, 92], "lp lpn"),
-        (F16, [128, 24], "llh llf ina inb inc woh wof weh wef"), (F16, [128, 64], "ex exm"),
-        (F16, [128, 16, 23], "pth ptf"), (F16, [128, 24, 8], "rmh rmf"), (F16, [128, 8, 32], "tbh tbf"),
-        (F32, [128, 384], "xh xf prh prf"), (B16, [128, 384], "nbh nbf"), (U16, [128, 24], "offh offf"),
-        (F32, [128, 120], "rs zsh zsf mnh mnf eqh eqf neh nef pph ppf soh sof"), (F32, [128, 24], "sth stf flh flf dfh dff"),
-        (F32, [128, 8, 32], "trh trf")):
+        (I32, [128, 2], "i_p i_b"), (I32, [128, 16], "i_m i_l"), (I32, [128, 64], "pb32 dn dhi dlo dnm dhim dlom"),
+        (I32, [128, 128], "pl32"), (I32, [128, 92], "pf32"),
+        (B16, [128, 1040], "i8"), (B16, [128, 512], "o8"), (B16, [128, 4, 16], "oa e2"), (B16, [128, 2048], "qq"),
+        (B16, [128, 4, 4, 16], "qa"), (B16, [128, 4, 128], "zo"),
+        (B16, [128, 192], "z0"), (B16, [128, 40], "rn"), (B16, [128, 8, 4, 4], "e24"), (B16, [128, 240], "ee"),
+        (B16, [128, 2064], "w2"), (F32, [128, 2056], "w1"), (F32, [128, 40], "s4"), (F32, [128, 128], "id"),
+        (F32, [128, 120], "rs zsh zsf mnh mnf eqh eqf neh nef pph ppf"), (F32, [128, 40, 3], "soh sof"),
+        (F32, [128, 32], "wq"), (F32, [128, 2], "bm"), (F32, [128, 8], "wr xb wb"), (F32, [128, 64], "d2 dfl dflm"),
+        (F32, [128, 24], "yo"), (F16, [128, 128], "thi nhi"), (F16, [128, 64], "tlo nlo dd ex exm"),
+        (F16, [128, 2, 128], "oh om"), (F16, [128, 92], "lp lpn"), (F16, [128, 24], "llh llf"),
+        (F16, [128, 8, 3], "ina inb inc woh wof weh wef"), (F16, [128, 16, 23], "pth ptf"), (F16, [128, 8, 24], "rmh rmf"),
+        (F16, [128, 9, 16], "tbh tbf"), (F32, [128, 384], "xh xf prh prf"), (B16, [128, 384], "nbh nbf"),
+        (U16, [128, 24], "offh offf"), (F32, [128, 8, 3], "sth stf flh flf dfh dff"), (F32, [128, 4, 32], "trh trf")):
     for _k in _n.split():
         SCRATCH[_k] = ("sbuf", _s, _d)
-for _s, _n in (([128, 512], "uh uf nh nf stg0 stg1"), ([128, 16, 32], "lh lf")):
+for _s, _n in (([128, 4, 128], "uh uf nh nf stg0 stg1"), ([128, 16, 32], "lh lf")):
     for _k in _n.split():
         SCRATCH[_k] = ("psum", _s, F32)
-SEMAPHORES = ["sv", "sa", "sp", "sg"] + ["d%d" % k for k in range(10)] + [a + b for a in ("arr", "loc") for b in "TLABC"]
+SEMAPHORES = ["sv", "sa", "sp", "sg"] + ["d%d" % k for k in range(15)] + [a + b for a in ("arr", "loc") for b in "TULABC"]
 CS = {"v": "sv", "a": "sa", "p": "sp", "g": "sg"}
-WAKE = 0.12
-SHORT = {"v": 0.07, "a": 0.3, "p": 0.065, "g": 0.4, "s": 0.06}
-DMA_T, SEND_T = 2.2, {"T": 3.5, "L": 5.5, "A": 2.2, "B": 2.2, "C": 2.2}
+WAKE = [0.18]
+SHORT = {"v": 0.09, "a": 0.36, "p": 0.096, "g": 0.48, "s": 0.072}
+DMA_T, SEND_T = 2.2, {"T": 2.5, "U": 3.4, "L": 3.2, "A": 2.4, "B": 2.4, "C": 2.4}
+BIAS = {"f0": -4, "f1": -4, "f2": 4, "h0": 6}
+WIN = [0.02]
 
 
 def rank_program(g, core, T, topo):
@@ -41,7 +43,7 @@ def rank_program(g, core, T, topo):
     V, S, PE, SY = g.vector, g.scalar, g.tensor, g.sync
     Q = {"v": V, "a": S, "p": PE, "s": SY, "g": g}
 
-    ops, base, app, rd = [], {}, {}, {}
+    ops, base, app, rd, grp = [], {}, {}, {}, [""]
 
     def add(q, fn, r=(), w=(), cost=None, dma=None, send=None, arr=None):
         n = len(ops)
@@ -63,7 +65,8 @@ def rank_program(g, core, T, topo):
                 base[k0], app[k0], rd[k0] = [n], [], []
         for k in r:
             rd.setdefault(k, []).append(n)
-        ops.append(dict(q=q, fn=fn, hard=hard - {n}, soft=soft, cost=SHORT[q] if cost is None else cost, dma=dma, send=send, arr=arr))
+        ops.append(dict(q=q, fn=fn, hard=hard - {n}, soft=soft, cost=SHORT[q] if cost is None else cost, dma=dma, send=send, arr=arr,
+                        grp=grp[0]))
 
     def ts(out, i, s1, s2, o0, *o1, r=(), w=(), cost=None):
         add("v", lambda: V.tensor_scalar(out, i, s1, s2, o0, *o1), r, w, cost)
@@ -71,8 +74,8 @@ def rank_program(g, core, T, topo):
     def tt(out, a, b, op, r=(), w=(), cost=None):
         add("v", lambda: V.tensor_tensor(out, a, b, op), r, w, cost)
 
-    def scan(out, a, b, o0, o1, r=(), w=()):
-        add("v", lambda: V.tensor_tensor_scan(out, a, b, 0.0, o0, o1), r, w, 0.12)
+    def scan(out, a, b, o0, o1, r=(), w=(), cost=None):
+        add("v", lambda: V.tensor_tensor_scan(out, a, b, 0.0, o0, o1), r, w, cost)
 
     def cp(out, i, r=(), w=(), cost=None):
         add("v", lambda: V.tensor_copy(out, i), r, w, cost)
@@ -89,147 +92,157 @@ def rank_program(g, core, T, topo):
     def ld(q, sem, out, i, r=(), w=()):
         add(q, lambda: Q[q].dma_start(out, i), r, w, dma=sem)
 
-    def io(key, pat, first, cm):
-        add("g", lambda: g.iota(T[key][:], pat, first, cm), (), [key])
+    def sel(key, ap, pat, op, fill, first, cm, cost=0.25):
+        add("g", lambda: g.affine_select(ap, ap, pat, op, fill, first, cm), [key], [key], cost)
 
     def send(name, dst_rank, out, src, keys, landing, engines):
         rid, pid, _ = topo.addr(T.cores[dst_rank])
         add("g", lambda: g.remote_dma(out, src, T.sem["arr" + name], T.sem["loc" + name], pid, rid, sum(1 << e for e in engines)),
-            keys, w=["+order"] if name in "LT" else (), cost=0.6, send=(name, len(engines)))
-        ops.append(dict(q=None, fn=None, hard={len(ops) - 1}, soft=set(), cost=0.0, dma=None, send=None, arr=(name, len(engines))))
+            keys, w=["+order"] if name in "LTU" else (), cost=1.6 if name == "L" else 0.6, send=(name, len(engines)))
+        ops.append(dict(q=None, fn=None, hard={len(ops) - 1}, soft=set(), cost=0.0, dma=None, send=None, arr=(name, len(engines)), grp=""))
         base[landing] = [len(ops) - 1]
 
-    on = topo.engines(core, T.cores[mate])[::2]
+    on = topo.engines(core, T.cores[mate])
     off_ = topo.engines(core, T.cores[part])
 
-    ld("s", "d0", T.pl32[:], T.planes[:, :], w=["pl32"])
-    ld("a", "d1", T.pb32[0:64, :], T.planes[3::4, :], w=["pb32d"])
-    ld("s", "d4", T.pf32[0:96, :], T.pts[:, :], w=["pf32p"])
-    ld("a", "d8", T.pf32[96:128, :], T.tet0[:, :], w=["pf32t"])
+    def spread(s, sem, src, key):
+        ld("s", sem[0], T["ll" + s][:, 0:23], src[96:128, :], r=[key], w=["ll" + s])
+        for k in range(8):
+            ld("s", sem[1], T["rm" + s][16 * k:16 * k + 16, k, 0:23], src[96 + 4 * k:100 + 4 * k, :], r=[key], w=["+rm" + s])
+
+    ld("s", "d3", T.pf32[0:96, :], T.pts[:, :], w=["pf32p"])
+    ld("a", "d4", T.pf32[96:128, :], T.tet0[:, :], w=["pf32t"])
     ld("s", "d2", T.pb32[64:128, :], T.nbr[:, :], w=["pb32n"])
-    ld("a", "d3", T.tl32[:], T.tet0[:, :], w=["tl32"])
-    ld("s", "d5", T.pr32[0:24], T.pts[:, :], w=["pr32"])
+    ld("a", "d1", T.pb32[0:64, :], T.planes[3::4, :], w=["pb32d"])
+    ld("s", "d0", T.pl32[:], T.planes[:, :], w=["pl32"])
     cp(T.lp[0:96, :], T.pf32[0:96, :], r=["pf32p"], w=["lp0"], cost=0.1)
     ts(T.lp[96:128, :], T.pf32[96:128, :], -2047, None, ALU.add, r=["pf32t"], w=["lp1"], cost=0.1)
     send("L", part, T.lpn[:], T.lp[:], ["lp0", "lp1"], "lpn", off_)
-    ts(T.plb[:], T.pl32[:], 1024, None, ALU.add, r=["pl32"], w=["plb"], cost=0.13)
-    ts(T.pbb[0:64, :], T.pb32[0:64, :], 1024, None, ALU.add, r=["pb32d"], w=["pbb"])
-    ts(T.pl32[:], T.plb[:], 2047, None, ALU.bitwise_and, r=["plb"], w=["pl32"], cost=0.13)
-    ts(T.pb32[0:64, :], T.pbb[0:64, :], 11, None, ALU.arith_shift_right, r=["pbb"], w=["pb32d"])
-    ts(T.tw[64:128, 128:192], T.pb32[64:128, :], -2047, None, ALU.add, r=["pb32n"], w=["tw2"])
-    ts(T.tw[:, 0:128], T.pl32[:], -1024, None, ALU.add, r=["pl32"], w=["tw0"], cost=0.13)
-    cp(T.tw[0:64, 128:192], T.pb32[0:64, :], r=["pb32d"], w=["tw1"])
-    send("T", mate, T.tn[:], T.tw[:], ["tw0", "tw1", "tw2"], "tn", on)
-    ts(T.llh[:, 0:23], T.tl32[:], -2047, None, ALU.add, r=["tl32"], w=["llh"])
-    io("ixp", [[1, 8], [8, 16]], 0, -1)
-    io("ixq", [[1, 16], [16, 4], [500, 4]], -1500, -1)
-    io("i_p", [[0, 8]], 0, 1)
-    io("ixd", [[1, 16], [16, 16]], 0, -1)
-    io("i_e", [[3, 8], [0, 4], [1, 4]], 0, -1)
-    io("i_m", [[-1, 16]], 256, 1)
-    io("i_g", [[-16, 2], [-32, 4]], 0, 1)
-    io("i_s", [[-16, 2], [-32, 4], [-4, 5]], 4, 1)
-    io("i_n", [[-16, 2], [-32, 4], [-1, 5]], 1, 1)
-    io("ic", [[16, 8], [1, 32]], 0, -1)
-    io("ixi", [[1, 128]], 0, -1)
-    ts(T.izp[:], T.ixp[:], 0, None, ALU.is_equal, r=["ixp"], w=["izp"], cost=0.13)
-    ts(T.izq[:], T.ixq[:], 0, 2048, ALU.is_equal, ALU.mult, r=["ixq"], w=["izq"], cost=0.26)
-    ts(T.izd[:], T.ixd[:], 0, None, ALU.is_equal, r=["ixd"], w=["izd"], cost=0.26)
+    ts(T.dd[0:64, :], T.pb32[0:64, :], 0.015625, None, ALU.mult, r=["pb32d"], w=["dd"])
+    ts(T.d2[0:64, :], T.pb32[0:64, :], 0.015625, None, ALU.mult, r=["pb32d"], w=["d2"])
+    ts(T.tlo[64:128, :], T.pb32[64:128, :], -2047, None, ALU.add, r=["pb32n"], w=["tlo2"])
+    tt(T.tlo[0:64, :], T.d2[0:64, :], T.dd[0:64, :], ALU.subtract, r=["d2", "dd"], w=["tlo1"], cost=0.13)
+    send("T", mate, T.nlo[:], T.tlo[:], ["tlo1", "tlo2"], "nlo", on[1::2])
+    ts(T.thi[:], T.pl32[:], 0.015625, None, ALU.mult, r=["pl32"], w=["thi"], cost=0.13)
+    send("U", mate, T.nhi[:], T.thi[:], ["thi"], "nhi", on[::2])
+    for ap, c, key in ((T.i8[:, 0:128], 0, "i8a"), (T.i8[:, 1024:1040], 0, "i8p"), (T.qa[0:64], 0, "qa"), (T.oa[0:80], 0, "oa"),
+                       (T.zo[0:64], 0, "zo"), (T.zsh[:], 0, "zsh"), (T.zsf[:], 0, "zsf"), (T.z0[:], 0, "z0"),
+                       (T.s4[:], 256, "s4"), (T.rn[:], 0, "rn"), (T.e2[:], 0, "e2"), (T.e24[0:32], 0, "e24"), (T.ee[:], 0, "ee"),
+                       (T.rs[:], -1e9, "rs"), (T.rs[:, 0:120:5], 0, "rs"), (T.id[:], 0, "id"),
+                       (T.xh[:, 368:384], 0, "xhp"), (T.xf[:, 368:384], 0, "xfp"), (T.offh[:, 23:24], 0, "offh2"), (T.offf[:, 23:24], 0, "offf2")):
+        ms(ap, c, w=[key], cost=0.12)
+    add("g", lambda: g.iota(T.i_p[:], [[0, 2]], 0, 1), (), ["i_p"], 0.2)
+    sel("i8a", T.i8[:, 0:128], [[-1, 128]], ALU.not_equal, 1.0, 0, 1, 0.42)
+    sel("oa", T.oa[0:80], [[-16, 4], [-1, 16]], ALU.not_equal, 1.0, 0, 1, 0.28)
+    sel("oa", T.oa[0:80, :, 12:16], [[-4, 4], [-1, 4]], ALU.not_equal, 1.0, -64, 1, 0.2)
+    sel("qa", T.qa[0:64, :, 3, :], [[-16, 4], [-1, 16]], ALU.not_equal, 1.0, 0, 1, 0.3)
+    add("g", lambda: g.iota(T.wq[:], [[0, 8], [1, 4]], 1, 0, allow_small_or_imprecise_dtypes=True), (), ["wq"], 0.25)
+    sel("wq", T.wq[:], [[-16, 8], [-4, 4]], ALU.is_equal, 0.0, -3, 1)
+    add("g", lambda: g.iota(T.i_m[:], [[-1, 16]], 256, 1), (), ["i_m"], 0.2)
+    sel("e24", T.e24[0:32, :, :, 0:3], [[-3, 8], [0, 4], [-1, 3]], ALU.not_equal, 1.0, 0, 1, 0.35)
+    sel("s4", T.s4[:], [[-16, 8], [-4, 5]], ALU.is_ge, 0.0, 4, 1)
+    sel("s4", T.s4[:], [[16, 8], [4, 5]], ALU.is_ge, 0.0, -1, -1)
+    ms(T.s4[:, 0:40:5], 0, w=["s4"])
+    sel("rn", T.rn[:], [[-16, 8], [-2, 5]], ALU.not_equal, 1.0, 2, 1)
+    sel("rn", T.rn[:], [[-16, 8], [-2, 5]], ALU.not_equal, 64.0, -6, 1)
+    ms(T.rn[:, 0:40:5], 0, w=["rn"])
+    sel("id", T.id[:], [[-1, 128]], ALU.not_equal, 1.0, 0, 1, 0.42)
+    sel("e2", T.e2[:], [[-32, 4], [-1, 16]], ALU.not_equal, 1.0, 0, 1, 0.3)
+    sel("e2", T.e2[:], [[-32, 4], [-1, 16]], ALU.not_equal, 1.0, -16, 1, 0.3)
     for k in range(8):
-        cp(T.yp[:, :, k, :], T.izp[:], r=["izp"], w=["+yp"])
-        for out, i, key, w in ((T.qq[0:64, :, k, :], T.izq[0:64], "izq", "+qq"), (T.yd[:, :, k, :], T.izd[:], "izd", "+yd")):
-            if k % 2:
-                act(out, i, r=[key], w=[w], cost=0.45)
-            else:
-                cp(out, i, r=[key], w=[w], cost=0.13)
-    ts(T.i_q[:], T.i_p[:], 3, None, ALU.bitwise_and, r=["i_p"], w=["i_q"])
-    ts(T.i_r[:], T.i_p[:], 15, 2, ALU.bitwise_and, ALU.arith_shift_right, r=["i_p"], w=["i_r"])
-    ts(T.xb[:], T.i_q[:], 3, None, ALU.is_equal, r=["i_q"], w=["xb"])
-    ts(T.wc[:], T.i_r[:], 1, 0.25, ALU.add, ALU.mult, r=["i_r"], w=["wc"])
-    tt(T.wb[:], T.wc[:], T.xb[:], ALU.mult, r=["wc", "xb"], w=["wb"])
-    ms(T.z0[:], 0, w=["z0"], cost=0.13)
-    ts(T.e24[0:32], T.i_e[0:32], 0, None, ALU.is_equal, r=["i_e"], w=["e24"], cost=0.13)
-    ms(T.e24[0:32, :, :, 3], 0, w=["e24"])
-    cp(T.pth[0:24], T.pr32[0:24], r=["pr32"], w=["pth"], cost=0.37)
-    ms(T.xh[:, 368:384], 0, w=["xhp"])
-    ms(T.xf[:, 368:384], 0, w=["xfp"])
-    ms(T.ee[:], 0, w=["ee"], cost=0.12)
-    ms(T.cc[:], 0, w=["cc"], cost=0.26)
-    ms(T.rs[:], -1e9, w=["rs"], cost=0.12)
-    ms(T.rs[:, 0:120:5], 0, w=["rs"])
-    ts(T.i_h[:], T.i_g[:], 4, None, ALU.arith_shift_right, r=["i_g"], w=["i_h"])
+        cp(T.o8[0:80, 64 * k:64 * k + 64], T.oa[0:80], r=["oa"], w=["+o8"])
+        if k:
+            cp(T.i8[:, 128 * k:128 * k + 128], T.i8[:, 0:128], r=["i8a"], w=["+i8"])
+        if k in (2, 4, 6):
+            cp(T.qq[0:64, 256 * k:256 * k + 256], T.qa[0:64], r=["qa"], w=["+qq"], cost=0.12)
+        else:
+            act(T.qq[0:64, 256 * k:256 * k + 256], T.qa[0:64], r=["qa"], w=["+qq"], cost=0.3)
+    add("v", lambda: V.tensor_reduce(T.wr[:, 0:1], T.wq[:], AX.X, ALU.add), ["wq"], ["wr"])
+    ts(T.xb[:, 0:1], T.wr[:, 0:1], 1, None, ALU.min, r=["wr"], w=["xb"])
+    ts(T.wb[:, 0:1], T.wr[:, 0:1], 0.00390625, None, ALU.mult, r=["wr"], w=["wb"])
     ts(T.i_l[:], T.i_m[:], 15, None, ALU.bitwise_and, r=["i_m"], w=["i_l"])
-    ts(T.s4a[:], T.i_s[:], 0, 4, ALU.is_ge, ALU.mult, r=["i_s"], w=["s4a"])
-    ts(T.s4b[:], T.i_s[:], 3, None, ALU.is_le, r=["i_s"], w=["s4b"])
-    ts(T.rna[:], T.i_n[:], 4, 64, ALU.is_equal, ALU.mult, r=["i_n"], w=["rna"])
-    ts(T.rnb[:], T.i_n[:], 0, None, ALU.is_equal, r=["i_n"], w=["rnb"])
-    ts(T.gm[:], T.i_h[:], 0, None, ALU.is_equal, r=["i_h"], w=["gm"])
     ts(T.ee[:, 112:128], T.i_l[:], 0, None, ALU.is_equal, r=["i_l"], w=["ee"])
-    ts(T.id[:], T.ixi[:], 0, None, ALU.is_equal, r=["ixi"], w=["id"], cost=0.13)
-    tt(T.s4[:], T.s4a[:], T.s4b[:], ALU.mult, r=["s4a", "s4b"], w=["s4"])
-    ms(T.s4[:, :, 0], 0, w=["s4"])
-    tt(T.rn[:], T.rna[:], T.rnb[:], ALU.add, r=["rna", "rnb"], w=["rn"])
-    ms(T.rn[:, :, 0], 0, w=["rn"])
-    for k in range(2):
-        ts(T.cc[:, k, :, 16 * k:16 * k + 16], T.ic[:, :, 16 * k:16 * k + 16], 16 * k, None, ALU.is_equal, r=["ic"], w=["+cc"], cost=0.13)
+    ts(T.i_b[:], T.i_p[:], 16, None, ALU.bitwise_and, r=["i_p"], w=["i_b"])
+    for bl in range(2):
+        ts(T.bm[:, bl:bl + 1], T.i_b[:, bl:bl + 1], 16 * bl, None, ALU.is_equal, r=["i_b"], w=["+bm"])
     for s in "hf":
-        ms(T["zs" + s][:], 0, w=["zs" + s], cost=0.12)
-        cp(T["tb" + s][:], T.z0[:], r=["z0"], w=["tb" + s], cost=0.13)
+        cp(T["tb" + s][:], T.z0[:, 0:144], r=["z0"], w=["tb" + s], cost=0.08)
+        cp(T["rm" + s][:], T.z0[:], r=["z0"], w=["rm" + s], cost=0.09)
+    cp(T.om[0:64], T.zo[0:64, 0:2, :], r=["zo"], w=["om"], cost=0.13)
     for c in (0, WN - 1):
         cp(T.w1[:, c:c + 1], T.xb[:, 0:1], r=["xb"], w=["+w1_d"])
         ms(T.w2[:, c:c + 1], 0, w=["+w2_d"])
+    ld("s", "d6", T.pth[0:24], T.lp[0:96, :], r=["lp0"], w=["pth"])
+    spread("h", ("d7", "d10"), T.lp, "lp1")
 
     def first_list(s):
         off, v, ks = T["off" + s], T["ll" + s][:, 0:23], ["+off%s%d" % (s, r) for r in range(3)]
-        ms(off[:, 23:24], 0, w=ks[2:])
         if low == 0:
             ts(off[:, 0:23], v, 1, 2048, ALU.min, ALU.add, r=["ll" + s], w=ks)
         else:
             ts(off[:, 0:23], v, 0, None, ALU.max, r=["ll" + s], w=ks)
 
-    nb_ = [0, 0]
-
-    def bank():
-        nb_[0] ^= 1
-        return ("stg0", "stg1")[nb_[0]]
-
-    def copy_out(dst, src, bias, r, w):
-        nb_[1] ^= 1
-        if nb_[1]:
-            act(dst, src, r, w, bias=0.0 if bias is None else bias, cost=0.7)
+    def copy_out(q, dst, src, bias, r, w):
+        if q == "a":
+            act(dst, src, r, w, bias=0.0 if bias is None else bias, cost=0.55)
         elif bias is None:
             cp(dst, src, r, w, cost=0.5)
         else:
             ts(dst, src, bias, None, ALU.add, r=r, w=w, cost=0.5)
 
-    def expand_planes(src, keys, z):
-        for h in range(2):
-            b = bank()
-            for tb in range(8 * h, 8 * h + 8):
-                o, lh, rh = T[b][:, 64 * (tb % 8):64 * (tb % 8) + 64], T.yp[:, tb // 2], src[:, 64 * (tb % 2):64 * (tb % 2) + 64]
-                mm(o, lh, rh, True, False, r=["yp", keys[0]], w=["+" + b, "+half%d" % z])
-                mm(o, T.qq[0:64, tb], src[0:64, 128:192], False, True, r=["qq", keys[1]], w=["+" + b, "+half%d" % z])
-            c0 = 1 + 1024 * z + 512 * h
-            copy_out(T.w1[:, c0:c0 + 512], T[b][:], T.wb[:, 0:1], [b, "wb"], ["w1_%d_%d" % (z, h)])
-
-    def moves(src, key, q, m):
-        n, P = src[64:128, 128:192], slice(64, 128)
-        dn, sh, fl, hi, lo, ex = (T[k + m] for k in ("dn", "dsh", "dfl", "dhi", "dlo", "ex"))
-        ts(dn[P, :], n, -1, None, ALU.add, r=[key], w=["dn" + m])
-        ts(sh[P, :], dn[P, :], 10, None, ALU.arith_shift_right, r=["dn" + m], w=["sh" + m])
-        ts(fl[P, :], sh[P, :], q - 2, FLAG // 64, ALU.not_equal, ALU.mult, r=["sh" + m], w=["fl_" + m])
+    def move_values(lo, key, q, m):
+        P = slice(64, 128)
+        dn, fl, hi, lw, ex = (T[k + m] for k in ("dn", "dfl", "dhi", "dlo", "ex"))
+        ts(dn[P, :], lo[P, :], -1, None, ALU.add, r=[key], w=["dn" + m])
+        ts(fl[P, :], dn[P, :], 1024 * (low + 1) - 2048, FLAG // 64, ALU.is_ge if q == low else ALU.is_lt, ALU.mult, r=["dn" + m], w=["fl_" + m])
         ts(hi[P, :], dn[P, :], 6, None, ALU.arith_shift_right, r=["dn" + m], w=["hi" + m])
-        ts(lo[P, :], dn[P, :], 63, None, ALU.bitwise_and, r=["dn" + m], w=["lo" + m])
+        ts(lw[P, :], dn[P, :], 63, None, ALU.bitwise_and, r=["dn" + m], w=["lo" + m])
         tt(ex[P, :], hi[P, :], fl[P, :], ALU.add, r=["hi" + m, "fl_" + m], w=["+ex" + m], cost=0.13)
-        ts(ex[0:64, :], lo[P, :], 1, None, ALU.add, r=["lo" + m], w=["+ex" + m])
+        ts(ex[0:64, :], lw[P, :], 1, None, ALU.add, r=["lo" + m], w=["+ex" + m])
 
-    def expand_moves(z, m):
-        for h in range(2):
-            b = bank()
-            for tb in range(8 * h, 8 * h + 8):
-                mm(T[b][:, 64 * (tb % 8):64 * (tb % 8) + 64], T.yd[:, tb], T["ex" + m][:], True, True, r=["yd", "ex" + m], w=["+" + b])
-            c0 = 1 + 1024 * z + 512 * h
-            copy_out(T.w2[:, c0:c0 + 512], T[b][:], None, [b], ["w2_%d_%d" % (z, h)])
+    def own_table(z):
+        for k, (src, K, key, banks) in enumerate(((T.oh, 80, "oh", ("stg0", "stg1")), (T.om, 64, "om", ("nh", "nf")))):
+            for h in range(2):
+                b = banks[h]
+                for c in (2 * h, 2 * h + 1):
+                    mm(T[b][:, 2 * (c % 2):2 * (c % 2) + 2, :], T.o8[0:K, c:c + 509:4], src[0:K], True, True,
+                       r=["o8", key], w=["+" + b, "+pe"], cost=0.23)
+                c0 = 1 + 1024 * z + 512 * h
+                if k:
+                    copy_out("av"[h], T.w2[:, c0:c0 + 512], T[b][:], None, [b], ["w2_%d_%d" % (z, h)])
+                else:
+                    copy_out("av"[h], T.w1[:, c0:c0 + 512], T[b][:], T.wb[:, 0:1], [b, "wb"], ["w1_%d_%d" % (z, h)])
+
+    def mate_table(z):
+        def small(h):
+            b = ("uh", "uf")[h]
+            for tb in range(8):
+                x = 64 * (tb % 2)
+                mm(T[b][:, tb // 2, x:x + 64], T.qq[0:64, 8 * h + tb:8 * h + tb + 2033:16], T.nlo[0:64, :], False, False,
+                   r=["qq", "nlo"], w=["+" + b, "+pe"])
+
+        def large(h):
+            b, c0 = ("uh", "uf")[h], 1 + 1024 * z + 512 * h
+            for cb in range(4):
+                mm(T[b][:, cb, :], T.i8[:, 4 * h + cb:4 * h + cb + 1017:8], T.nhi[:], False, cb == 3, r=["i8", "i8a", "nhi"], w=["+" + b, "+pe"], cost=0.13)
+            copy_out("v", T.w1[:, c0:c0 + 512], T[b][:], T.wb[:, 0:1], [b, "wb"], ["w1_%d_%d" % (z, h)])
+
+        def move(h):
+            b, c0 = "stg%d" % h, 1 + 1024 * z + 512 * h
+            for tb in range(8):
+                x = 64 * (tb % 2)
+                mm(T[b][:, tb // 2, x:x + 64], T.i8[:, 8 * h + tb:8 * h + tb + 1017:8], T.exm[:], True, True,
+                   r=["i8", "i8a", "i8p", "exm"], w=["+" + b, "+pe"])
+            copy_out("a", T.w2[:, c0:c0 + 512], T[b][:], None, [b], ["w2_%d_%d" % (z, h)])
+
+        for b in ("uh", "uf"):
+            mm(T[b][:], T.zo[0:64, 0, :], T.zo[0:64], True, False, r=["zo"], w=["+" + b], cost=0.45)
+        small(0)
+        small(1)
+        move(0)
+        large(0)
+        large(1)
+        move(1)
 
     def expand_points(s):
         b, x = T["l" + s][:, :, 0:23], T["x" + s]
@@ -238,25 +251,27 @@ def rank_program(g, core, T, topo):
 
     def to_points(s):
         rm, l = T["rm" + s], T["l" + s]
-        cp(rm[:, 23, :], T.z0[:, 0, 0:8], r=["z0"], w=["+rm" + s])
-        for k in range(8):
-            ts(rm[:, 0:23, k], T["ll" + s][:, 0:23], T.gm[:, k:k + 1], None, ALU.mult, r=["gm", "ll" + s], w=["+rm" + s])
         for b in range(8):
-            mm(l[:, 0:3, 0:8], T.ee[:, 112 - 16 * b:240 - 16 * b], rm[:, b::8, :], b == 0, b == 7, r=["ee", "rm" + s], w=["+l" + s])
-        cp(T["st" + s][:], l[:, 0:3, 0:8], r=["l" + s], w=["st" + s])
+            mm(l[:, 0:8, 0:3], T.ee[:, 112 - 16 * b:240 - 16 * b], rm[:, :, b::8], b == 0, b == 7, r=["ee", "rm" + s], w=["+l" + s])
+        cp(T["st" + s][:], l[:, 0:8, 0:3], r=["l" + s], w=["st" + s])
 
     zw, zh = (0, 1) if rank == low else (1, 0)
-    moves(T.tw, "tw2", rank, "")
-    expand_planes(T.tw, ("tw0", "tw1"), zw)
-    expand_moves(zw, "")
+    move_values(T.tlo, "tlo2", rank, "")
+    ld("s", "d12", T.oh[0:64], T.thi[:], r=["thi"], w=["+oh"])
+    ld("s", "d13", T.oh[64:80], T.tlo[0:64, :], r=["tlo1"], w=["+oh"])
+    for k in range(8):
+        ld("s", "d14", T.om[8 * k:8 * k + 4], T.ex[16 * k:16 * k + 16, :], r=["ex"], w=["+om"])
+    own_table(zw)
     expand_points("h")
     first_list("h")
+    grp[0] = "h0"
     to_points("h")
-    moves(T.tn, "tn", mate, "m")
-    expand_planes(T.tn, ("tn", "tn"), zh)
-    expand_moves(zh, "m")
-    ld("s", "d9", T.llf[:, 0:23], T.lpn[96:128, :], r=["lpn"], w=["llf"])
-    ld("s", "d6", T.ptf[0:24], T.lpn[0:96, :], r=["lpn"], w=["ptf"])
+    grp[0] = ""
+    move_values(T.nlo, "nlo", mate, "m")
+    mate_table(zh)
+    spread("f", ("d9", "d11"), T.lpn, "lpn")
+    ld("s", "d8", T.ptf[0:24], T.lpn[0:96, :], r=["lpn"], w=["ptf"])
+    grp[0] = "f0"
     first_list("f")
     expand_points("f")
     to_points("f")
@@ -270,49 +285,52 @@ def rank_program(g, core, T, topo):
             c = slice(128 * r, 128 * r + 128)
             add("v", lambda: V.tensor_tensor(T["pr" + s][:, c], T.w1[:, 0:WN].indirect(off[:, 8 * r:8 * r + 8]), T["x" + s][:, c], ALU.mult),
                 ["w1" + k for k in halves] + [ks[r], "x" + s, "x%sp" % s], ["pr%s%d" % (s, r)], cost=0.25)
-            mm(T["u" + s][:, 40 * r:40 * r + 40], T["pr" + s][:, c], T.s4[:], True, True, r=["pr%s%d" % (s, r), "s4"], w=["+u" + s], cost=0.26)
+            mm(T["u" + s][:, 0, 40 * r:40 * r + 40], T["pr" + s][:, c], T.s4[:], True, True, r=["pr%s%d" % (s, r), "s4"], w=["+u" + s], cost=0.22)
 
-        cp(T["zs" + s][:, 0:120:5], state, r=[key], w=["zs" + s])
-        mm(T["n" + s][:, 0:120], T.id[:], T["zs" + s][:], True, False, r=["id", "zs" + s], w=["+n" + s], cost=0.48)
         for r in range(3):
             third(r)
-        act(T["nb" + s][:], T.w2[:, 0:WN].indirect(off[:, 0:24]), ["w2" + k for k in halves] + ks, ["nb" + s], cost=0.77)
+        act(T["nb" + s][:], T.w2[:, 0:WN].indirect(off[:, 0:24]), ["w2" + k for k in halves] + ks, ["nb" + s], cost=0.65)
         for r in range(3):
-            mm(T["n" + s][:, 40 * r:40 * r + 40], T["nb" + s][:, 128 * r:128 * r + 128], T.rn[:], False, r == 2, r=["nb" + s, "rn"], w=["+n" + s])
+            act(T["zs" + s][:, 40 * r:40 * r + 40:5], state[r], r=[key], w=["+zs" + s], cost=0.1)
+        mm(T["n" + s][:, 0, 0:120], T.id[:], T["zs" + s][:], True, False, r=["id", "zs" + s], w=["+n" + s], cost=0.4)
+        for r in range(3):
+            mm(T["n" + s][:, 0, 40 * r:40 * r + 40], T["nb" + s][:, 128 * r:128 * r + 128], T.rn[:], False, r == 2, r=["nb" + s, "rn"], w=["+n" + s])
 
     def choose(s):
-        u, n = T["u" + s][:, 0:120], T["n" + s][:, 0:120]
-        mn, eq, ne, pp, so = (T[k + s][:] for k in ("mn", "eq", "ne", "pp", "so"))
-        scan(mn, T.rs[:], u, ALU.max, ALU.min, r=["rs", "u" + s], w=["mn" + s])
-        tt(eq, u, mn, ALU.is_equal, r=["u" + s, "mn" + s], w=["eq" + s], cost=0.12)
-        tt(pp, eq, n, ALU.mult, r=["eq" + s, "n" + s], w=["pp" + s], cost=0.12)
-        tt(ne, u, mn, ALU.not_equal, r=["u" + s, "mn" + s], w=["ne" + s], cost=0.12)
-        scan(so, ne, pp, ALU.mult, ALU.add, r=["ne" + s, "pp" + s], w=["so" + s])
+        u, n = T["u" + s][:, 0, 0:120], T["n" + s][:, 0, 0:120]
+        mn, eq, ne, pp, so = (T[k + s] for k in ("mn", "eq", "ne", "pp", "so"))
+        scan(mn[:], T.rs[:], u, ALU.max, ALU.min, r=["rs", "u" + s], w=["mn" + s], cost=0.12)
+        tt(eq[:], u, mn[:], ALU.is_equal, r=["u" + s, "mn" + s], w=["eq" + s], cost=0.12)
+        tt(pp[:], eq[:], n, ALU.mult, r=["eq" + s, "n" + s], w=["pp" + s], cost=0.12)
+        tt(ne[:], u, mn[:], ALU.not_equal, r=["u" + s, "mn" + s], w=["ne" + s], cost=0.12)
+        for r in range(3):
+            c = slice(40 * r, 40 * r + 40)
+            scan(so[:, :, r], ne[:, c], pp[:, c], ALU.mult, ALU.add, r=["ne" + s, "pp" + s], w=["+so" + s])
 
-    def to_list(s, put, last=False):
+    def to_list(s, src, key, last=False):
         tb, l, tr = T["tb" + s], T["l" + s], T["tr" + s]
-        for r in range(3):
-            put(tb[:, :, r], r, "+tb" + s)
+        for bl in range(2):
+            ts(tb[:, 0:8, bl:6:2], src, T.bm[:, bl:bl + 1], None, ALU.mult, r=[key, "bm"], w=["+tb" + s])
         for par in range(2):
-            mm(l[:, 0:8, :], tb[:, 4 * par:4 * par + 4, :], T.cc[:, par], par == 0, par == 1, r=["tb" + s, "cc"], w=["+l" + s], cost=0.26)
-        add("v", lambda: V.transpose(tr[:], l[:, 0:8, :]), ["l" + s], ["tr" + s], cost=0.26)
+            mm(l[:, 0:4, 16 * par:16 * par + 16], tb[:, par:par + 8, :], T.e2[:], True, True, r=["tb" + s, "e2"], w=["+l" + s])
+        add("v", lambda: V.transpose(tr[:], l[:, 0:4, :]), ["l" + s], ["tr" + s], cost=0.13)
         for r in range(3):
-            src, c, k = tr[:, :, r], slice(8 * r, 8 * r + 8), ["off%s%d" % (s, r)]
+            v, c, k = tr[:, :, 2 * r:2 * r + 2], slice(8 * r, 8 * r + 8), ["off%s%d" % (s, r)]
             if last:
-                ts(T.yo[:, c], src, 2047, None, ALU.add, r=["tr" + s], w=["+yo"])
+                ts(T.yo[:, c], v, 2047, None, ALU.add, r=["tr" + s], w=["+yo"])
             elif low == 0:
-                ts(T["off" + s][:, c], src, 1, 2048, ALU.min, ALU.add, r=["tr" + s], w=k)
+                ts(T["off" + s][:, c], v, 1, 2048, ALU.min, ALU.add, r=["tr" + s], w=k)
             else:
-                ts(T["off" + s][:, c], src, 2049, 0, ALU.min, ALU.max, r=["tr" + s], w=k)
+                ts(T["off" + s][:, c], v, 2049, 0, ALU.min, ALU.max, r=["tr" + s], w=k)
 
     def rounds(s, wo, name, landing):
         so, st, fl, w = T["so" + s], T["st" + s], T["fl" + s], T[wo + s]
-        gather(s, st[:], "st" + s)
+        v = so[:, 4::5, :]
+        gather(s, [st[:, :, r] for r in range(3)], "st" + s)
         choose(s)
-        to_list(s, lambda out, r, k: cp(out, so[:, 40 * r + 4:40 * r + 40:5], r=["so" + s], w=[k]))
-        gather(s, so[:, 4:120:5], "so" + s)
+        to_list(s, v, "so" + s)
+        gather(s, [so[:, 4::5, r] for r in range(3)], "so" + s)
         choose(s)
-        v = so[:, 4:120:5]
         ts(fl[:], v, 3000, -FLAG, ALU.is_ge, ALU.mult, r=["so" + s], w=["fl" + s])
         tt(w[:], v, fl[:], ALU.add, r=["so" + s, "fl" + s], w=[wo + s])
         if name:
@@ -320,19 +338,21 @@ def rank_program(g, core, T, topo):
         tt(T["df" + s][:], w[:], st[:], ALU.subtract, r=[wo + s, "st" + s], w=["df" + s])
 
     def merge(s, inn, last=False):
-        df, i, ks = T["df" + s], T[inn], ["df" + s, inn]
-        to_list(s, lambda out, r, k: tt(out, df[:, 8 * r:8 * r + 8], i[:, 8 * r:8 * r + 8], ALU.add, r=ks, w=[k]), last)
-        if not last:
-            tt(T["st" + s][:], df[:], i[:], ALU.add, r=ks, w=["st" + s])
+        tt(T["st" + s][:], T["df" + s][:], T[inn][:], ALU.add, r=["df" + s, inn], w=["st" + s])
+        to_list(s, T["st" + s][:], "st" + s, last)
 
+    grp[0] = "h1"
     rounds("h", "wo", "A", "ina")
+    grp[0] = "f1"
     rounds("f", "wo", "B", "inb")
+    grp[0] = "f2"
     merge("f", "ina")
     rounds("f", "we", "C", "inc")
+    grp[0] = "h2"
     merge("h", "inb")
     rounds("h", "we", None, None)
     merge("h", "inc", last=True)
-    ld("s", "d7", T.y[:, :], T.yo[:, 0:23], r=["yo"])
+    ld("s", "d5", T.y[:, :], T.yo[:, 0:23], r=["yo"])
 
     N = len(ops)
     succ = [[] for _ in ops]
@@ -345,7 +365,9 @@ def rank_program(g, core, T, topo):
 
     tail = [0.0] * N
     for n in range(N - 1, -1, -1):
-        tail[n] = lat(ops[n]) + max([tail[m] + WAKE for m in succ[n]], default=0.0)
+        tail[n] = lat(ops[n]) + max([tail[m] + WAKE[0] for m in succ[n]], default=0.0)
+    for n in range(N):
+        tail[n] += BIAS.get(ops[n]["grp"], 0.0)
     left = [len(o["hard"] | o["soft"]) for o in ops]
     at, free, order = [0.0] * N, {q: 0.0 for q in Q}, []
     ready = {n for n in range(N) if not left[n]}
@@ -353,13 +375,13 @@ def rank_program(g, core, T, topo):
         start = {n: max(at[n], free.get(ops[n]["q"], 0.0)) for n in ready}
         t0 = min(start.values())
         q0 = ops[min((n for n in ready), key=lambda n: (start[n], n))]["q"]
-        n = max((n for n in ready if ops[n]["q"] == q0 and start[n] <= t0 + 0.02), key=lambda n: (tail[n], -n))
+        n = max((n for n in ready if ops[n]["q"] == q0 and start[n] <= t0 + WIN[0]), key=lambda n: (tail[n], -n))
         ready.discard(n)
         order.append(n)
         if q0:
             free[q0] = start[n] + ops[n]["cost"]
         for m in succ[n]:
-            at[m] = max(at[m], start[n] + (lat(ops[n]) + WAKE if n in ops[m]["hard"] else 0.0))
+            at[m] = max(at[m], start[n] + (lat(ops[n]) + WAKE[0] if n in ops[m]["hard"] else 0.0))
             left[m] -= 1
             if not left[m]:
                 ready.add(m)

@@ -1,35 +1,38 @@
 from concourse.mybir import AluOpType as ALU, ActivationFunctionType as ACTF, AxisListType as AX
 
 I32, F32, F16, B16, U16 = "int32", "float32", "float16", "bfloat16", "uint16"
-WN = 2050
+WN, W0 = 2056, 4
 FLAG = 8192
 SCRATCH = {}
 for _d, _s, _n in (
-        (I32, [128, 2], "i_p i_b"), (I32, [128, 16], "i_m i_l"), (I32, [128, 64], "pb32 dn dhi dlo dnm dhim dlom"),
-        (I32, [128, 128], "pl32"), (I32, [128, 92], "pf32"),
-        (B16, [128, 1040], "i8"), (B16, [128, 512], "o8"), (B16, [128, 4, 16], "oa e2"), (B16, [128, 2048], "qq"),
+        (I32, [128, 2], "i_p i_b"), (I32, [128, 16], "i_m i_l"), (I32, [128, 64], "pb32"),
+        (I32, [128, 128], "pl32"), (I32, [128, 92], "pf32"), (I32, [128, 2056], "w1"),
+        (B16, [128, 1040], "i8"), (B16, [128, 4, 16], "e2"), (B16, [128, 2048], "qq"), (B16, [128, 120], "cst"),
         (B16, [128, 4, 4, 16], "qa"), (B16, [128, 4, 128], "zo"),
-        (B16, [128, 192], "z0"), (B16, [128, 40], "rn"), (B16, [128, 8, 4, 4], "e24"), (B16, [128, 240], "ee"),
-        (B16, [128, 2064], "w2"), (F32, [128, 2056], "w1"), (F32, [128, 40], "s4"), (F32, [128, 128], "id"),
-        (F32, [128, 120], "rs zsh zsf mnh mnf eqh eqf neh nef pph ppf"), (F32, [128, 40, 3], "soh sof"),
-        (F32, [128, 32], "wq"), (F32, [128, 2], "bm"), (F32, [128, 8], "wr xb wb"), (F32, [128, 64], "d2 dfl dflm"),
+        (B16, [128, 192], "z0"), (B16, [128, 40], "rn ru"), (B16, [128, 8, 4, 4], "e24"), (B16, [128, 240], "ee"),
+        (F32, [128, 2056], "w2"), (F32, [128, 40], "s4"),
+        (F32, [128, 120], "rs mnh mnf eqh eqf neh nef pph ppf"), (F32, [128, 40, 3], "soh sof"),
+        (F32, [128, 32], "wq"), (F32, [128, 2], "bm"), (F32, [128, 8], "wr xb"), (F32, [128, 64], "d2"),
         (F32, [128, 24], "yo"), (F16, [128, 128], "thi nhi"), (F16, [128, 64], "tlo nlo dd ex exm"),
-        (F16, [128, 2, 128], "oh om"), (F16, [128, 92], "lp lpn"), (F16, [128, 24], "llh llf"),
-        (F16, [128, 8, 3], "ina inb inc woh wof weh wef"), (F16, [128, 16, 23], "pth ptf"), (F16, [128, 8, 24], "rmh rmf"),
-        (F16, [128, 9, 16], "tbh tbf"), (F32, [128, 384], "xh xf prh prf"), (B16, [128, 384], "nbh nbf"),
-        (U16, [128, 24], "offh offf"), (F32, [128, 8, 3], "sth stf flh flf dfh dff"), (F32, [128, 4, 32], "trh trf")):
+        (F16, [128, 92], "lp lpn"), (F16, [128, 24], "llh llf"), (F16, [128, 120], "zsh zsf"),
+        (F16, [128, 8, 3], "ina inb inc woh wof weh wef umh umf"), (F16, [128, 16, 23], "pth ptf"), (F16, [128, 8, 24], "rmh rmf"),
+        (F16, [128, 9, 16], "tbh tbf tch tcf"), (F32, [128, 384], "xh xf prh prf"), (F16, [128, 384], "nbh nbf"),
+        (U16, [128, 24], "offh offf"), (F32, [128, 8, 3], "sth stf flh flf suh suf mkh mkf"), (F32, [128, 4, 32], "trh trf")):
     for _k in _n.split():
         SCRATCH[_k] = ("sbuf", _s, _d)
 for _s, _n in (([128, 4, 128], "uh uf nh nf stg0 stg1"), ([128, 16, 32], "lh lf")):
     for _k in _n.split():
         SCRATCH[_k] = ("psum", _s, F32)
-SEMAPHORES = ["sv", "sa", "sp", "sg"] + ["d%d" % k for k in range(15)] + [a + b for a in ("arr", "loc") for b in "TULABC"]
+SEMAPHORES = ["sv", "sa", "sp", "sg"] + ["d%d" % k for k in range(14)] + [a + b for a in ("arr", "loc") for b in "TULABC"]
 CS = {"v": "sv", "a": "sa", "p": "sp", "g": "sg"}
 WAKE = [0.18]
 SHORT = {"v": 0.09, "a": 0.36, "p": 0.096, "g": 0.48, "s": 0.072}
 DMA_T, SEND_T = 2.2, {"T": 2.5, "U": 3.4, "L": 3.2, "A": 2.4, "B": 2.4, "C": 2.4}
-BIAS = {"f0": -4, "f1": -4, "f2": 4, "h0": 6}
-WIN = [0.02]
+BIAS = {"f2": 1.5, "h0": 6, "h2": 1}
+TBA = ["va"]
+ORD = [(2, 0, 1, 3)]
+EARLY, LATE = [4], ["thi"]
+WIN = [0.1]
 
 
 def rank_program(g, core, T, topo):
@@ -40,6 +43,7 @@ def rank_program(g, core, T, topo):
     mate = [r for r in range(len(chips)) if r != rank and chips[r] == chips[rank]][0]
     part = [r for r in range(len(chips)) if chips[r] != chips[rank] and topo.die(T.cores[r]) == topo.die(core)][0]
     low = min(rank, mate)
+    flag = FLAG if low == 0 else -FLAG
     V, S, PE, SY = g.vector, g.scalar, g.tensor, g.sync
     Q = {"v": V, "a": S, "p": PE, "s": SY, "g": g}
 
@@ -115,6 +119,13 @@ def rank_program(g, core, T, topo):
     ld("s", "d2", T.pb32[64:128, :], T.nbr[:, :], w=["pb32n"])
     ld("a", "d1", T.pb32[0:64, :], T.planes[3::4, :], w=["pb32d"])
     ld("s", "d0", T.pl32[:], T.planes[:, :], w=["pl32"])
+    zw, zh = (0, 1) if rank == low else (1, 0)
+
+    def own_planes(k, sem, r, h):
+        ld("s", sem, T.w1[16 * k:16 * k + 16, W0 + 1024 * zw:W0 + 1024 * zw + 1024], T.planes[:, :], r=r, w=["+w1_%d_%d" % (zw, h)])
+
+    for k in range(EARLY[0]):
+        own_planes(k, "d12", [], 0)
     cp(T.lp[0:96, :], T.pf32[0:96, :], r=["pf32p"], w=["lp0"], cost=0.1)
     ts(T.lp[96:128, :], T.pf32[96:128, :], -2047, None, ALU.add, r=["pf32t"], w=["lp1"], cost=0.1)
     send("L", part, T.lpn[:], T.lp[:], ["lp0", "lp1"], "lpn", off_)
@@ -125,32 +136,31 @@ def rank_program(g, core, T, topo):
     send("T", mate, T.nlo[:], T.tlo[:], ["tlo1", "tlo2"], "nlo", on[1::2])
     ts(T.thi[:], T.pl32[:], 0.015625, None, ALU.mult, r=["pl32"], w=["thi"], cost=0.13)
     send("U", mate, T.nhi[:], T.thi[:], ["thi"], "nhi", on[::2])
-    for ap, c, key in ((T.i8[:, 0:128], 0, "i8a"), (T.i8[:, 1024:1040], 0, "i8p"), (T.qa[0:64], 0, "qa"), (T.oa[0:80], 0, "oa"),
-                       (T.zo[0:64], 0, "zo"), (T.zsh[:], 0, "zsh"), (T.zsf[:], 0, "zsf"), (T.z0[:], 0, "z0"),
-                       (T.s4[:], 256, "s4"), (T.rn[:], 0, "rn"), (T.e2[:], 0, "e2"), (T.e24[0:32], 0, "e24"), (T.ee[:], 0, "ee"),
-                       (T.rs[:], -1e9, "rs"), (T.rs[:, 0:120:5], 0, "rs"), (T.id[:], 0, "id"),
+    for k in range(EARLY[0], 8):
+        own_planes(k, "d13", LATE, 1)
+    for ap, c, key in ((T.i8[:, 0:128], 0, "i8a"), (T.i8[:, 1024:1040], 0, "i8p"), (T.qa[0:64], 0, "qa"), (T.cst[:], 0, "cst"),
+                       (T.cst[:, 0:120:5], -0.5, "cst"), (T.zo[0:64], 0, "zo"), (T.z0[:], 0, "z0"),
+                       (T.s4[:], 1, "s4"), (T.ru[:], 0, "ru"), (T.e2[:], 0, "e2"), (T.e24[0:32], 0, "e24"), (T.ee[:], 0, "ee"),
+                       (T.rs[:], -1e9, "rs"), (T.rs[:, 0:120:5], 0, "rs"), (T.zsh[:], 0, "zsh"), (T.zsf[:], 0, "zsf"),
                        (T.xh[:, 368:384], 0, "xhp"), (T.xf[:, 368:384], 0, "xfp"), (T.offh[:, 23:24], 0, "offh2"), (T.offf[:, 23:24], 0, "offf2")):
         ms(ap, c, w=[key], cost=0.12)
     add("g", lambda: g.iota(T.i_p[:], [[0, 2]], 0, 1), (), ["i_p"], 0.2)
     sel("i8a", T.i8[:, 0:128], [[-1, 128]], ALU.not_equal, 1.0, 0, 1, 0.42)
-    sel("oa", T.oa[0:80], [[-16, 4], [-1, 16]], ALU.not_equal, 1.0, 0, 1, 0.28)
-    sel("oa", T.oa[0:80, :, 12:16], [[-4, 4], [-1, 4]], ALU.not_equal, 1.0, -64, 1, 0.2)
     sel("qa", T.qa[0:64, :, 3, :], [[-16, 4], [-1, 16]], ALU.not_equal, 1.0, 0, 1, 0.3)
     add("g", lambda: g.iota(T.wq[:], [[0, 8], [1, 4]], 1, 0, allow_small_or_imprecise_dtypes=True), (), ["wq"], 0.25)
     sel("wq", T.wq[:], [[-16, 8], [-4, 4]], ALU.is_equal, 0.0, -3, 1)
     add("g", lambda: g.iota(T.i_m[:], [[-1, 16]], 256, 1), (), ["i_m"], 0.2)
     sel("e24", T.e24[0:32, :, :, 0:3], [[-3, 8], [0, 4], [-1, 3]], ALU.not_equal, 1.0, 0, 1, 0.35)
-    sel("s4", T.s4[:], [[-16, 8], [-4, 5]], ALU.is_ge, 0.0, 4, 1)
-    sel("s4", T.s4[:], [[16, 8], [4, 5]], ALU.is_ge, 0.0, -1, -1)
+    sel("s4", T.s4[:], [[-16, 8], [4, 5]], ALU.is_ge, 0.0, -16, 1)
+    sel("s4", T.s4[:], [[16, 8], [-4, 5]], ALU.is_ge, 0.0, 19, -1)
     ms(T.s4[:, 0:40:5], 0, w=["s4"])
-    sel("rn", T.rn[:], [[-16, 8], [-2, 5]], ALU.not_equal, 1.0, 2, 1)
-    sel("rn", T.rn[:], [[-16, 8], [-2, 5]], ALU.not_equal, 64.0, -6, 1)
+    sel("ru", T.ru[:], [[-16, 8], [2, 5]], ALU.not_equal, 1.0, -16, 1)
+    ms(T.ru[:, 0:40:5], 0, w=["ru"])
+    add("g", lambda: g.affine_select(T.rn[:], T.ru[:], [[-16, 8], [2, 5]], ALU.not_equal, 1.0, -8, 1), ["ru"], ["rn"], 0.25)
     ms(T.rn[:, 0:40:5], 0, w=["rn"])
-    sel("id", T.id[:], [[-1, 128]], ALU.not_equal, 1.0, 0, 1, 0.42)
     sel("e2", T.e2[:], [[-32, 4], [-1, 16]], ALU.not_equal, 1.0, 0, 1, 0.3)
     sel("e2", T.e2[:], [[-32, 4], [-1, 16]], ALU.not_equal, 1.0, -16, 1, 0.3)
     for k in range(8):
-        cp(T.o8[0:80, 64 * k:64 * k + 64], T.oa[0:80], r=["oa"], w=["+o8"])
         if k:
             cp(T.i8[:, 128 * k:128 * k + 128], T.i8[:, 0:128], r=["i8a"], w=["+i8"])
         if k in (2, 4, 6):
@@ -159,7 +169,6 @@ def rank_program(g, core, T, topo):
             act(T.qq[0:64, 256 * k:256 * k + 256], T.qa[0:64], r=["qa"], w=["+qq"], cost=0.3)
     add("v", lambda: V.tensor_reduce(T.wr[:, 0:1], T.wq[:], AX.X, ALU.add), ["wq"], ["wr"])
     ts(T.xb[:, 0:1], T.wr[:, 0:1], 1, None, ALU.min, r=["wr"], w=["xb"])
-    ts(T.wb[:, 0:1], T.wr[:, 0:1], 0.00390625, None, ALU.mult, r=["wr"], w=["wb"])
     ts(T.i_l[:], T.i_m[:], 15, None, ALU.bitwise_and, r=["i_m"], w=["i_l"])
     ts(T.ee[:, 112:128], T.i_l[:], 0, None, ALU.is_equal, r=["i_l"], w=["ee"])
     ts(T.i_b[:], T.i_p[:], 16, None, ALU.bitwise_and, r=["i_p"], w=["i_b"])
@@ -167,51 +176,35 @@ def rank_program(g, core, T, topo):
         ts(T.bm[:, bl:bl + 1], T.i_b[:, bl:bl + 1], 16 * bl, None, ALU.is_equal, r=["i_b"], w=["+bm"])
     for s in "hf":
         cp(T["tb" + s][:], T.z0[:, 0:144], r=["z0"], w=["tb" + s], cost=0.08)
+        cp(T["tc" + s][:], T.z0[:, 0:144], r=["z0"], w=["tc" + s], cost=0.08)
         cp(T["rm" + s][:], T.z0[:], r=["z0"], w=["rm" + s], cost=0.09)
-    cp(T.om[0:64], T.zo[0:64, 0:2, :], r=["zo"], w=["om"], cost=0.13)
-    for c in (0, WN - 1):
-        cp(T.w1[:, c:c + 1], T.xb[:, 0:1], r=["xb"], w=["+w1_d"])
-        ms(T.w2[:, c:c + 1], 0, w=["+w2_d"])
+    for c in (0, WN - 4):
+        ms(T.w1[:, c:c + 4], 0, w=["+w1_d"])
+        ms(T.w2[:, c:c + 4], 0, w=["+w2_d"])
     ld("s", "d6", T.pth[0:24], T.lp[0:96, :], r=["lp0"], w=["pth"])
     spread("h", ("d7", "d10"), T.lp, "lp1")
 
-    def first_list(s):
-        off, v, ks = T["off" + s], T["ll" + s][:, 0:23], ["+off%s%d" % (s, r) for r in range(3)]
+    def offsets(out, v, r, w):
         if low == 0:
-            ts(off[:, 0:23], v, 1, 2048, ALU.min, ALU.add, r=["ll" + s], w=ks)
+            ts(out, v, 1, W0 + 2047, ALU.min, ALU.add, r=r, w=w)
         else:
-            ts(off[:, 0:23], v, 0, None, ALU.max, r=["ll" + s], w=ks)
+            ts(out, v, 1 - W0, W0 - 1, ALU.max, ALU.add, r=r, w=w)
 
-    def copy_out(q, dst, src, bias, r, w):
-        if q == "a":
-            act(dst, src, r, w, bias=0.0 if bias is None else bias, cost=0.55)
-        elif bias is None:
-            cp(dst, src, r, w, cost=0.5)
-        else:
-            ts(dst, src, bias, None, ALU.add, r=r, w=w, cost=0.5)
+    def first_list(s):
+        offsets(T["off" + s][:, 0:23], T["ll" + s][:, 0:23], ["ll" + s], ["+off%s%d" % (s, r) for r in range(3)])
 
     def move_values(lo, key, q, m):
-        P = slice(64, 128)
-        dn, fl, hi, lw, ex = (T[k + m] for k in ("dn", "dfl", "dhi", "dlo", "ex"))
-        ts(dn[P, :], lo[P, :], -1, None, ALU.add, r=[key], w=["dn" + m])
-        ts(fl[P, :], dn[P, :], 1024 * (low + 1) - 2048, FLAG // 64, ALU.is_ge if q == low else ALU.is_lt, ALU.mult, r=["dn" + m], w=["fl_" + m])
-        ts(hi[P, :], dn[P, :], 6, None, ALU.arith_shift_right, r=["dn" + m], w=["hi" + m])
-        ts(lw[P, :], dn[P, :], 63, None, ALU.bitwise_and, r=["dn" + m], w=["lo" + m])
-        tt(ex[P, :], hi[P, :], fl[P, :], ALU.add, r=["hi" + m, "fl_" + m], w=["+ex" + m], cost=0.13)
-        ts(ex[0:64, :], lw[P, :], 1, None, ALU.add, r=["lo" + m], w=["+ex" + m])
+        ex = T["ex" + m]
+        ts(ex[0:64, :], lo[64:128, :], 1024 * (low + 1) - 2047, flag, ALU.is_ge if q == low else ALU.is_lt, ALU.mult, r=[key], w=["+ex" + m])
+        cp(ex[64:128, :], lo[64:128, :], r=[key], w=["+ex" + m])
 
-    def own_table(z):
-        for k, (src, K, key, banks) in enumerate(((T.oh, 80, "oh", ("stg0", "stg1")), (T.om, 64, "om", ("nh", "nf")))):
-            for h in range(2):
-                b = banks[h]
-                for c in (2 * h, 2 * h + 1):
-                    mm(T[b][:, 2 * (c % 2):2 * (c % 2) + 2, :], T.o8[0:K, c:c + 509:4], src[0:K], True, True,
-                       r=["o8", key], w=["+" + b, "+pe"], cost=0.23)
-                c0 = 1 + 1024 * z + 512 * h
-                if k:
-                    copy_out("av"[h], T.w2[:, c0:c0 + 512], T[b][:], None, [b], ["w2_%d_%d" % (z, h)])
-                else:
-                    copy_out("av"[h], T.w1[:, c0:c0 + 512], T[b][:], T.wb[:, 0:1], [b, "wb"], ["w1_%d_%d" % (z, h)])
+    def move(z, h, ex):
+        b, c0 = "stg%d" % h, W0 + 1024 * z + 512 * h
+        for tb in range(8):
+            x = 64 * (tb % 2)
+            mm(T[b][:, tb // 2, x:x + 64], T.i8[:, 8 * h + tb:8 * h + tb + 1017:8], T[ex][:], True, True,
+               r=["i8", "i8a", "i8p", ex], w=["+" + b, "+pe"])
+        act(T.w2[:, c0:c0 + 512], T[b][:], r=[b], w=["w2_%d_%d" % (z, h)], cost=0.55)
 
     def mate_table(z):
         def small(h):
@@ -222,46 +215,42 @@ def rank_program(g, core, T, topo):
                    r=["qq", "nlo"], w=["+" + b, "+pe"])
 
         def large(h):
-            b, c0 = ("uh", "uf")[h], 1 + 1024 * z + 512 * h
+            b, c0 = ("uh", "uf")[h], W0 + 1024 * z + 512 * h
             for cb in range(4):
                 mm(T[b][:, cb, :], T.i8[:, 4 * h + cb:4 * h + cb + 1017:8], T.nhi[:], False, cb == 3, r=["i8", "i8a", "nhi"], w=["+" + b, "+pe"], cost=0.13)
-            copy_out("v", T.w1[:, c0:c0 + 512], T[b][:], T.wb[:, 0:1], [b, "wb"], ["w1_%d_%d" % (z, h)])
-
-        def move(h):
-            b, c0 = "stg%d" % h, 1 + 1024 * z + 512 * h
-            for tb in range(8):
-                x = 64 * (tb % 2)
-                mm(T[b][:, tb // 2, x:x + 64], T.i8[:, 8 * h + tb:8 * h + tb + 1017:8], T.exm[:], True, True,
-                   r=["i8", "i8a", "i8p", "exm"], w=["+" + b, "+pe"])
-            copy_out("a", T.w2[:, c0:c0 + 512], T[b][:], None, [b], ["w2_%d_%d" % (z, h)])
+            ts(T.w1[:, c0:c0 + 512], T[b][:], 64, None, ALU.mult, r=[b], w=["w1_%d_%d" % (z, h)], cost=0.5)
 
         for b in ("uh", "uf"):
             mm(T[b][:], T.zo[0:64, 0, :], T.zo[0:64], True, False, r=["zo"], w=["+" + b], cost=0.45)
         small(0)
         small(1)
-        move(0)
-        large(0)
-        large(1)
-        move(1)
+        for o in ORD[0]:
+            if o < 2:
+                large(o)
+            else:
+                move(z, o - 2, "exm")
 
     def expand_points(s):
         b, x = T["l" + s][:, :, 0:23], T["x" + s]
         mm(b, T.e24[0:24], T["pt" + s][0:24], True, True, r=["e24", "pt" + s], w=["+l" + s], cost=0.37)
         ts(x[:, 0:368], b, T.xb[:, 0:1], None, ALU.add, r=["l" + s, "xb"], w=["x" + s], cost=0.37)
 
+    def on_chip(s, v, key):
+        if low == 0:
+            ts(T["mk" + s][:], v, FLAG, FLAG, ALU.mult, ALU.min, r=[key], w=["mk" + s])
+            tt(T["st" + s][:], v, T["mk" + s][:], ALU.max, r=[key, "mk" + s], w=["st" + s])
+        else:
+            ts(T["st" + s][:], v, 0, None, ALU.max, r=[key], w=["st" + s])
+
     def to_points(s):
         rm, l = T["rm" + s], T["l" + s]
         for b in range(8):
             mm(l[:, 0:8, 0:3], T.ee[:, 112 - 16 * b:240 - 16 * b], rm[:, :, b::8], b == 0, b == 7, r=["ee", "rm" + s], w=["+l" + s])
-        cp(T["st" + s][:], l[:, 0:8, 0:3], r=["l" + s], w=["st" + s])
+        on_chip(s, l[:, 0:8, 0:3], "l" + s)
 
-    zw, zh = (0, 1) if rank == low else (1, 0)
     move_values(T.tlo, "tlo2", rank, "")
-    ld("s", "d12", T.oh[0:64], T.thi[:], r=["thi"], w=["+oh"])
-    ld("s", "d13", T.oh[64:80], T.tlo[0:64, :], r=["tlo1"], w=["+oh"])
-    for k in range(8):
-        ld("s", "d14", T.om[8 * k:8 * k + 4], T.ex[16 * k:16 * k + 16, :], r=["ex"], w=["+om"])
-    own_table(zw)
+    for h in range(2):
+        move(zw, h, "ex")
     expand_points("h")
     first_list("h")
     grp[0] = "h0"
@@ -278,23 +267,24 @@ def rank_program(g, core, T, topo):
 
     halves = ["_d"] + ["_%d_%d" % (z, h) for z in range(2) for h in range(2)]
 
-    def gather(s, state, key):
+    def gather(s, state, key, rn):
         off, ks = T["off" + s], ["off%s%d" % (s, r) for r in range(3)]
 
         def third(r):
             c = slice(128 * r, 128 * r + 128)
             add("v", lambda: V.tensor_tensor(T["pr" + s][:, c], T.w1[:, 0:WN].indirect(off[:, 8 * r:8 * r + 8]), T["x" + s][:, c], ALU.mult),
                 ["w1" + k for k in halves] + [ks[r], "x" + s, "x%sp" % s], ["pr%s%d" % (s, r)], cost=0.25)
-            mm(T["u" + s][:, 0, 40 * r:40 * r + 40], T["pr" + s][:, c], T.s4[:], True, True, r=["pr%s%d" % (s, r), "s4"], w=["+u" + s], cost=0.22)
+            mm(T["u" + s][:, 0, 40 * r:40 * r + 40], T["pr" + s][:, c], T.s4[:], False, r == 2, r=["pr%s%d" % (s, r), "s4"], w=["+u" + s], cost=0.22)
 
+        mm(T["u" + s][:, 0, 0:120], T.i8[:, 0:128], T.cst[:], True, False, r=["i8a", "cst"], w=["+u" + s], cost=0.13)
         for r in range(3):
             third(r)
         act(T["nb" + s][:], T.w2[:, 0:WN].indirect(off[:, 0:24]), ["w2" + k for k in halves] + ks, ["nb" + s], cost=0.65)
         for r in range(3):
             act(T["zs" + s][:, 40 * r:40 * r + 40:5], state[r], r=[key], w=["+zs" + s], cost=0.1)
-        mm(T["n" + s][:, 0, 0:120], T.id[:], T["zs" + s][:], True, False, r=["id", "zs" + s], w=["+n" + s], cost=0.4)
+        mm(T["n" + s][:, 0, 0:120], T.i8[:, 0:128], T["zs" + s][:], True, False, r=["i8a", "zs" + s], w=["+n" + s], cost=0.13)
         for r in range(3):
-            mm(T["n" + s][:, 0, 40 * r:40 * r + 40], T["nb" + s][:, 128 * r:128 * r + 128], T.rn[:], False, r == 2, r=["nb" + s, "rn"], w=["+n" + s])
+            mm(T["n" + s][:, 0, 40 * r:40 * r + 40], T["nb" + s][:, 128 * r:128 * r + 128], T[rn][:], False, r == 2, r=["nb" + s, rn], w=["+n" + s])
 
     def choose(s):
         u, n = T["u" + s][:, 0, 0:120], T["n" + s][:, 0, 0:120]
@@ -307,51 +297,68 @@ def rank_program(g, core, T, topo):
             c = slice(40 * r, 40 * r + 40)
             scan(so[:, :, r], ne[:, c], pp[:, c], ALU.mult, ALU.add, r=["ne" + s, "pp" + s], w=["+so" + s])
 
-    def to_list(s, src, key, last=False):
-        tb, l, tr = T["tb" + s], T["l" + s], T["tr" + s]
+    def to_tb(s, tb, src, key):
         for bl in range(2):
-            ts(tb[:, 0:8, bl:6:2], src, T.bm[:, bl:bl + 1], None, ALU.mult, r=[key, "bm"], w=["+tb" + s])
+            out, k = T[tb + s][:, 0:8, bl:6:2], T.bm[:, bl:bl + 1]
+            if TBA[0][bl] == "v":
+                ts(out, src, k, None, ALU.mult, r=[key, "bm"], w=["+" + tb + s])
+            else:
+                add("a", lambda out=out, k=k: S.activation(out, src, ACTF.Identity, scale=k), [key, "bm"], ["+" + tb + s], 0.12)
+
+    def turn(s, tb, first, last):
         for par in range(2):
-            mm(l[:, 0:4, 16 * par:16 * par + 16], tb[:, par:par + 8, :], T.e2[:], True, True, r=["tb" + s, "e2"], w=["+l" + s])
+            mm(T["l" + s][:, 0:4, 16 * par:16 * par + 16], T[tb + s][:, par:par + 8, :], T.e2[:], first, last and (first or par == 1),
+               r=[tb + s, "e2"], w=["+l" + s])
+
+    def from_list(s, last=False):
+        l, tr = T["l" + s], T["tr" + s]
         add("v", lambda: V.transpose(tr[:], l[:, 0:4, :]), ["l" + s], ["tr" + s], cost=0.13)
         for r in range(3):
             v, c, k = tr[:, :, 2 * r:2 * r + 2], slice(8 * r, 8 * r + 8), ["off%s%d" % (s, r)]
             if last:
                 ts(T.yo[:, c], v, 2047, None, ALU.add, r=["tr" + s], w=["+yo"])
-            elif low == 0:
-                ts(T["off" + s][:, c], v, 1, 2048, ALU.min, ALU.add, r=["tr" + s], w=k)
             else:
-                ts(T["off" + s][:, c], v, 2049, 0, ALU.min, ALU.max, r=["tr" + s], w=k)
+                offsets(T["off" + s][:, c], v, ["tr" + s], k)
 
     def rounds(s, wo, name, landing):
-        so, st, fl, w = T["so" + s], T["st" + s], T["fl" + s], T[wo + s]
+        so, st, fl, um, w = T["so" + s], T["st" + s], T["fl" + s], T["um" + s], T[wo + s]
         v = so[:, 4::5, :]
-        gather(s, [st[:, :, r] for r in range(3)], "st" + s)
+        gather(s, [st[:, :, r] for r in range(3)], "st" + s, "rn")
         choose(s)
-        to_list(s, v, "so" + s)
-        gather(s, [so[:, 4::5, r] for r in range(3)], "so" + s)
+        to_tb(s, "tb", v, "so" + s)
+        turn(s, "tb", True, True)
+        from_list(s)
+        ts(fl[:], v, 3000 if flag > 0 else -3000, -flag, ALU.is_ge if flag > 0 else ALU.is_le, ALU.mult, r=["so" + s], w=["fl" + s])
+        tt(um[:], v, fl[:], ALU.add, r=["so" + s, "fl" + s], w=["um" + s])
+        gather(s, [um[:, :, r] for r in range(3)], "um" + s, "ru")
         choose(s)
-        ts(fl[:], v, 3000, -FLAG, ALU.is_ge, ALU.mult, r=["so" + s], w=["fl" + s])
-        tt(w[:], v, fl[:], ALU.add, r=["so" + s, "fl" + s], w=[wo + s])
+        cp(w[:], v, r=["so" + s], w=[wo + s])
         if name:
             send(name, part, T[landing][:], w[:], [wo + s], landing, off_)
-        tt(T["df" + s][:], w[:], st[:], ALU.subtract, r=[wo + s, "st" + s], w=["df" + s])
+        if name != "C":
+            mm(T["l" + s][:, 0:4, :], T.zo[0:64, 0, :], T.zo[0:64, :, 0:32], True, False, r=["zo"], w=["+l" + s], cost=0.15)
+            to_tb(s, "tb", w[:], wo + s)
+            turn(s, "tb", False, False)
 
-    def merge(s, inn, last=False):
-        tt(T["st" + s][:], T["df" + s][:], T[inn][:], ALU.add, r=["df" + s, inn], w=["st" + s])
-        to_list(s, T["st" + s][:], "st" + s, last)
+    def merge(s, wo, inn, last=False):
+        to_tb(s, "tc", T[inn][:], inn)
+        turn(s, "tc", False, True)
+        from_list(s, last)
+        if not last:
+            tt(T["su" + s][:], T[wo + s][:], T[inn][:], ALU.add, r=[wo + s, inn], w=["su" + s])
+            on_chip(s, T["su" + s][:], "su" + s)
 
     grp[0] = "h1"
     rounds("h", "wo", "A", "ina")
     grp[0] = "f1"
     rounds("f", "wo", "B", "inb")
     grp[0] = "f2"
-    merge("f", "ina")
+    merge("f", "wo", "ina")
     rounds("f", "we", "C", "inc")
     grp[0] = "h2"
-    merge("h", "inb")
+    merge("h", "wo", "inb")
     rounds("h", "we", None, None)
-    merge("h", "inc", last=True)
+    merge("h", "we", "inc", last=True)
     ld("s", "d5", T.y[:, :], T.yo[:, 0:23], r=["yo"])
 
     N = len(ops)

from concourse.mybir import AluOpType as ALU, ActivationFunctionType as ACTF, AxisListType as AX

I32, F32, F16, B16, U16 = "int32", "float32", "float16", "bfloat16", "uint16"
WN, W0 = 2056, 4
FLAG = 8192
SCRATCH = {}
for _d, _s, _n in (
        (I32, [128, 2], "i_p i_b"), (I32, [128, 16], "i_m i_l"), (I32, [128, 64], "pb32"),
        (I32, [128, 128], "pl32"), (I32, [128, 92], "pf32"), (I32, [128, 2056], "w1"),
        (B16, [128, 1040], "i8"), (B16, [128, 4, 16], "e2"), (B16, [128, 2048], "qq"), (B16, [128, 120], "cst"),
        (B16, [128, 4, 4, 16], "qa"), (B16, [128, 4, 128], "zo"),
        (B16, [128, 192], "z0"), (B16, [128, 40], "rn ru"), (B16, [128, 8, 4, 4], "e24"), (B16, [128, 240], "ee"),
        (F32, [128, 2056], "w2"), (F32, [128, 40], "s4"),
        (F32, [128, 120], "rs mnh mnf eqh eqf neh nef pph ppf"), (F32, [128, 40, 3], "soh sof"),
        (F32, [128, 32], "wq"), (F32, [128, 2], "bm"), (F32, [128, 8], "wr xb"), (F32, [128, 64], "d2"),
        (F32, [128, 24], "yo"), (F16, [128, 128], "thi nhi"), (F16, [128, 64], "tlo nlo dd ex exm"),
        (F16, [128, 92], "lp lpn"), (F16, [128, 24], "llh llf"), (F16, [128, 120], "zsh zsf"),
        (F16, [128, 8, 3], "ina inb inc woh wof weh wef umh umf"), (F16, [128, 16, 23], "pth ptf"), (F16, [128, 8, 24], "rmh rmf"),
        (F16, [128, 9, 16], "tbh tbf tch tcf"), (F32, [128, 384], "xh xf prh prf"), (F16, [128, 384], "nbh nbf"),
        (U16, [128, 24], "offh offf"), (F32, [128, 8, 3], "sth stf flh flf suh suf mkh mkf"), (F32, [128, 4, 32], "trh trf")):
    for _k in _n.split():
        SCRATCH[_k] = ("sbuf", _s, _d)
for _s, _n in (([128, 4, 128], "uh uf nh nf stg0 stg1"), ([128, 16, 32], "lh lf")):
    for _k in _n.split():
        SCRATCH[_k] = ("psum", _s, F32)
SEMAPHORES = ["sv", "sa", "sp", "sg"] + ["d%d" % k for k in range(14)] + [a + b for a in ("arr", "loc") for b in "TULABC"]
CS = {"v": "sv", "a": "sa", "p": "sp", "g": "sg"}
WAKE = [0.18]
SHORT = {"v": 0.09, "a": 0.36, "p": 0.096, "g": 0.48, "s": 0.072}
DMA_T, SEND_T = 2.2, {"T": 2.5, "U": 3.4, "L": 3.2, "A": 2.4, "B": 2.4, "C": 2.4}
BIAS = {"f2": 1.5, "h0": 6, "h2": 1}
TBA = ["va"]
ORD = [(2, 0, 1, 3)]
EARLY, LATE = [4], ["thi"]
WIN = [0.1]


def rank_program(g, core, T, topo):
    rank = T.rank_of(core)
    if rank is None:
        return
    chips = [topo.chip(c) for c in T.cores]
    mate = [r for r in range(len(chips)) if r != rank and chips[r] == chips[rank]][0]
    part = [r for r in range(len(chips)) if chips[r] != chips[rank] and topo.die(T.cores[r]) == topo.die(core)][0]
    low = min(rank, mate)
    flag = FLAG if low == 0 else -FLAG
    V, S, PE, SY = g.vector, g.scalar, g.tensor, g.sync
    Q = {"v": V, "a": S, "p": PE, "s": SY, "g": g}

    ops, base, app, rd, grp = [], {}, {}, {}, [""]

    def add(q, fn, r=(), w=(), cost=None, dma=None, send=None, arr=None):
        n = len(ops)
        hard, soft = set(), set()
        for k in r:
            hard |= set(base.get(k, [])) | set(app.get(k, []))
        for k in w:
            k0 = k.lstrip("+")
            if k0 != k:
                if rd.get(k0):
                    base[k0], app[k0] = list(rd[k0]), []
                    rd[k0] = []
                hard |= set(base.get(k0, []))
                if q in "pg":
                    soft |= set(app.get(k0, [])[-1:])
                app.setdefault(k0, []).append(n)
            else:
                hard |= set(base.get(k0, [])) | set(app.get(k0, [])) | set(rd.get(k0, []))
                base[k0], app[k0], rd[k0] = [n], [], []
        for k in r:
            rd.setdefault(k, []).append(n)
        ops.append(dict(q=q, fn=fn, hard=hard - {n}, soft=soft, cost=SHORT[q] if cost is None else cost, dma=dma, send=send, arr=arr,
                        grp=grp[0]))

    def ts(out, i, s1, s2, o0, *o1, r=(), w=(), cost=None):
        add("v", lambda: V.tensor_scalar(out, i, s1, s2, o0, *o1), r, w, cost)

    def tt(out, a, b, op, r=(), w=(), cost=None):
        add("v", lambda: V.tensor_tensor(out, a, b, op), r, w, cost)

    def scan(out, a, b, o0, o1, r=(), w=(), cost=None):
        add("v", lambda: V.tensor_tensor_scan(out, a, b, 0.0, o0, o1), r, w, cost)

    def cp(out, i, r=(), w=(), cost=None):
        add("v", lambda: V.tensor_copy(out, i), r, w, cost)

    def ms(out, c, w=(), cost=None):
        add("v", lambda: V.memset(out, c), (), w, cost)

    def act(out, i, r=(), w=(), bias=0.0, cost=None):
        add("a", lambda: S.activation(out, i, ACTF.Identity, bias=bias), r, w, cost)

    def mm(out, l, rhs, a, b, r=(), w=(), cost=None):
        add("p", lambda: PE.matmul(out, l, rhs, a, b), r, w, cost)

    def ld(q, sem, out, i, r=(), w=()):
        add(q, lambda: Q[q].dma_start(out, i), r, w, dma=sem)

    def sel(key, ap, pat, op, fill, first, cm, cost=0.25):
        add("g", lambda: g.affine_select(ap, ap, pat, op, fill, first, cm), [key], [key], cost)

    def send(name, dst_rank, out, src, keys, landing, engines):
        rid, pid, _ = topo.addr(T.cores[dst_rank])
        add("g", lambda: g.remote_dma(out, src, T.sem["arr" + name], T.sem["loc" + name], pid, rid, sum(1 << e for e in engines)),
            keys, w=["+order"] if name in "LTU" else (), cost=1.6 if name == "L" else 0.6, send=(name, len(engines)))
        ops.append(dict(q=None, fn=None, hard={len(ops) - 1}, soft=set(), cost=0.0, dma=None, send=None, arr=(name, len(engines)), grp=""))
        base[landing] = [len(ops) - 1]

    on = topo.engines(core, T.cores[mate])
    off_ = topo.engines(core, T.cores[part])

    def spread(s, sem, src, key):
        ld("s", sem[0], T["ll" + s][:, 0:23], src[96:128, :], r=[key], w=["ll" + s])
        for k in range(8):
            ld("s", sem[1], T["rm" + s][16 * k:16 * k + 16, k, 0:23], src[96 + 4 * k:100 + 4 * k, :], r=[key], w=["+rm" + s])

    ld("s", "d3", T.pf32[0:96, :], T.pts[:, :], w=["pf32p"])
    ld("a", "d4", T.pf32[96:128, :], T.tet0[:, :], w=["pf32t"])
    ld("s", "d2", T.pb32[64:128, :], T.nbr[:, :], w=["pb32n"])
    ld("a", "d1", T.pb32[0:64, :], T.planes[3::4, :], w=["pb32d"])
    ld("s", "d0", T.pl32[:], T.planes[:, :], w=["pl32"])
    zw, zh = (0, 1) if rank == low else (1, 0)

    def own_planes(k, sem, r, h):
        ld("s", sem, T.w1[16 * k:16 * k + 16, W0 + 1024 * zw:W0 + 1024 * zw + 1024], T.planes[:, :], r=r, w=["+w1_%d_%d" % (zw, h)])

    for k in range(EARLY[0]):
        own_planes(k, "d12", [], 0)
    cp(T.lp[0:96, :], T.pf32[0:96, :], r=["pf32p"], w=["lp0"], cost=0.1)
    ts(T.lp[96:128, :], T.pf32[96:128, :], -2047, None, ALU.add, r=["pf32t"], w=["lp1"], cost=0.1)
    send("L", part, T.lpn[:], T.lp[:], ["lp0", "lp1"], "lpn", off_)
    ts(T.dd[0:64, :], T.pb32[0:64, :], 0.015625, None, ALU.mult, r=["pb32d"], w=["dd"])
    ts(T.d2[0:64, :], T.pb32[0:64, :], 0.015625, None, ALU.mult, r=["pb32d"], w=["d2"])
    ts(T.tlo[64:128, :], T.pb32[64:128, :], -2047, None, ALU.add, r=["pb32n"], w=["tlo2"])
    tt(T.tlo[0:64, :], T.d2[0:64, :], T.dd[0:64, :], ALU.subtract, r=["d2", "dd"], w=["tlo1"], cost=0.13)
    send("T", mate, T.nlo[:], T.tlo[:], ["tlo1", "tlo2"], "nlo", on[1::2])
    ts(T.thi[:], T.pl32[:], 0.015625, None, ALU.mult, r=["pl32"], w=["thi"], cost=0.13)
    send("U", mate, T.nhi[:], T.thi[:], ["thi"], "nhi", on[::2])
    for k in range(EARLY[0], 8):
        own_planes(k, "d13", LATE, 1)
    for ap, c, key in ((T.i8[:, 0:128], 0, "i8a"), (T.i8[:, 1024:1040], 0, "i8p"), (T.qa[0:64], 0, "qa"), (T.cst[:], 0, "cst"),
                       (T.cst[:, 0:120:5], -0.5, "cst"), (T.zo[0:64], 0, "zo"), (T.z0[:], 0, "z0"),
                       (T.s4[:], 1, "s4"), (T.ru[:], 0, "ru"), (T.e2[:], 0, "e2"), (T.e24[0:32], 0, "e24"), (T.ee[:], 0, "ee"),
                       (T.rs[:], -1e9, "rs"), (T.rs[:, 0:120:5], 0, "rs"), (T.zsh[:], 0, "zsh"), (T.zsf[:], 0, "zsf"),
                       (T.xh[:, 368:384], 0, "xhp"), (T.xf[:, 368:384], 0, "xfp"), (T.offh[:, 23:24], 0, "offh2"), (T.offf[:, 23:24], 0, "offf2")):
        ms(ap, c, w=[key], cost=0.12)
    add("g", lambda: g.iota(T.i_p[:], [[0, 2]], 0, 1), (), ["i_p"], 0.2)
    sel("i8a", T.i8[:, 0:128], [[-1, 128]], ALU.not_equal, 1.0, 0, 1, 0.42)
    sel("qa", T.qa[0:64, :, 3, :], [[-16, 4], [-1, 16]], ALU.not_equal, 1.0, 0, 1, 0.3)
    add("g", lambda: g.iota(T.wq[:], [[0, 8], [1, 4]], 1, 0, allow_small_or_imprecise_dtypes=True), (), ["wq"], 0.25)
    sel("wq", T.wq[:], [[-16, 8], [-4, 4]], ALU.is_equal, 0.0, -3, 1)
    add("g", lambda: g.iota(T.i_m[:], [[-1, 16]], 256, 1), (), ["i_m"], 0.2)
    sel("e24", T.e24[0:32, :, :, 0:3], [[-3, 8], [0, 4], [-1, 3]], ALU.not_equal, 1.0, 0, 1, 0.35)
    sel("s4", T.s4[:], [[-16, 8], [4, 5]], ALU.is_ge, 0.0, -16, 1)
    sel("s4", T.s4[:], [[16, 8], [-4, 5]], ALU.is_ge, 0.0, 19, -1)
    ms(T.s4[:, 0:40:5], 0, w=["s4"])
    sel("ru", T.ru[:], [[-16, 8], [2, 5]], ALU.not_equal, 1.0, -16, 1)
    ms(T.ru[:, 0:40:5], 0, w=["ru"])
    add("g", lambda: g.affine_select(T.rn[:], T.ru[:], [[-16, 8], [2, 5]], ALU.not_equal, 1.0, -8, 1), ["ru"], ["rn"], 0.25)
    ms(T.rn[:, 0:40:5], 0, w=["rn"])
    sel("e2", T.e2[:], [[-32, 4], [-1, 16]], ALU.not_equal, 1.0, 0, 1, 0.3)
    sel("e2", T.e2[:], [[-32, 4], [-1, 16]], ALU.not_equal, 1.0, -16, 1, 0.3)
    for k in range(8):
        if k:
            cp(T.i8[:, 128 * k:128 * k + 128], T.i8[:, 0:128], r=["i8a"], w=["+i8"])
        if k in (2, 4, 6):
            cp(T.qq[0:64, 256 * k:256 * k + 256], T.qa[0:64], r=["qa"], w=["+qq"], cost=0.12)
        else:
            act(T.qq[0:64, 256 * k:256 * k + 256], T.qa[0:64], r=["qa"], w=["+qq"], cost=0.3)
    add("v", lambda: V.tensor_reduce(T.wr[:, 0:1], T.wq[:], AX.X, ALU.add), ["wq"], ["wr"])
    ts(T.xb[:, 0:1], T.wr[:, 0:1], 1, None, ALU.min, r=["wr"], w=["xb"])
    ts(T.i_l[:], T.i_m[:], 15, None, ALU.bitwise_and, r=["i_m"], w=["i_l"])
    ts(T.ee[:, 112:128], T.i_l[:], 0, None, ALU.is_equal, r=["i_l"], w=["ee"])
    ts(T.i_b[:], T.i_p[:], 16, None, ALU.bitwise_and, r=["i_p"], w=["i_b"])
    for bl in range(2):
        ts(T.bm[:, bl:bl + 1], T.i_b[:, bl:bl + 1], 16 * bl, None, ALU.is_equal, r=["i_b"], w=["+bm"])
    for s in "hf":
        cp(T["tb" + s][:], T.z0[:, 0:144], r=["z0"], w=["tb" + s], cost=0.08)
        cp(T["tc" + s][:], T.z0[:, 0:144], r=["z0"], w=["tc" + s], cost=0.08)
        cp(T["rm" + s][:], T.z0[:], r=["z0"], w=["rm" + s], cost=0.09)
    for c in (0, WN - 4):
        ms(T.w1[:, c:c + 4], 0, w=["+w1_d"])
        ms(T.w2[:, c:c + 4], 0, w=["+w2_d"])
    ld("s", "d6", T.pth[0:24], T.lp[0:96, :], r=["lp0"], w=["pth"])
    spread("h", ("d7", "d10"), T.lp, "lp1")

    def offsets(out, v, r, w):
        if low == 0:
            ts(out, v, 1, W0 + 2047, ALU.min, ALU.add, r=r, w=w)
        else:
            ts(out, v, 1 - W0, W0 - 1, ALU.max, ALU.add, r=r, w=w)

    def first_list(s):
        offsets(T["off" + s][:, 0:23], T["ll" + s][:, 0:23], ["ll" + s], ["+off%s%d" % (s, r) for r in range(3)])

    def move_values(lo, key, q, m):
        ex = T["ex" + m]
        ts(ex[0:64, :], lo[64:128, :], 1024 * (low + 1) - 2047, flag, ALU.is_ge if q == low else ALU.is_lt, ALU.mult, r=[key], w=["+ex" + m])
        cp(ex[64:128, :], lo[64:128, :], r=[key], w=["+ex" + m])

    def move(z, h, ex):
        b, c0 = "stg%d" % h, W0 + 1024 * z + 512 * h
        for tb in range(8):
            x = 64 * (tb % 2)
            mm(T[b][:, tb // 2, x:x + 64], T.i8[:, 8 * h + tb:8 * h + tb + 1017:8], T[ex][:], True, True,
               r=["i8", "i8a", "i8p", ex], w=["+" + b, "+pe"])
        act(T.w2[:, c0:c0 + 512], T[b][:], r=[b], w=["w2_%d_%d" % (z, h)], cost=0.55)

    def mate_table(z):
        def small(h):
            b = ("uh", "uf")[h]
            for tb in range(8):
                x = 64 * (tb % 2)
                mm(T[b][:, tb // 2, x:x + 64], T.qq[0:64, 8 * h + tb:8 * h + tb + 2033:16], T.nlo[0:64, :], False, False,
                   r=["qq", "nlo"], w=["+" + b, "+pe"])

        def large(h):
            b, c0 = ("uh", "uf")[h], W0 + 1024 * z + 512 * h
            for cb in range(4):
                mm(T[b][:, cb, :], T.i8[:, 4 * h + cb:4 * h + cb + 1017:8], T.nhi[:], False, cb == 3, r=["i8", "i8a", "nhi"], w=["+" + b, "+pe"], cost=0.13)
            ts(T.w1[:, c0:c0 + 512], T[b][:], 64, None, ALU.mult, r=[b], w=["w1_%d_%d" % (z, h)], cost=0.5)

        for b in ("uh", "uf"):
            mm(T[b][:], T.zo[0:64, 0, :], T.zo[0:64], True, False, r=["zo"], w=["+" + b], cost=0.45)
        small(0)
        small(1)
        for o in ORD[0]:
            if o < 2:
                large(o)
            else:
                move(z, o - 2, "exm")

    def expand_points(s):
        b, x = T["l" + s][:, :, 0:23], T["x" + s]
        mm(b, T.e24[0:24], T["pt" + s][0:24], True, True, r=["e24", "pt" + s], w=["+l" + s], cost=0.37)
        ts(x[:, 0:368], b, T.xb[:, 0:1], None, ALU.add, r=["l" + s, "xb"], w=["x" + s], cost=0.37)

    def on_chip(s, v, key):
        if low == 0:
            ts(T["mk" + s][:], v, FLAG, FLAG, ALU.mult, ALU.min, r=[key], w=["mk" + s])
            tt(T["st" + s][:], v, T["mk" + s][:], ALU.max, r=[key, "mk" + s], w=["st" + s])
        else:
            ts(T["st" + s][:], v, 0, None, ALU.max, r=[key], w=["st" + s])

    def to_points(s):
        rm, l = T["rm" + s], T["l" + s]
        for b in range(8):
            mm(l[:, 0:8, 0:3], T.ee[:, 112 - 16 * b:240 - 16 * b], rm[:, :, b::8], b == 0, b == 7, r=["ee", "rm" + s], w=["+l" + s])
        on_chip(s, l[:, 0:8, 0:3], "l" + s)

    move_values(T.tlo, "tlo2", rank, "")
    for h in range(2):
        move(zw, h, "ex")
    expand_points("h")
    first_list("h")
    grp[0] = "h0"
    to_points("h")
    grp[0] = ""
    move_values(T.nlo, "nlo", mate, "m")
    mate_table(zh)
    spread("f", ("d9", "d11"), T.lpn, "lpn")
    ld("s", "d8", T.ptf[0:24], T.lpn[0:96, :], r=["lpn"], w=["ptf"])
    grp[0] = "f0"
    first_list("f")
    expand_points("f")
    to_points("f")

    halves = ["_d"] + ["_%d_%d" % (z, h) for z in range(2) for h in range(2)]

    def gather(s, state, key, rn):
        off, ks = T["off" + s], ["off%s%d" % (s, r) for r in range(3)]

        def third(r):
            c = slice(128 * r, 128 * r + 128)
            add("v", lambda: V.tensor_tensor(T["pr" + s][:, c], T.w1[:, 0:WN].indirect(off[:, 8 * r:8 * r + 8]), T["x" + s][:, c], ALU.mult),
                ["w1" + k for k in halves] + [ks[r], "x" + s, "x%sp" % s], ["pr%s%d" % (s, r)], cost=0.25)
            mm(T["u" + s][:, 0, 40 * r:40 * r + 40], T["pr" + s][:, c], T.s4[:], False, r == 2, r=["pr%s%d" % (s, r), "s4"], w=["+u" + s], cost=0.22)

        mm(T["u" + s][:, 0, 0:120], T.i8[:, 0:128], T.cst[:], True, False, r=["i8a", "cst"], w=["+u" + s], cost=0.13)
        for r in range(3):
            third(r)
        act(T["nb" + s][:], T.w2[:, 0:WN].indirect(off[:, 0:24]), ["w2" + k for k in halves] + ks, ["nb" + s], cost=0.65)
        for r in range(3):
            act(T["zs" + s][:, 40 * r:40 * r + 40:5], state[r], r=[key], w=["+zs" + s], cost=0.1)
        mm(T["n" + s][:, 0, 0:120], T.i8[:, 0:128], T["zs" + s][:], True, False, r=["i8a", "zs" + s], w=["+n" + s], cost=0.13)
        for r in range(3):
            mm(T["n" + s][:, 0, 40 * r:40 * r + 40], T["nb" + s][:, 128 * r:128 * r + 128], T[rn][:], False, r == 2, r=["nb" + s, rn], w=["+n" + s])

    def choose(s):
        u, n = T["u" + s][:, 0, 0:120], T["n" + s][:, 0, 0:120]
        mn, eq, ne, pp, so = (T[k + s] for k in ("mn", "eq", "ne", "pp", "so"))
        scan(mn[:], T.rs[:], u, ALU.max, ALU.min, r=["rs", "u" + s], w=["mn" + s], cost=0.12)
        tt(eq[:], u, mn[:], ALU.is_equal, r=["u" + s, "mn" + s], w=["eq" + s], cost=0.12)
        tt(pp[:], eq[:], n, ALU.mult, r=["eq" + s, "n" + s], w=["pp" + s], cost=0.12)
        tt(ne[:], u, mn[:], ALU.not_equal, r=["u" + s, "mn" + s], w=["ne" + s], cost=0.12)
        for r in range(3):
            c = slice(40 * r, 40 * r + 40)
            scan(so[:, :, r], ne[:, c], pp[:, c], ALU.mult, ALU.add, r=["ne" + s, "pp" + s], w=["+so" + s])

    def to_tb(s, tb, src, key):
        for bl in range(2):
            out, k = T[tb + s][:, 0:8, bl:6:2], T.bm[:, bl:bl + 1]
            if TBA[0][bl] == "v":
                ts(out, src, k, None, ALU.mult, r=[key, "bm"], w=["+" + tb + s])
            else:
                add("a", lambda out=out, k=k: S.activation(out, src, ACTF.Identity, scale=k), [key, "bm"], ["+" + tb + s], 0.12)

    def turn(s, tb, first, last):
        for par in range(2):
            mm(T["l" + s][:, 0:4, 16 * par:16 * par + 16], T[tb + s][:, par:par + 8, :], T.e2[:], first, last and (first or par == 1),
               r=[tb + s, "e2"], w=["+l" + s])

    def from_list(s, last=False):
        l, tr = T["l" + s], T["tr" + s]
        add("v", lambda: V.transpose(tr[:], l[:, 0:4, :]), ["l" + s], ["tr" + s], cost=0.13)
        for r in range(3):
            v, c, k = tr[:, :, 2 * r:2 * r + 2], slice(8 * r, 8 * r + 8), ["off%s%d" % (s, r)]
            if last:
                ts(T.yo[:, c], v, 2047, None, ALU.add, r=["tr" + s], w=["+yo"])
            else:
                offsets(T["off" + s][:, c], v, ["tr" + s], k)

    def rounds(s, wo, name, landing):
        so, st, fl, um, w = T["so" + s], T["st" + s], T["fl" + s], T["um" + s], T[wo + s]
        v = so[:, 4::5, :]
        gather(s, [st[:, :, r] for r in range(3)], "st" + s, "rn")
        choose(s)
        to_tb(s, "tb", v, "so" + s)
        turn(s, "tb", True, True)
        from_list(s)
        ts(fl[:], v, 3000 if flag > 0 else -3000, -flag, ALU.is_ge if flag > 0 else ALU.is_le, ALU.mult, r=["so" + s], w=["fl" + s])
        tt(um[:], v, fl[:], ALU.add, r=["so" + s, "fl" + s], w=["um" + s])
        gather(s, [um[:, :, r] for r in range(3)], "um" + s, "ru")
        choose(s)
        cp(w[:], v, r=["so" + s], w=[wo + s])
        if name:
            send(name, part, T[landing][:], w[:], [wo + s], landing, off_)
        if name != "C":
            mm(T["l" + s][:, 0:4, :], T.zo[0:64, 0, :], T.zo[0:64, :, 0:32], True, False, r=["zo"], w=["+l" + s], cost=0.15)
            to_tb(s, "tb", w[:], wo + s)
            turn(s, "tb", False, False)

    def merge(s, wo, inn, last=False):
        to_tb(s, "tc", T[inn][:], inn)
        turn(s, "tc", False, True)
        from_list(s, last)
        if not last:
            tt(T["su" + s][:], T[wo + s][:], T[inn][:], ALU.add, r=[wo + s, inn], w=["su" + s])
            on_chip(s, T["su" + s][:], "su" + s)

    grp[0] = "h1"
    rounds("h", "wo", "A", "ina")
    grp[0] = "f1"
    rounds("f", "wo", "B", "inb")
    grp[0] = "f2"
    merge("f", "wo", "ina")
    rounds("f", "we", "C", "inc")
    grp[0] = "h2"
    merge("h", "wo", "inb")
    rounds("h", "we", None, None)
    merge("h", "we", "inc", last=True)
    ld("s", "d5", T.y[:, :], T.yo[:, 0:23], r=["yo"])

    N = len(ops)
    succ = [[] for _ in ops]
    for n, o in enumerate(ops):
        for d in o["hard"] | o["soft"]:
            succ[d].append(n)

    def lat(o):
        return o["cost"] + (DMA_T if o["dma"] else 0.0) + (SEND_T[o["send"][0]] if o["send"] else 0.0)

    tail = [0.0] * N
    for n in range(N - 1, -1, -1):
        tail[n] = lat(ops[n]) + max([tail[m] + WAKE[0] for m in succ[n]], default=0.0)
    for n in range(N):
        tail[n] += BIAS.get(ops[n]["grp"], 0.0)
    left = [len(o["hard"] | o["soft"]) for o in ops]
    at, free, order = [0.0] * N, {q: 0.0 for q in Q}, []
    ready = {n for n in range(N) if not left[n]}
    while ready:
        start = {n: max(at[n], free.get(ops[n]["q"], 0.0)) for n in ready}
        t0 = min(start.values())
        q0 = ops[min((n for n in ready), key=lambda n: (start[n], n))]["q"]
        n = max((n for n in ready if ops[n]["q"] == q0 and start[n] <= t0 + WIN[0]), key=lambda n: (tail[n], -n))
        ready.discard(n)
        order.append(n)
        if q0:
            free[q0] = start[n] + ops[n]["cost"]
        for m in succ[n]:
            at[m] = max(at[m], start[n] + (lat(ops[n]) + WAKE[0] if n in ops[m]["hard"] else 0.0))
            left[m] -= 1
            if not left[m]:
                ready.add(m)

    cnt, known, snap, tok = {}, {q: {} for q in Q}, {}, {}

    def need(q, toks):
        kn = known[q]
        for sem, c in sorted(toks, key=lambda t: -t[1]):
            if kn.get(sem, 0) < c:
                Q[q].wait_ge(T.sem[sem], c)
                kn[sem] = c
                for s2, c2 in snap.get((sem, c), {}).items():
                    kn[s2] = max(kn.get(s2, 0), c2)

    for n in order:
        o = ops[n]
        if o["arr"]:
            tok[n] = ("arr" + o["arr"][0], o["arr"][1])
            cnt[tok[n][0]] = tok[n][1]
            continue
        need(o["q"], {tok[d] for d in o["hard"]})
        ins = o["fn"]()
        if o["send"]:
            tok[n] = ("loc" + o["send"][0], o["send"][1])
            cnt[tok[n][0]] = tok[n][1]
        else:
            sem, inc = (o["dma"], 16) if o["dma"] else (CS[o["q"]], 1)
            ins.then_inc(T.sem[sem], inc)
            cnt[sem] = cnt.get(sem, 0) + inc
            tok[n] = (sem, cnt[sem])
        snap[tok[n]] = dict(known[o["q"]])
    need("g", list(cnt.items()))
